import numpy as np
import ml_dtypes


def mxq(x, axis, fmt="e4m3"):
    dtype, down = {"e4m3": (ml_dtypes.float8_e4m3fn, 7), "e5m2": (ml_dtypes.float8_e5m2, 14)}[fmt]
    v = np.moveaxis(np.asarray(x, np.float32).astype(ml_dtypes.bfloat16).astype(np.float64), axis, -1)
    blocks = v.reshape(v.shape[:-1] + (-1, 32))
    amax = np.abs(blocks).max(-1, keepdims=True)
    byte = np.maximum(np.where(amax > 0, np.frexp(amax)[1] - 1 + 127, 0) - down, 1)
    scale = np.exp2(byte - 127.0)
    codes = (blocks / scale).astype(np.float32).astype(dtype).astype(np.float64)
    return np.moveaxis((codes * scale).reshape(v.shape), -1, axis)


WIDE = False


def mx_kscale(k):
    if not WIDE:
        return np.ones(k)
    levels = np.array([18, -18])
    if k % 512:
        return np.exp2(np.random.permutation(np.resize(levels, k // 32))).repeat(32)
    a = np.empty((k // 512, 16))
    for p in range(k // 512):
        a[p, :8] = np.random.permutation(np.resize(levels, 8))
        for g in range(8):
            far = levels[np.abs(levels - a[p, g]) >= 10]
            a[p, g + 8] = far[np.random.randint(len(far))]
    return np.exp2(a.ravel()).repeat(32)


def f64(x):
    return np.asarray(x).astype(np.float64)


def striped(idx):
    return np.tile(np.asarray(idx).reshape(-1, 16).T, (8, 1)).astype(np.uint16)


def unstriped(offs):
    return offs[:16].T.reshape(-1).astype(np.int64)


B, N, T, D, R = 1, 512, 2048, 512, 1024
PAGE = 32


def setup_inputs():
    n = np.random.standard_normal
    pages = np.random.permutation(T // PAGE)[:B * N // PAGE]
    idx = (pages[:, None] * PAGE + np.arange(PAGE)[None, :]).reshape(-1)
    s = mx_kscale(D)[:, None]
    z = mx_kscale(R)[:, None]
    x = n((B, D, R))
    return {
        "xT": (x * s).astype(np.float32),
        "wT": (n((D, T)) * (1.00 / np.sqrt(D)) / s).astype(np.float32),
        "y": np.random.randint(0, 2, (B, R, N)).astype(np.float32),
        "wt": (np.random.uniform(0.5, 1.5, (B, R, 1)) * 1.0 / np.sqrt(R) * z).astype(np.float32),
        "xm": (x.transpose(0, 2, 1) / z).astype(np.float32),
        "offs": striped(idx),
    }


def reference(xT, wT, y, wt, xm, offs):
    idx = unstriped(offs)
    pick = lambda x: x[:, idx].reshape(x.shape[0], B, N).transpose(1, 0, 2)
    a = mxq(f64(xT), 1, "e4m3").transpose(0, 2, 1) @ mxq(pick(f64(wT)), 1, "e4m3")
    g = f64(wt) * (1.0 / (1.0 + np.exp(-a)) - f64(y))
    dw = mxq(f64(xm), 1, "e4m3").transpose(0, 2, 1) @ mxq(g, 1, "e5m2")
    gw = np.zeros((D, T))
    gw[:, idx] = dw.transpose(1, 0, 2).reshape(D, B * N)
    return gw

@@ -1,0 +1,243 @@
+from contextlib import ExitStack
+
+import concourse.mybir as mybir
+
+D, R, T, N = 512, 1024, 2048, 512
+FLOPS = 2 * 2 * D * R * N
+
+F32 = mybir.dt.float32
+BF16 = mybir.dt.bfloat16
+U32 = mybir.dt.uint32
+U16 = mybir.dt.uint16
+U8 = mybir.dt.uint8
+E4M3 = mybir.dt.float8_e4m3fn_x4
+E5M2 = mybir.dt.float8_e5m2_x4
+ACT = mybir.ActivationFunctionType
+ALU = mybir.AluOpType
+
+P = 128
+PACK = 4
+K_PASS = P * PACK
+CHUNKS = R // K_PASS
+HALF = N // 2
+
+
+def tile_attend_gnce_w_kernel(tc, xT, wT, y, wt, xm, offs, out):
+    nc = tc.nc
+    with ExitStack() as ctx:
+        lists = ctx.enter_context(tc.tile_pool(name="lists", bufs=1))
+        keep = ctx.enter_context(tc.tile_pool(name="keep", bufs=1))
+        score_banks = ctx.enter_context(tc.psum_pool(name="score_banks", bufs=4))
+        grad_banks = ctx.enter_context(tc.psum_pool(name="grad_banks", bufs=1))
+
+        def copy_on(engine, dst, src):
+            if engine == "vector":
+                nc.vector.tensor_copy(out=dst, in_=src)
+            else:
+                nc.scalar.copy(out=dst, in_=src)
+
+        offsets = lists.tile([P, N // 16], U16, name="offsets")
+        w_rows = wT.rearrange("(p t) c -> p t c", t=PACK)
+        table = [keep.tile([P, T], F32, name=f"table{t}") for t in range(PACK)]
+        nc.sync.dma_start(out=table[0][:], in_=w_rows[:, 0, :])
+        nc.sync.dma_start(offsets[:], offs)
+        for t in range(1, PACK):
+            nc.sync.dma_start(out=table[t][:], in_=w_rows[:, t, :])
+
+        x_rows = xT[0].rearrange("(p j) r -> p j r", j=PACK)
+        x_raw = {}
+        for c in range(CHUNKS):
+            for h in range(2):
+                x_raw[c, h] = keep.tile([P, PACK, K_PASS // 2], F32, name=f"x_raw{c}{h}")
+                r0 = c * K_PASS + h * (K_PASS // 2)
+                nc.sync.dma_start(out=x_raw[c, h][:], in_=x_rows[:, :, r0 : r0 + K_PASS // 2])
+
+        weight = keep.tile([P, CHUNKS, PACK], F32, name="weight")
+        nc.sync.dma_start(out=weight[:], in_=wt[0].rearrange("(c p t) o -> p c (t o)", c=CHUNKS, t=PACK))
+
+        y_rows = y[0].rearrange("(c p t) i -> c p t i", c=CHUNKS, t=PACK)
+        y_raw = {}
+        for c in range(CHUNKS):
+            for u in range(2):
+                y_raw[c, u] = keep.tile([P, 2, N], F32, name=f"y_raw{c}{u}")
+                nc.sync.dma_start(out=y_raw[c, u][:], in_=y_rows[c, :, 2 * u : 2 * u + 2, :])
+
+        m_rows = xm[0].rearrange("(c p t) d -> c p t d", c=CHUNKS, t=PACK)
+        m_raw0 = keep.tile([P, PACK, D], F32, name="m_raw0")
+        nc.sync.dma_start(out=m_raw0[:], in_=m_rows[0])
+        m_raw1 = [keep.tile([P, PACK, D // 2], F32, name=f"m_raw1{h}") for h in range(2)]
+        for h in range(2):
+            nc.sync.dma_start(out=m_raw1[h][:], in_=m_rows[1, :, :, h * (D // 2) : (h + 1) * (D // 2)])
+
+        def m_source(c, b):
+            if c == 0:
+                return m_raw0[:, :, b * P : (b + 1) * P]
+            return m_raw1[b // 2][:, :, (b % 2) * P : (b % 2 + 1) * P]
+
+        window = [keep.tile([P, T], F32, name=f"window{b}") for b in range(D // P)]
+        for b in range(D // P):
+            nc.vector.memset(window[b][:], 0.0)
+
+        w_bf = keep.tile([P, N, PACK], BF16, name="w_bf", align_bytes=64)
+        w_codes = keep.tile([P, N], U32, name="w_codes", align_bytes=64)
+        w_scales = keep.tile([P, N], U8, name="w_scales", align_bytes=64)
+        for t in range(PACK - 1):
+            nc.vector.tensor_copy(out=w_bf[:, :, t], in_=table[t][:].indirect(offsets[:]))
+        for h in range(2):
+            nc.vector.tensor_copy(
+                out=w_bf[:, h * HALF : (h + 1) * HALF, PACK - 1],
+                in_=table[PACK - 1][:].indirect(offsets[:, h * (HALF // 16) : (h + 1) * (HALF // 16)]),
+            )
+        for h in range(2):
+            cols = slice(h * HALF, (h + 1) * HALF)
+            nc.vector.quantize_mx(
+                out=w_codes[:, cols].bitcast(E4M3),
+                scales=w_scales[:, cols],
+                in_=w_bf[:, cols, :].rearrange("p n t -> p (n t)"),
+            )
+
+        sig = {}
+
+        def scores(c):
+            x_bf = keep.tile([P, PACK, P, PACK], BF16, name=f"x_bf{c}", align_bytes=64)
+            x_codes = keep.tile([P, K_PASS], U32, name=f"x_codes{c}", align_bytes=64)
+            x_scales = keep.tile([P, K_PASS], U8, name=f"x_scales{c}", align_bytes=64)
+            for h, engine in ((0, "scalar"), (1, "vector")):
+                copy_on(
+                    engine,
+                    x_bf[:, :, h * (P // 2) : (h + 1) * (P // 2), :].rearrange("p t m j -> p m j t"),
+                    x_raw[c, h][:].rearrange("p j (m t) -> p m j t", t=PACK),
+                )
+            for u in range(2):
+                cols = slice(u * 2 * P, (u + 1) * 2 * P)
+                nc.vector.quantize_mx(
+                    out=x_codes[:, cols].bitcast(E4M3),
+                    scales=x_scales[:, cols],
+                    in_=x_bf[:, 2 * u : 2 * u + 2, :, :].rearrange("p t m j -> p (t m j)"),
+                )
+            for t in range(PACK):
+                cols = slice(t * P, (t + 1) * P)
+                bank = score_banks.tile([P, N], F32, name="bank")
+                nc.tensor.matmul_mx(
+                    out=bank[:],
+                    lhsT=x_codes[:, cols].bitcast(E4M3),
+                    lhsT_scale=x_scales[:, cols],
+                    rhs=w_codes[:].bitcast(E4M3),
+                    rhs_scale=w_scales[:],
+                    start=True,
+                    stop=True,
+                )
+                sig[c, t] = keep.tile([P, N], F32, name=f"sig{c}{t}")
+                nc.scalar.activation(out=sig[c, t][:], in_=bank[:], func=ACT.Sigmoid)
+
+        yw = {}
+
+        def weighted_targets(c, t, engine):
+            yw[c, t] = keep.tile([P, N], F32, name=f"yw{c}{t}")
+            src = y_raw[c, t // 2][:, t % 2, :]
+            if engine == "vector":
+                nc.vector.tensor_scalar(
+                    out=yw[c, t][:], in0=src, scalar1=weight[:, c, t : t + 1], scalar2=None, op0=ALU.mult
+                )
+            else:
+                nc.scalar.activation(out=yw[c, t][:], in_=src, func=ACT.Copy, scale=weight[:, c, t : t + 1])
+
+        g_codes = [keep.tile([P, N], U32, name=f"g_codes{c}", align_bytes=64) for c in range(CHUNKS)]
+        g_scales = [keep.tile([P, N], U8, name=f"g_scales{c}", align_bytes=64) for c in range(CHUNKS)]
+        g_rows = {}
+        g_bf = {}
+
+        def gradient(c, h):
+            cols = slice(h * HALF, (h + 1) * HALF)
+            g_rows[c, h] = keep.tile([P, PACK, HALF], BF16, name=f"g_rows{c}{h}")
+            for t in range(PACK):
+                nc.vector.scalar_tensor_tensor(
+                    out=g_rows[c, h][:, t, :],
+                    in0=sig[c, t][:, cols],
+                    scalar=weight[:, c, t : t + 1],
+                    in1=yw[c, t][:, cols],
+                    op0=ALU.mult,
+                    op1=ALU.subtract,
+                )
+
+        def interleave_gradient(c, h, engine):
+            g_bf[c, h] = keep.tile([P, HALF, PACK], BF16, name=f"g_bf{c}{h}", align_bytes=64)
+            copy_on(
+                engine,
+                g_bf[c, h][:].rearrange("p (n i) t -> p n t i", i=4),
+                g_rows[c, h][:].rearrange("p t (n i) -> p n t i", i=4),
+            )
+
+        def quantise_gradient(c, h):
+            cols = slice(h * HALF, (h + 1) * HALF)
+            nc.vector.quantize_mx(
+                out=g_codes[c][:, cols].bitcast(E5M2),
+                scales=g_scales[c][:, cols],
+                in_=g_bf[c, h][:].rearrange("p n t -> p (n t)"),
+            )
+
+        m_bf = {}
+        m_codes = {}
+        m_scales = {}
+
+        def interleave_xm(b, engine):
+            m_bf[b] = keep.tile([P, CHUNKS, P, PACK], BF16, name=f"m_bf{b}", align_bytes=64)
+            for c in range(CHUNKS):
+                copy_on(
+                    engine,
+                    m_bf[b][:, c].rearrange("p (n i) t -> p n t i", i=4),
+                    m_source(c, b).rearrange("p t (n i) -> p n t i", i=4),
+                )
+
+        def quantise_xm(b):
+            m_codes[b] = keep.tile([P, CHUNKS * P], U32, name=f"m_codes{b}", align_bytes=64)
+            m_scales[b] = keep.tile([P, CHUNKS * P], U8, name=f"m_scales{b}", align_bytes=64)
+            nc.vector.quantize_mx(
+                out=m_codes[b][:].bitcast(E4M3),
+                scales=m_scales[b][:],
+                in_=m_bf[b][:].rearrange("p c n t -> p (c n t)"),
+            )
+
+        def output_block(b):
+            acc = grad_banks.tile([P, N], F32, name=f"acc{b}")
+            for c in range(CHUNKS):
+                cols = slice(c * P, (c + 1) * P)
+                nc.tensor.matmul_mx(
+                    out=acc[:],
+                    lhsT=m_codes[b][:, cols].bitcast(E4M3),
+                    lhsT_scale=m_scales[b][:, cols],
+                    rhs=g_codes[c][:].bitcast(E5M2),
+                    rhs_scale=g_scales[c][:],
+                    start=(c == 0),
+                    stop=(c == CHUNKS - 1),
+                )
+            dense = keep.tile([P, N], F32, name=f"dense{b}")
+            nc.scalar.copy(out=dense[:], in_=acc[:])
+            nc.vector.tensor_copy(out=window[b][:].indirect(offsets[:]), in_=dense[:])
+            nc.sync.dma_start(out=out[b * P : (b + 1) * P, :], in_=window[b][:])
+
+        scores(0)
+        scores(1)
+        for t in range(PACK):
+            weighted_targets(0, t, "vector")
+        gradient(0, 0)
+        interleave_gradient(0, 0, "scalar")
+        gradient(0, 1)
+        for t in range(PACK):
+            weighted_targets(1, t, "scalar")
+        interleave_gradient(0, 1, "vector")
+        quantise_gradient(0, 0)
+        quantise_gradient(0, 1)
+        interleave_xm(0, "scalar")
+        gradient(1, 0)
+        interleave_gradient(1, 0, "scalar")
+        gradient(1, 1)
+        quantise_xm(0)
+        interleave_gradient(1, 1, "vector")
+        quantise_gradient(1, 0)
+        quantise_gradient(1, 1)
+        for b in range(D // P):
+            if b + 1 < D // P:
+                interleave_xm(b + 1, "scalar")
+                quantise_xm(b + 1)
+            output_block(b)

@@ -36,24 +36,28 @@ def tile_attend_gnce_w_kernel(tc, xT, wT, y, wt, xm, offs, out):
             else:
                 nc.scalar.copy(out=dst, in_=src)
 
+        weight = keep.tile([P, CHUNKS, PACK], F32, name="weight")
+        nc.scalar.dma_start(out=weight[:], in_=wt[0].rearrange("(c p t) o -> p c (t o)", c=CHUNKS, t=PACK))
+        warm_in = keep.tile([P, 1], F32, name="warm_in")
+        warm_out = keep.tile([P, 1], F32, name="warm_out")
+        nc.gpsimd.memset(warm_in[:], 0.0)
+        nc.scalar.activation(out=warm_out[:], in_=warm_in[:], func=ACT.Sigmoid)
         offsets = lists.tile([P, N // 16], U16, name="offsets")
         w_rows = wT.rearrange("(p t) c -> p t c", t=PACK)
         table = [keep.tile([P, T], F32, name=f"table{t}") for t in range(PACK)]
         nc.sync.dma_start(out=table[0][:], in_=w_rows[:, 0, :])
         nc.sync.dma_start(offsets[:], offs)
+        x_rows = xT[0].rearrange("(p j) r -> p j r", j=PACK)
+        x_first = keep.tile([P, PACK, K_PASS], F32, name="x_first")
+        nc.sync.dma_start(out=x_first[:], in_=x_rows[:, :, :K_PASS])
+        x_raw = {(0, h): x_first[:, :, h * (K_PASS // 2) : (h + 1) * (K_PASS // 2)] for h in range(2)}
         for t in range(1, PACK):
             nc.sync.dma_start(out=table[t][:], in_=w_rows[:, t, :])
-
-        x_rows = xT[0].rearrange("(p j) r -> p j r", j=PACK)
-        x_raw = {}
-        for c in range(CHUNKS):
-            for h in range(2):
-                x_raw[c, h] = keep.tile([P, PACK, K_PASS // 2], F32, name=f"x_raw{c}{h}")
-                r0 = c * K_PASS + h * (K_PASS // 2)
-                nc.sync.dma_start(out=x_raw[c, h][:], in_=x_rows[:, :, r0 : r0 + K_PASS // 2])
-
-        weight = keep.tile([P, CHUNKS, PACK], F32, name="weight")
-        nc.sync.dma_start(out=weight[:], in_=wt[0].rearrange("(c p t) o -> p c (t o)", c=CHUNKS, t=PACK))
+        for h in range(2):
+            x_half = keep.tile([P, PACK, K_PASS // 2], F32, name=f"x_half{h}")
+            r0 = K_PASS + h * (K_PASS // 2)
+            nc.sync.dma_start(out=x_half[:], in_=x_rows[:, :, r0 : r0 + K_PASS // 2])
+            x_raw[1, h] = x_half[:]
 
         y_rows = y[0].rearrange("(c p t) i -> c p t i", c=CHUNKS, t=PACK)
         y_raw = {}
@@ -76,7 +80,7 @@ def tile_attend_gnce_w_kernel(tc, xT, wT, y, wt, xm, offs, out):
 
         window = [keep.tile([P, T], F32, name=f"window{b}") for b in range(D // P)]
         for b in range(D // P):
-            nc.vector.memset(window[b][:], 0.0)
+            (nc.vector if b < 2 else nc.gpsimd).memset(window[b][:], 0.0)
 
         w_bf = keep.tile([P, N, PACK], BF16, name="w_bf", align_bytes=64)
         w_codes = keep.tile([P, N], U32, name="w_codes", align_bytes=64)
@@ -106,7 +110,7 @@ def tile_attend_gnce_w_kernel(tc, xT, wT, y, wt, xm, offs, out):
                 copy_on(
                     engine,
                     x_bf[:, :, h * (P // 2) : (h + 1) * (P // 2), :].rearrange("p t m j -> p m j t"),
-                    x_raw[c, h][:].rearrange("p j (m t) -> p m j t", t=PACK),
+                    x_raw[c, h].rearrange("p j (m t) -> p m j t", t=PACK),
                 )
             for u in range(2):
                 cols = slice(u * 2 * P, (u + 1) * 2 * P)
@@ -176,36 +180,25 @@ def tile_attend_gnce_w_kernel(tc, xT, wT, y, wt, xm, offs, out):
                 in_=g_bf[c, h][:].rearrange("p n t -> p (n t)"),
             )
 
-        m_bf = {}
-        m_codes = {}
-        m_scales = {}
-
-        def interleave_xm(b, engine):
-            m_bf[b] = keep.tile([P, CHUNKS, P, PACK], BF16, name=f"m_bf{b}", align_bytes=64)
-            for c in range(CHUNKS):
-                copy_on(
-                    engine,
-                    m_bf[b][:, c].rearrange("p (n i) t -> p n t i", i=4),
-                    m_source(c, b).rearrange("p t (n i) -> p n t i", i=4),
-                )
-
-        def quantise_xm(b):
-            m_codes[b] = keep.tile([P, CHUNKS * P], U32, name=f"m_codes{b}", align_bytes=64)
-            m_scales[b] = keep.tile([P, CHUNKS * P], U8, name=f"m_scales{b}", align_bytes=64)
-            nc.vector.quantize_mx(
-                out=m_codes[b][:].bitcast(E4M3),
-                scales=m_scales[b][:],
-                in_=m_bf[b][:].rearrange("p c n t -> p (c n t)"),
-            )
-
         def output_block(b):
             acc = grad_banks.tile([P, N], F32, name=f"acc{b}")
             for c in range(CHUNKS):
-                cols = slice(c * P, (c + 1) * P)
+                m_bf = keep.tile([P, P, PACK], BF16, name=f"m_bf{b}{c}", align_bytes=64)
+                m_codes = keep.tile([P, P], U32, name=f"m_codes{b}{c}", align_bytes=64)
+                m_scales = keep.tile([P, P], U8, name=f"m_scales{b}{c}", align_bytes=64)
+                nc.scalar.copy(
+                    out=m_bf[:].rearrange("p (n i) t -> p n t i", i=4),
+                    in_=m_source(c, b).rearrange("p t (n i) -> p n t i", i=4),
+                )
+                nc.vector.quantize_mx(
+                    out=m_codes[:].bitcast(E4M3),
+                    scales=m_scales[:],
+                    in_=m_bf[:].rearrange("p n t -> p (n t)"),
+                )
                 nc.tensor.matmul_mx(
                     out=acc[:],
-                    lhsT=m_codes[b][:, cols].bitcast(E4M3),
-                    lhsT_scale=m_scales[b][:, cols],
+                    lhsT=m_codes[:].bitcast(E4M3),
+                    lhsT_scale=m_scales[:],
                     rhs=g_codes[c][:].bitcast(E5M2),
                     rhs_scale=g_scales[c][:],
                     start=(c == 0),
@@ -216,28 +209,14 @@ def tile_attend_gnce_w_kernel(tc, xT, wT, y, wt, xm, offs, out):
             nc.vector.tensor_copy(out=window[b][:].indirect(offsets[:]), in_=dense[:])
             nc.sync.dma_start(out=out[b * P : (b + 1) * P, :], in_=window[b][:])
 
-        scores(0)
-        scores(1)
-        for t in range(PACK):
-            weighted_targets(0, t, "vector")
-        gradient(0, 0)
-        interleave_gradient(0, 0, "scalar")
-        gradient(0, 1)
-        for t in range(PACK):
-            weighted_targets(1, t, "scalar")
-        interleave_gradient(0, 1, "vector")
-        quantise_gradient(0, 0)
-        quantise_gradient(0, 1)
-        interleave_xm(0, "scalar")
-        gradient(1, 0)
-        interleave_gradient(1, 0, "scalar")
-        gradient(1, 1)
-        quantise_xm(0)
-        interleave_gradient(1, 1, "vector")
-        quantise_gradient(1, 0)
-        quantise_gradient(1, 1)
+        for c in range(CHUNKS):
+            scores(c)
+        for c, engines in enumerate((("vector",) * 4, ("scalar", "scalar", "vector", "scalar"))):
+            for t in range(PACK):
+                weighted_targets(c, t, engines[t])
+            for h, engine in ((0, "scalar"), (1, "vector")):
+                gradient(c, h)
+                interleave_gradient(c, h, engine)
+                quantise_gradient(c, h)
         for b in range(D // P):
-            if b + 1 < D // P:
-                interleave_xm(b + 1, "scalar")
-                quantise_xm(b + 1)
             output_block(b)

@@ -20,6 +20,7 @@ PACK = 4
 K_PASS = P * PACK
 CHUNKS = R // K_PASS
 HALF = N // 2
+UNIT = 64
 
 
 def tile_attend_gnce_w_kernel(tc, xT, wT, y, wt, xm, offs, out):
@@ -45,38 +46,49 @@ def tile_attend_gnce_w_kernel(tc, xT, wT, y, wt, xm, offs, out):
         offsets = lists.tile([P, N // 16], U16, name="offsets")
         w_rows = wT.rearrange("(p t) c -> p t c", t=PACK)
         table = [keep.tile([P, T], F32, name=f"table{t}") for t in range(PACK)]
+        x_rows = xT[0].rearrange("(p j) r -> p j r", j=PACK)
+        y_rows = y[0].rearrange("(c p t) i -> c p t i", c=CHUNKS, t=PACK)
+        m_rows = xm[0].rearrange("(c p t) d -> c p t d", c=CHUNKS, t=PACK)
+        x_raw, y_raw, m_raw = {}, {}, {}
+
+        def load_x(c, h):
+            x_half = keep.tile([P, PACK, K_PASS // 2], F32, name=f"x_half{c}{h}")
+            r0 = c * K_PASS + h * (K_PASS // 2)
+            nc.sync.dma_start(out=x_half[:], in_=x_rows[:, :, r0 : r0 + K_PASS // 2])
+            x_raw[c, h] = x_half[:]
+
+        def load_x_whole(c):
+            x_whole = keep.tile([P, PACK, K_PASS], F32, name=f"x_whole{c}")
+            nc.sync.dma_start(out=x_whole[:], in_=x_rows[:, :, c * K_PASS : (c + 1) * K_PASS])
+            for h in range(2):
+                x_raw[c, h] = x_whole[:, :, h * (K_PASS // 2) : (h + 1) * (K_PASS // 2)]
+
+        def load_y(c, u):
+            y_raw[c, u] = keep.tile([P, 2, N], F32, name=f"y_raw{c}{u}")
+            nc.sync.dma_start(out=y_raw[c, u][:], in_=y_rows[c, :, 2 * u : 2 * u + 2, :])
+
+        def load_m(c, h):
+            m_half = keep.tile([P, PACK, D // 2], F32, name=f"m_half{c}{h}")
+            nc.sync.dma_start(out=m_half[:], in_=m_rows[c, :, :, h * (D // 2) : (h + 1) * (D // 2)])
+            for i in range(2):
+                m_raw[2 * h + i, c] = m_half[:, :, i * P : (i + 1) * P]
+
         nc.sync.dma_start(out=table[0][:], in_=w_rows[:, 0, :])
         nc.sync.dma_start(offsets[:], offs)
-        x_rows = xT[0].rearrange("(p j) r -> p j r", j=PACK)
-        x_first = keep.tile([P, PACK, K_PASS], F32, name="x_first")
-        nc.sync.dma_start(out=x_first[:], in_=x_rows[:, :, :K_PASS])
-        x_raw = {(0, h): x_first[:, :, h * (K_PASS // 2) : (h + 1) * (K_PASS // 2)] for h in range(2)}
-        for t in range(1, PACK):
-            nc.sync.dma_start(out=table[t][:], in_=w_rows[:, t, :])
-        for h in range(2):
-            x_half = keep.tile([P, PACK, K_PASS // 2], F32, name=f"x_half{h}")
-            r0 = K_PASS + h * (K_PASS // 2)
-            nc.sync.dma_start(out=x_half[:], in_=x_rows[:, :, r0 : r0 + K_PASS // 2])
-            x_raw[1, h] = x_half[:]
-
-        y_rows = y[0].rearrange("(c p t) i -> c p t i", c=CHUNKS, t=PACK)
-        y_raw = {}
-        for c in range(CHUNKS):
-            for u in range(2):
-                y_raw[c, u] = keep.tile([P, 2, N], F32, name=f"y_raw{c}{u}")
-                nc.sync.dma_start(out=y_raw[c, u][:], in_=y_rows[c, :, 2 * u : 2 * u + 2, :])
-
-        m_rows = xm[0].rearrange("(c p t) d -> c p t d", c=CHUNKS, t=PACK)
-        m_raw0 = keep.tile([P, PACK, D], F32, name="m_raw0")
-        nc.sync.dma_start(out=m_raw0[:], in_=m_rows[0])
-        m_raw1 = [keep.tile([P, PACK, D // 2], F32, name=f"m_raw1{h}") for h in range(2)]
-        for h in range(2):
-            nc.sync.dma_start(out=m_raw1[h][:], in_=m_rows[1, :, :, h * (D // 2) : (h + 1) * (D // 2)])
-
-        def m_source(c, b):
-            if c == 0:
-                return m_raw0[:, :, b * P : (b + 1) * P]
-            return m_raw1[b // 2][:, :, (b % 2) * P : (b % 2 + 1) * P]
+        nc.sync.dma_start(out=table[1][:], in_=w_rows[:, 1, :])
+        nc.sync.dma_start(out=table[2][:], in_=w_rows[:, 2, :])
+        nc.sync.dma_start(out=table[3][:], in_=w_rows[:, 3, :])
+        load_x_whole(0)
+        load_x(1, 0)
+        load_x(1, 1)
+        load_y(0, 0)
+        load_y(0, 1)
+        load_y(1, 0)
+        load_y(1, 1)
+        load_m(0, 0)
+        load_m(1, 0)
+        load_m(0, 1)
+        load_m(1, 1)
 
         window = [keep.tile([P, T], F32, name=f"window{b}") for b in range(D // P)]
         for b in range(D // P):
@@ -85,138 +97,242 @@ def tile_attend_gnce_w_kernel(tc, xT, wT, y, wt, xm, offs, out):
         w_bf = keep.tile([P, N, PACK], BF16, name="w_bf", align_bytes=64)
         w_codes = keep.tile([P, N], U32, name="w_codes", align_bytes=64)
         w_scales = keep.tile([P, N], U8, name="w_scales", align_bytes=64)
-        for t in range(PACK - 1):
-            nc.vector.tensor_copy(out=w_bf[:, :, t], in_=table[t][:].indirect(offsets[:]))
-        for h in range(2):
+
+        def slots(lo, hi):
+            return slice(lo * UNIT, hi * UNIT)
+
+        def gather(t, lo, hi):
             nc.vector.tensor_copy(
-                out=w_bf[:, h * HALF : (h + 1) * HALF, PACK - 1],
-                in_=table[PACK - 1][:].indirect(offsets[:, h * (HALF // 16) : (h + 1) * (HALF // 16)]),
+                out=w_bf[:, slots(lo, hi), t], in_=table[t][:].indirect(offsets[:, lo * UNIT // 16 : hi * UNIT // 16])
             )
-        for h in range(2):
-            cols = slice(h * HALF, (h + 1) * HALF)
+
+        def quantise_w(lo, hi):
             nc.vector.quantize_mx(
-                out=w_codes[:, cols].bitcast(E4M3),
-                scales=w_scales[:, cols],
-                in_=w_bf[:, cols, :].rearrange("p n t -> p (n t)"),
+                out=w_codes[:, slots(lo, hi)].bitcast(E4M3),
+                scales=w_scales[:, slots(lo, hi)],
+                in_=w_bf[:, slots(lo, hi), :].rearrange("p n t -> p (n t)"),
             )
 
-        sig = {}
+        x_bf = [keep.tile([P, PACK, P, PACK], BF16, name=f"x_bf{c}", align_bytes=64) for c in range(CHUNKS)]
+        x_codes = [keep.tile([P, K_PASS], U32, name=f"x_codes{c}", align_bytes=64) for c in range(CHUNKS)]
+        x_scales = [keep.tile([P, K_PASS], U8, name=f"x_scales{c}", align_bytes=64) for c in range(CHUNKS)]
 
-        def scores(c):
-            x_bf = keep.tile([P, PACK, P, PACK], BF16, name=f"x_bf{c}", align_bytes=64)
-            x_codes = keep.tile([P, K_PASS], U32, name=f"x_codes{c}", align_bytes=64)
-            x_scales = keep.tile([P, K_PASS], U8, name=f"x_scales{c}", align_bytes=64)
-            for h, engine in ((0, "scalar"), (1, "vector")):
-                copy_on(
-                    engine,
-                    x_bf[:, :, h * (P // 2) : (h + 1) * (P // 2), :].rearrange("p t m j -> p m j t"),
-                    x_raw[c, h].rearrange("p j (m t) -> p m j t", t=PACK),
-                )
-            for u in range(2):
-                cols = slice(u * 2 * P, (u + 1) * 2 * P)
-                nc.vector.quantize_mx(
-                    out=x_codes[:, cols].bitcast(E4M3),
-                    scales=x_scales[:, cols],
-                    in_=x_bf[:, 2 * u : 2 * u + 2, :, :].rearrange("p t m j -> p (t m j)"),
-                )
-            for t in range(PACK):
-                cols = slice(t * P, (t + 1) * P)
-                bank = score_banks.tile([P, N], F32, name="bank")
-                nc.tensor.matmul_mx(
-                    out=bank[:],
-                    lhsT=x_codes[:, cols].bitcast(E4M3),
-                    lhsT_scale=x_scales[:, cols],
-                    rhs=w_codes[:].bitcast(E4M3),
-                    rhs_scale=w_scales[:],
-                    start=True,
-                    stop=True,
-                )
-                sig[c, t] = keep.tile([P, N], F32, name=f"sig{c}{t}")
-                nc.scalar.activation(out=sig[c, t][:], in_=bank[:], func=ACT.Sigmoid)
+        def interleave_x(c, lo, hi, engine):
+            h = lo // 4
+            copy_on(
+                engine,
+                x_bf[c][:, :, lo * 16 : hi * 16, :].rearrange("p t m j -> p m j t"),
+                x_raw[c, h][:, :, (lo - 4 * h) * UNIT : (hi - 4 * h) * UNIT].rearrange("p j (m t) -> p m j t", t=PACK),
+            )
 
-        yw = {}
+        def quantise_x(c, lo, hi):
+            cols = slice(lo * P, hi * P)
+            nc.vector.quantize_mx(
+                out=x_codes[c][:, cols].bitcast(E4M3),
+                scales=x_scales[c][:, cols],
+                in_=x_bf[c][:, lo:hi, :, :].rearrange("p t m j -> p (t m j)"),
+            )
 
-        def weighted_targets(c, t, engine):
-            yw[c, t] = keep.tile([P, N], F32, name=f"yw{c}{t}")
-            src = y_raw[c, t // 2][:, t % 2, :]
+        sig = [keep.tile([P, PACK, N], F32, name=f"sig{c}") for c in range(CHUNKS)]
+
+        def score_product(dst, c, t, cols):
+            nc.tensor.matmul_mx(
+                out=dst,
+                lhsT=x_codes[c][:, t * P : (t + 1) * P].bitcast(E4M3),
+                lhsT_scale=x_scales[c][:, t * P : (t + 1) * P],
+                rhs=w_codes[:, cols].bitcast(E4M3),
+                rhs_scale=w_scales[:, cols],
+                start=True,
+                stop=True,
+            )
+
+        def scores(c, t):
+            bank = score_banks.tile([P, N], F32, name="bank")
+            score_product(bank[:], c, t, slots(0, 8))
+            nc.scalar.activation(out=sig[c][:, t, :], in_=bank[:], func=ACT.Sigmoid)
+
+        def scores_half(c, u, h):
+            bank = score_banks.tile([P, 2, HALF], F32, name="bank")
+            cols = slots(4 * h, 4 * h + 4)
+            for i in range(2):
+                score_product(bank[:, i, :], c, 2 * u + i, cols)
+            nc.scalar.activation(out=sig[c][:, 2 * u : 2 * u + 2, cols], in_=bank[:], func=ACT.Sigmoid)
+
+        yw = [keep.tile([P, PACK, N], F32, name=f"yw{c}") for c in range(CHUNKS)]
+
+        def weighted_targets(c, t, lo, hi, engine):
+            src = y_raw[c, t // 2][:, t % 2, slots(lo, hi)]
+            dst = yw[c][:, t, slots(lo, hi)]
             if engine == "vector":
-                nc.vector.tensor_scalar(
-                    out=yw[c, t][:], in0=src, scalar1=weight[:, c, t : t + 1], scalar2=None, op0=ALU.mult
-                )
+                nc.vector.tensor_scalar(out=dst, in0=src, scalar1=weight[:, c, t : t + 1], scalar2=None, op0=ALU.mult)
             else:
-                nc.scalar.activation(out=yw[c, t][:], in_=src, func=ACT.Copy, scale=weight[:, c, t : t + 1])
+                nc.scalar.activation(out=dst, in_=src, func=ACT.Copy, scale=weight[:, c, t : t + 1])
 
         g_codes = [keep.tile([P, N], U32, name=f"g_codes{c}", align_bytes=64) for c in range(CHUNKS)]
         g_scales = [keep.tile([P, N], U8, name=f"g_scales{c}", align_bytes=64) for c in range(CHUNKS)]
-        g_rows = {}
-        g_bf = {}
+        g_rows = [keep.tile([P, PACK, N], BF16, name=f"g_rows{c}") for c in range(CHUNKS)]
+        g_bf = [keep.tile([P, N, PACK], BF16, name=f"g_bf{c}", tag=f"g_bf{c}", align_bytes=64) for c in range(CHUNKS)]
+        diff = [keep.tile([P, PACK, N], F32, name=f"diff{c}") for c in range(CHUNKS)]
 
-        def gradient(c, h):
-            cols = slice(h * HALF, (h + 1) * HALF)
-            g_rows[c, h] = keep.tile([P, PACK, HALF], BF16, name=f"g_rows{c}{h}")
-            for t in range(PACK):
-                nc.vector.scalar_tensor_tensor(
-                    out=g_rows[c, h][:, t, :],
-                    in0=sig[c, t][:, cols],
-                    scalar=weight[:, c, t : t + 1],
-                    in1=yw[c, t][:, cols],
-                    op0=ALU.mult,
-                    op1=ALU.subtract,
-                )
-
-        def interleave_gradient(c, h, engine):
-            g_bf[c, h] = keep.tile([P, HALF, PACK], BF16, name=f"g_bf{c}{h}", align_bytes=64)
-            copy_on(
-                engine,
-                g_bf[c, h][:].rearrange("p (n i) t -> p n t i", i=4),
-                g_rows[c, h][:].rearrange("p t (n i) -> p n t i", i=4),
+        def gradient(c, t, lo, hi):
+            nc.vector.scalar_tensor_tensor(
+                out=g_rows[c][:, t, slots(lo, hi)],
+                in0=sig[c][:, t, slots(lo, hi)],
+                scalar=weight[:, c, t : t + 1],
+                in1=yw[c][:, t, slots(lo, hi)],
+                op0=ALU.mult,
+                op1=ALU.subtract,
             )
 
-        def quantise_gradient(c, h):
-            cols = slice(h * HALF, (h + 1) * HALF)
+        def interleave_gradient(c, lo, hi, engine):
+            copy_on(
+                engine,
+                g_bf[c][:, slots(lo, hi), :].rearrange("p (n i) t -> p n t i", i=4),
+                g_rows[c][:, :, slots(lo, hi)].rearrange("p t (n i) -> p n t i", i=4),
+            )
+
+        def difference(c, u, lo, hi):
+            nc.vector.tensor_tensor(
+                out=diff[c][:, 2 * u : 2 * u + 2, slots(lo, hi)],
+                in0=sig[c][:, 2 * u : 2 * u + 2, slots(lo, hi)],
+                in1=y_raw[c, u][:, :, slots(lo, hi)],
+                op=ALU.subtract,
+            )
+
+        def weigh_interleave(c, lo, hi):
+            groups = (hi - lo) * UNIT // 4
+            nc.vector.tensor_tensor(
+                out=g_bf[c][:, slots(lo, hi), :].rearrange("p (n i) t -> p n t i", i=4),
+                in0=diff[c][:, :, slots(lo, hi)].rearrange("p t (n i) -> p n t i", i=4),
+                in1=weight[:, c, :].rearrange("p (n t i) -> p n t i", n=1, i=1).to_broadcast([P, groups, PACK, 4]),
+                op=ALU.mult,
+            )
+
+        def quantise_gradient(c, lo, hi):
             nc.vector.quantize_mx(
-                out=g_codes[c][:, cols].bitcast(E5M2),
-                scales=g_scales[c][:, cols],
-                in_=g_bf[c, h][:].rearrange("p n t -> p (n t)"),
+                out=g_codes[c][:, slots(lo, hi)].bitcast(E5M2),
+                scales=g_scales[c][:, slots(lo, hi)],
+                in_=g_bf[c][:, slots(lo, hi), :].rearrange("p n t -> p (n t)"),
+            )
+
+        m_bf, m_codes, m_scales, acc = {}, {}, {}, {}
+
+        def interleave_m(b, c, engine):
+            if b == 0:
+                m_bf[b, c] = keep.tile([P, P, PACK], BF16, name=f"m_bf{c}", align_bytes=64)
+            else:
+                if (b, c) == (1, 0):
+                    m_bf["late"] = keep.tile([P, 6, P, PACK], BF16, name="m_late", tag="g_bf1", align_bytes=64)
+                m_bf[b, c] = m_bf["late"][:, 2 * (b - 1) + c]
+            copy_on(
+                engine,
+                m_bf[b, c][:].rearrange("p (n i) t -> p n t i", i=4),
+                m_raw[b, c].rearrange("p t (n i) -> p n t i", i=4),
+            )
+
+        def quantise_m(b, c):
+            m_codes[b, c] = keep.tile([P, P], U32, name=f"m_codes{b}{c}", align_bytes=64)
+            m_scales[b, c] = keep.tile([P, P], U8, name=f"m_scales{b}{c}", align_bytes=64)
+            nc.vector.quantize_mx(
+                out=m_codes[b, c][:].bitcast(E4M3),
+                scales=m_scales[b, c][:],
+                in_=m_bf[b, c][:].rearrange("p n t -> p (n t)"),
+            )
+
+        def product(b, c):
+            if c == 0:
+                acc[b] = grad_banks.tile([P, N], F32, name=f"acc{b}")
+            nc.tensor.matmul_mx(
+                out=acc[b][:],
+                lhsT=m_codes[b, c][:].bitcast(E4M3),
+                lhsT_scale=m_scales[b, c][:],
+                rhs=g_codes[c][:].bitcast(E5M2),
+                rhs_scale=g_scales[c][:],
+                start=(c == 0),
+                stop=(c == CHUNKS - 1),
             )
 
         def output_block(b):
-            acc = grad_banks.tile([P, N], F32, name=f"acc{b}")
-            for c in range(CHUNKS):
-                m_bf = keep.tile([P, P, PACK], BF16, name=f"m_bf{b}{c}", align_bytes=64)
-                m_codes = keep.tile([P, P], U32, name=f"m_codes{b}{c}", align_bytes=64)
-                m_scales = keep.tile([P, P], U8, name=f"m_scales{b}{c}", align_bytes=64)
-                nc.scalar.copy(
-                    out=m_bf[:].rearrange("p (n i) t -> p n t i", i=4),
-                    in_=m_source(c, b).rearrange("p t (n i) -> p n t i", i=4),
-                )
-                nc.vector.quantize_mx(
-                    out=m_codes[:].bitcast(E4M3),
-                    scales=m_scales[:],
-                    in_=m_bf[:].rearrange("p n t -> p (n t)"),
-                )
-                nc.tensor.matmul_mx(
-                    out=acc[:],
-                    lhsT=m_codes[:].bitcast(E4M3),
-                    lhsT_scale=m_scales[:],
-                    rhs=g_codes[c][:].bitcast(E5M2),
-                    rhs_scale=g_scales[c][:],
-                    start=(c == 0),
-                    stop=(c == CHUNKS - 1),
-                )
             dense = keep.tile([P, N], F32, name=f"dense{b}")
-            nc.scalar.copy(out=dense[:], in_=acc[:])
+            nc.scalar.copy(out=dense[:], in_=acc[b][:])
             nc.vector.tensor_copy(out=window[b][:].indirect(offsets[:]), in_=dense[:])
             nc.sync.dma_start(out=out[b * P : (b + 1) * P, :], in_=window[b][:])
 
-        for c in range(CHUNKS):
-            scores(c)
-        for c, engines in enumerate((("vector",) * 4, ("scalar", "scalar", "vector", "scalar"))):
-            for t in range(PACK):
-                weighted_targets(c, t, engines[t])
-            for h, engine in ((0, "scalar"), (1, "vector")):
-                gradient(c, h)
-                interleave_gradient(c, h, engine)
-                quantise_gradient(c, h)
-        for b in range(D // P):
-            output_block(b)
+        gather(0, 0, 8)
+        gather(1, 0, 8)
+        gather(2, 0, 8)
+        gather(3, 0, 8)
+        quantise_w(0, 8)
+        interleave_x(0, 0, 3, "scalar")
+        interleave_x(0, 3, 4, "vector")
+        interleave_x(0, 4, 8, "vector")
+        quantise_x(0, 0, 1)
+        quantise_x(0, 1, 2)
+        quantise_x(0, 2, 4)
+        scores(0, 0)
+        scores(0, 1)
+        scores(0, 2)
+        scores(0, 3)
+        interleave_x(1, 0, 2, "scalar")
+        interleave_x(1, 2, 4, "vector")
+        interleave_x(1, 4, 8, "vector")
+        quantise_x(1, 0, 2)
+        quantise_x(1, 2, 4)
+        weighted_targets(0, 0, 0, 8, "vector")
+        weighted_targets(0, 1, 0, 8, "vector")
+        gradient(0, 0, 0, 8)
+        gradient(0, 1, 0, 8)
+        weighted_targets(0, 2, 0, 8, "vector")
+        weighted_targets(0, 3, 0, 8, "vector")
+        gradient(0, 2, 0, 8)
+        gradient(0, 3, 0, 8)
+        scores(1, 0)
+        scores(1, 1)
+        scores(1, 2)
+        scores(1, 3)
+        weighted_targets(1, 0, 0, 8, "scalar")
+        weighted_targets(1, 1, 0, 8, "vector")
+        weighted_targets(1, 2, 0, 8, "vector")
+        weighted_targets(1, 3, 0, 8, "vector")
+        gradient(1, 0, 0, 8)
+        gradient(1, 1, 0, 8)
+        gradient(1, 2, 0, 4)
+        gradient(1, 3, 0, 4)
+        gradient(1, 2, 4, 8)
+        gradient(1, 3, 4, 8)
+        interleave_gradient(0, 0, 4, "scalar")
+        interleave_gradient(0, 4, 8, "scalar")
+        quantise_gradient(0, 0, 4)
+        quantise_gradient(0, 4, 8)
+        interleave_m(0, 0, "scalar")
+        interleave_m(0, 1, "vector")
+        quantise_m(0, 0)
+        quantise_m(0, 1)
+        product(0, 0)
+        interleave_gradient(1, 0, 4, "scalar")
+        interleave_gradient(1, 4, 8, "vector")
+        quantise_gradient(1, 0, 4)
+        quantise_gradient(1, 4, 8)
+        product(0, 1)
+        output_block(0)
+        interleave_m(1, 0, "scalar")
+        interleave_m(1, 1, "vector")
+        quantise_m(1, 0)
+        quantise_m(1, 1)
+        product(1, 0)
+        product(1, 1)
+        output_block(1)
+        interleave_m(2, 0, "scalar")
+        interleave_m(2, 1, "vector")
+        quantise_m(2, 0)
+        quantise_m(2, 1)
+        product(2, 0)
+        product(2, 1)
+        output_block(2)
+        interleave_m(3, 0, "scalar")
+        interleave_m(3, 1, "vector")
+        quantise_m(3, 0)
+        quantise_m(3, 1)
+        product(3, 0)
+        product(3, 1)
+        output_block(3)

@@ -315,21 +315,21 @@ def tile_attend_gnce_w_kernel(tc, xT, wT, y, wt, xm, offs, out):
         quantise_gradient(1, 4, 8)
         product(0, 1)
         output_block(0)
-        interleave_m(1, 0, "scalar")
+        interleave_m(1, 0, "vector")
         interleave_m(1, 1, "vector")
         quantise_m(1, 0)
         quantise_m(1, 1)
         product(1, 0)
         product(1, 1)
         output_block(1)
-        interleave_m(2, 0, "scalar")
+        interleave_m(2, 0, "vector")
         interleave_m(2, 1, "vector")
         quantise_m(2, 0)
         quantise_m(2, 1)
         product(2, 0)
         product(2, 1)
         output_block(2)
-        interleave_m(3, 0, "scalar")
+        interleave_m(3, 0, "vector")
         interleave_m(3, 1, "vector")
         quantise_m(3, 0)
         quantise_m(3, 1)

@@ -60,8 +60,15 @@ def tile_attend_gnce_w_kernel(tc, xT, wT, y, wt, xm, offs, out):
         def load_x_whole(c):
             x_whole = keep.tile([P, PACK, K_PASS], F32, name=f"x_whole{c}")
             nc.sync.dma_start(out=x_whole[:], in_=x_rows[:, :, c * K_PASS : (c + 1) * K_PASS])
+            x_raw[c] = x_whole[:]
             for h in range(2):
                 x_raw[c, h] = x_whole[:, :, h * (K_PASS // 2) : (h + 1) * (K_PASS // 2)]
+
+        def load_x_part(lo, hi):
+            part = keep.tile([P, PACK, (hi - lo) * UNIT], F32, name=f"x_part{lo}")
+            nc.sync.dma_start(out=part[:], in_=x_rows[:, :, K_PASS + lo * UNIT : K_PASS + hi * UNIT])
+            for unit in range(lo, hi):
+                x_raw["part", unit] = (part, lo)
 
         def load_y(c, u):
             y_raw[c, u] = keep.tile([P, 2, N], F32, name=f"y_raw{c}{u}")
@@ -79,8 +86,8 @@ def tile_attend_gnce_w_kernel(tc, xT, wT, y, wt, xm, offs, out):
         nc.sync.dma_start(out=table[2][:], in_=w_rows[:, 2, :])
         nc.sync.dma_start(out=table[3][:], in_=w_rows[:, 3, :])
         load_x_whole(0)
-        load_x(1, 0)
-        load_x(1, 1)
+        load_x_part(0, 6)
+        load_x_part(6, 8)
         load_y(0, 0)
         load_y(0, 1)
         load_y(1, 0)
@@ -123,6 +130,21 @@ def tile_attend_gnce_w_kernel(tc, xT, wT, y, wt, xm, offs, out):
                 engine,
                 x_bf[c][:, :, lo * 16 : hi * 16, :].rearrange("p t m j -> p m j t"),
                 x_raw[c, h][:, :, (lo - 4 * h) * UNIT : (hi - 4 * h) * UNIT].rearrange("p j (m t) -> p m j t", t=PACK),
+            )
+
+        def interleave_x_pair(c, u, engine):
+            copy_on(
+                engine,
+                x_bf[c][:, 2 * u : 2 * u + 2, :, :].rearrange("p t m j -> p m j t"),
+                x_raw[c].rearrange("p j (m t) -> p m j t", t=PACK)[:, :, :, 2 * u : 2 * u + 2],
+            )
+
+        def interleave_x_part(lo, hi, engine):
+            part, first = x_raw["part", lo]
+            copy_on(
+                engine,
+                x_bf[1][:, :, lo * 16 : hi * 16, :].rearrange("p t m j -> p m j t"),
+                part[:, :, (lo - first) * UNIT : (hi - first) * UNIT].rearrange("p j (m t) -> p m j t", t=PACK),
             )
 
         def quantise_x(c, lo, hi):
@@ -263,9 +285,8 @@ def tile_attend_gnce_w_kernel(tc, xT, wT, y, wt, xm, offs, out):
         gather(2, 0, 8)
         gather(3, 0, 8)
         quantise_w(0, 8)
-        interleave_x(0, 0, 3, "scalar")
-        interleave_x(0, 3, 4, "vector")
-        interleave_x(0, 4, 8, "vector")
+        interleave_x_pair(0, 0, "vector")
+        interleave_x_pair(0, 1, "scalar")
         quantise_x(0, 0, 1)
         quantise_x(0, 1, 2)
         quantise_x(0, 2, 4)
@@ -273,9 +294,8 @@ def tile_attend_gnce_w_kernel(tc, xT, wT, y, wt, xm, offs, out):
         scores(0, 1)
         scores(0, 2)
         scores(0, 3)
-        interleave_x(1, 0, 2, "scalar")
-        interleave_x(1, 2, 4, "vector")
-        interleave_x(1, 4, 8, "vector")
+        interleave_x_part(0, 6, "vector")
+        interleave_x_part(6, 8, "vector")
         quantise_x(1, 0, 2)
         quantise_x(1, 2, 4)
         weighted_targets(0, 0, 0, 8, "vector")

@@ -274,6 +274,28 @@ def tile_attend_gnce_w_kernel(tc, xT, wT, y, wt, xm, offs, out):
                 stop=(c == CHUNKS - 1),
             )
 
+        def warm_up(h):
+            spare = score_banks.tile([P, N], F32, name="bank")
+            nc.tensor.matmul_mx(
+                out=spare[:],
+                lhsT=g_codes[0][:, h * HALF : h * HALF + P].bitcast(E5M2),
+                lhsT_scale=g_scales[0][:, h * HALF : h * HALF + P],
+                rhs=w_codes[:].bitcast(E4M3),
+                rhs_scale=w_scales[:],
+                start=True,
+                stop=True,
+            )
+
+        def output_block_halves(b):
+            dense = keep.tile([P, N], F32, name=f"dense{b}")
+            for h in range(2):
+                nc.scalar.copy(out=dense[:, slots(4 * h, 4 * h + 4)], in_=acc[b][:, slots(4 * h, 4 * h + 4)])
+                nc.vector.tensor_copy(
+                    out=window[b][:].indirect(offsets[:, h * HALF // 16 : (h + 1) * HALF // 16]),
+                    in_=dense[:, slots(4 * h, 4 * h + 4)],
+                )
+            nc.sync.dma_start(out=out[b * P : (b + 1) * P, :], in_=window[b][:])
+
         def output_block(b):
             dense = keep.tile([P, N], F32, name=f"dense{b}")
             nc.scalar.copy(out=dense[:], in_=acc[b][:])
@@ -323,6 +345,8 @@ def tile_attend_gnce_w_kernel(tc, xT, wT, y, wt, xm, offs, out):
         interleave_gradient(0, 0, 4, "scalar")
         interleave_gradient(0, 4, 8, "scalar")
         quantise_gradient(0, 0, 4)
+        warm_up(0)
+        warm_up(0)
         quantise_gradient(0, 4, 8)
         interleave_m(0, 0, "scalar")
         interleave_m(0, 1, "vector")

@@ -326,8 +326,10 @@ def tile_attend_gnce_w_kernel(tc, xT, wT, y, wt, xm, offs, out):
         gradient(0, 1, 0, 8)
         weighted_targets(0, 2, 0, 8, "vector")
         weighted_targets(0, 3, 0, 8, "vector")
-        gradient(0, 2, 0, 8)
-        gradient(0, 3, 0, 8)
+        gradient(0, 2, 0, 4)
+        gradient(0, 3, 0, 4)
+        gradient(0, 2, 4, 8)
+        gradient(0, 3, 4, 8)
         scores(1, 0)
         scores(1, 1)
         scores(1, 2)
@@ -336,27 +338,30 @@ def tile_attend_gnce_w_kernel(tc, xT, wT, y, wt, xm, offs, out):
         weighted_targets(1, 1, 0, 8, "vector")
         weighted_targets(1, 2, 0, 8, "vector")
         weighted_targets(1, 3, 0, 8, "vector")
-        gradient(1, 0, 0, 8)
-        gradient(1, 1, 0, 8)
+        gradient(1, 0, 0, 4)
+        gradient(1, 1, 0, 4)
         gradient(1, 2, 0, 4)
         gradient(1, 3, 0, 4)
-        gradient(1, 2, 4, 8)
-        gradient(1, 3, 4, 8)
+        gradient(1, 0, 4, 8)
         interleave_gradient(0, 0, 4, "scalar")
-        interleave_gradient(0, 4, 8, "scalar")
         quantise_gradient(0, 0, 4)
         warm_up(0)
         warm_up(0)
-        quantise_gradient(0, 4, 8)
+        warm_up(0)
+        gradient(1, 1, 4, 8)
+        gradient(1, 2, 4, 8)
+        gradient(1, 3, 4, 8)
+        interleave_gradient(0, 4, 8, "scalar")
         interleave_m(0, 0, "scalar")
-        interleave_m(0, 1, "vector")
-        quantise_m(0, 0)
-        quantise_m(0, 1)
-        product(0, 0)
         interleave_gradient(1, 0, 4, "scalar")
+        interleave_m(0, 1, "scalar")
+        quantise_gradient(0, 4, 8)
+        quantise_m(0, 0)
+        product(0, 0)
         interleave_gradient(1, 4, 8, "vector")
         quantise_gradient(1, 0, 4)
         quantise_gradient(1, 4, 8)
+        quantise_m(0, 1)
         product(0, 1)
         output_block(0)
         interleave_m(1, 0, "vector")

@@ -70,6 +70,11 @@ def tile_attend_gnce_w_kernel(tc, xT, wT, y, wt, xm, offs, out):
             for unit in range(lo, hi):
                 x_raw["part", unit] = (part, lo)
 
+        def load_y_row(c, t):
+            row = keep.tile([P, N], F32, name=f"y_row{c}{t}")
+            nc.sync.dma_start(out=row[:], in_=y_rows[c, :, t, :])
+            y_raw["row", c, t] = row
+
         def load_y(c, u):
             y_raw[c, u] = keep.tile([P, 2, N], F32, name=f"y_raw{c}{u}")
             nc.sync.dma_start(out=y_raw[c, u][:], in_=y_rows[c, :, 2 * u : 2 * u + 2, :])
@@ -88,7 +93,8 @@ def tile_attend_gnce_w_kernel(tc, xT, wT, y, wt, xm, offs, out):
         load_x_whole(0)
         load_x_part(0, 6)
         load_x_part(6, 8)
-        load_y(0, 0)
+        load_y_row(0, 0)
+        load_y_row(0, 1)
         load_y(0, 1)
         load_y(1, 0)
         load_y(1, 1)
@@ -147,6 +153,15 @@ def tile_attend_gnce_w_kernel(tc, xT, wT, y, wt, xm, offs, out):
                 part[:, :, (lo - first) * UNIT : (hi - first) * UNIT].rearrange("p j (m t) -> p m j t", t=PACK),
             )
 
+        def interleave_x_part_pair(lo, hi, u, engine):
+            part, first = x_raw["part", lo]
+            rows = part[:, :, (lo - first) * UNIT : (hi - first) * UNIT].rearrange("p j (m t) -> p m j t", t=PACK)
+            copy_on(
+                engine,
+                x_bf[1][:, 2 * u : 2 * u + 2, lo * 16 : hi * 16, :].rearrange("p t m j -> p m j t"),
+                rows[:, :, :, 2 * u : 2 * u + 2],
+            )
+
         def quantise_x(c, lo, hi):
             cols = slice(lo * P, hi * P)
             nc.vector.quantize_mx(
@@ -180,10 +195,16 @@ def tile_attend_gnce_w_kernel(tc, xT, wT, y, wt, xm, offs, out):
                 score_product(bank[:, i, :], c, 2 * u + i, cols)
             nc.scalar.activation(out=sig[c][:, 2 * u : 2 * u + 2, cols], in_=bank[:], func=ACT.Sigmoid)
 
+        def scores_narrow(c, t, h):
+            bank = score_banks.tile([P, HALF], F32, name="bank")
+            cols = slots(4 * h, 4 * h + 4)
+            score_product(bank[:], c, t, cols)
+            nc.scalar.activation(out=sig[c][:, t, cols], in_=bank[:], func=ACT.Sigmoid)
+
         yw = [keep.tile([P, PACK, N], F32, name=f"yw{c}") for c in range(CHUNKS)]
 
         def weighted_targets(c, t, lo, hi, engine):
-            src = y_raw[c, t // 2][:, t % 2, slots(lo, hi)]
+            src = y_raw["row", c, t][:, slots(lo, hi)] if ("row", c, t) in y_raw else y_raw[c, t // 2][:, t % 2, slots(lo, hi)]
             dst = yw[c][:, t, slots(lo, hi)]
             if engine == "vector":
                 nc.vector.tensor_scalar(out=dst, in0=src, scalar1=weight[:, c, t : t + 1], scalar2=None, op0=ALU.mult)
@@ -317,7 +338,8 @@ def tile_attend_gnce_w_kernel(tc, xT, wT, y, wt, xm, offs, out):
         scores(0, 2)
         scores(0, 3)
         interleave_x_part(0, 6, "vector")
-        interleave_x_part(6, 8, "vector")
+        interleave_x_part_pair(6, 8, 0, "vector")
+        interleave_x_part_pair(6, 8, 1, "vector")
         quantise_x(1, 0, 2)
         quantise_x(1, 2, 4)
         weighted_targets(0, 0, 0, 8, "vector")

@@ -1,6 +1,7 @@
 from contextlib import ExitStack
 
 import concourse.mybir as mybir
+from concourse.masks import make_identity
 
 D, R, T, N = 512, 1024, 2048, 512
 FLOPS = 2 * 2 * D * R * N
@@ -38,11 +39,24 @@ def tile_attend_gnce_w_kernel(tc, xT, wT, y, wt, xm, offs, out):
                 nc.scalar.copy(out=dst, in_=src)
 
         weight = keep.tile([P, CHUNKS, PACK], F32, name="weight")
-        nc.scalar.dma_start(out=weight[:], in_=wt[0].rearrange("(c p t) o -> p c (t o)", c=CHUNKS, t=PACK))
+        apart = P // CHUNKS
+        wt_rows = keep.tile([P, K_PASS], F32, name="wt_rows")
+        nc.scalar.dma_start(out=wt_rows[0:P:apart, :], in_=wt[0].rearrange("(c k) o -> c (k o)", c=CHUNKS))
         warm_in = keep.tile([P, 1], F32, name="warm_in")
         warm_out = keep.tile([P, 1], F32, name="warm_out")
         nc.gpsimd.memset(warm_in[:], 0.0)
         nc.scalar.activation(out=warm_out[:], in_=warm_in[:], func=ACT.Sigmoid)
+        identity = keep.tile([P, P], F32, name="identity")
+        make_identity(nc, identity[:])
+        wt_dealt = keep.tile([P, PACK, P], F32, name="wt_dealt")
+        nc.gpsimd.memset(wt_dealt[:], 0.0)
+        for c in range(CHUNKS):
+            row = slice(c * apart, c * apart + 1)
+            nc.scalar.copy(out=wt_dealt[row, :, :], in_=wt_rows[row, :].rearrange("c (p t) -> c t p", t=PACK))
+        wt_bank = score_banks.tile([P, PACK, P], F32, name="bank")
+        for t in range(PACK):
+            nc.tensor.transpose(wt_bank[:, t, :], wt_dealt[:, t, :], identity[:])
+        nc.scalar.copy(out=weight[:], in_=wt_bank[:].rearrange("p t (c k) -> p c t k", c=CHUNKS)[:, :, :, 0])
         offsets = lists.tile([P, N // 16], U16, name="offsets")
         w_rows = wT.rearrange("(p t) c -> p t c", t=PACK)
         table = [keep.tile([P, T], F32, name=f"table{t}") for t in range(PACK)]
@@ -215,7 +229,6 @@ def tile_attend_gnce_w_kernel(tc, xT, wT, y, wt, xm, offs, out):
         g_scales = [keep.tile([P, N], U8, name=f"g_scales{c}", align_bytes=64) for c in range(CHUNKS)]
         g_rows = [keep.tile([P, PACK, N], BF16, name=f"g_rows{c}") for c in range(CHUNKS)]
         g_bf = [keep.tile([P, N, PACK], BF16, name=f"g_bf{c}", tag=f"g_bf{c}", align_bytes=64) for c in range(CHUNKS)]
-        diff = [keep.tile([P, PACK, N], F32, name=f"diff{c}") for c in range(CHUNKS)]
 
         def gradient(c, t, lo, hi):
             nc.vector.scalar_tensor_tensor(
@@ -232,23 +245,6 @@ def tile_attend_gnce_w_kernel(tc, xT, wT, y, wt, xm, offs, out):
                 engine,
                 g_bf[c][:, slots(lo, hi), :].rearrange("p (n i) t -> p n t i", i=4),
                 g_rows[c][:, :, slots(lo, hi)].rearrange("p t (n i) -> p n t i", i=4),
-            )
-
-        def difference(c, u, lo, hi):
-            nc.vector.tensor_tensor(
-                out=diff[c][:, 2 * u : 2 * u + 2, slots(lo, hi)],
-                in0=sig[c][:, 2 * u : 2 * u + 2, slots(lo, hi)],
-                in1=y_raw[c, u][:, :, slots(lo, hi)],
-                op=ALU.subtract,
-            )
-
-        def weigh_interleave(c, lo, hi):
-            groups = (hi - lo) * UNIT // 4
-            nc.vector.tensor_tensor(
-                out=g_bf[c][:, slots(lo, hi), :].rearrange("p (n i) t -> p n t i", i=4),
-                in0=diff[c][:, :, slots(lo, hi)].rearrange("p t (n i) -> p n t i", i=4),
-                in1=weight[:, c, :].rearrange("p (n t i) -> p n t i", n=1, i=1).to_broadcast([P, groups, PACK, 4]),
-                op=ALU.mult,
             )
 
         def quantise_gradient(c, lo, hi):

@@ -40,7 +40,7 @@ def tile_attend_gnce_w_kernel(tc, xT, wT, y, wt, xm, offs, out):
 
         weight = keep.tile([P, CHUNKS, PACK], F32, name="weight")
         apart = P // CHUNKS
-        wt_rows = keep.tile([P, K_PASS], F32, name="wt_rows")
+        wt_rows = keep.tile([P, K_PASS], F32, name="wt_rows", align_bytes=256)
         nc.scalar.dma_start(out=wt_rows[0:P:apart, :], in_=wt[0].rearrange("(c k) o -> c (k o)", c=CHUNKS))
         warm_in = keep.tile([P, 1], F32, name="warm_in")
         warm_out = keep.tile([P, 1], F32, name="warm_out")
@@ -59,7 +59,7 @@ def tile_attend_gnce_w_kernel(tc, xT, wT, y, wt, xm, offs, out):
         nc.scalar.copy(out=weight[:], in_=wt_bank[:].rearrange("p t (c k) -> p c t k", c=CHUNKS)[:, :, :, 0])
         offsets = lists.tile([P, N // 16], U16, name="offsets")
         w_rows = wT.rearrange("(p t) c -> p t c", t=PACK)
-        table = [keep.tile([P, T], F32, name=f"table{t}") for t in range(PACK)]
+        table = [keep.tile([P, T], F32, name=f"table{t}", align_bytes=256) for t in range(PACK)]
         x_rows = xT[0].rearrange("(p j) r -> p j r", j=PACK)
         y_rows = y[0].rearrange("(c p t) i -> c p t i", c=CHUNKS, t=PACK)
         m_rows = xm[0].rearrange("(c p t) d -> c p t d", c=CHUNKS, t=PACK)
@@ -72,29 +72,29 @@ def tile_attend_gnce_w_kernel(tc, xT, wT, y, wt, xm, offs, out):
             x_raw[c, h] = x_half[:]
 
         def load_x_whole(c):
-            x_whole = keep.tile([P, PACK, K_PASS], F32, name=f"x_whole{c}")
+            x_whole = keep.tile([P, PACK, K_PASS], F32, name=f"x_whole{c}", align_bytes=256)
             nc.sync.dma_start(out=x_whole[:], in_=x_rows[:, :, c * K_PASS : (c + 1) * K_PASS])
             x_raw[c] = x_whole[:]
             for h in range(2):
                 x_raw[c, h] = x_whole[:, :, h * (K_PASS // 2) : (h + 1) * (K_PASS // 2)]
 
         def load_x_part(lo, hi):
-            part = keep.tile([P, PACK, (hi - lo) * UNIT], F32, name=f"x_part{lo}")
+            part = keep.tile([P, PACK, (hi - lo) * UNIT], F32, name=f"x_part{lo}", align_bytes=256)
             nc.sync.dma_start(out=part[:], in_=x_rows[:, :, K_PASS + lo * UNIT : K_PASS + hi * UNIT])
             for unit in range(lo, hi):
                 x_raw["part", unit] = (part, lo)
 
         def load_y_row(c, t):
-            row = keep.tile([P, N], F32, name=f"y_row{c}{t}")
+            row = keep.tile([P, N], F32, name=f"y_row{c}{t}", align_bytes=256)
             nc.sync.dma_start(out=row[:], in_=y_rows[c, :, t, :])
             y_raw["row", c, t] = row
 
         def load_y(c, u):
-            y_raw[c, u] = keep.tile([P, 2, N], F32, name=f"y_raw{c}{u}")
+            y_raw[c, u] = keep.tile([P, 2, N], F32, name=f"y_raw{c}{u}", align_bytes=256)
             nc.sync.dma_start(out=y_raw[c, u][:], in_=y_rows[c, :, 2 * u : 2 * u + 2, :])
 
         def load_m(c, h):
-            m_half = keep.tile([P, PACK, D // 2], F32, name=f"m_half{c}{h}")
+            m_half = keep.tile([P, PACK, D // 2], F32, name=f"m_half{c}{h}", align_bytes=256)
             nc.sync.dma_start(out=m_half[:], in_=m_rows[c, :, :, h * (D // 2) : (h + 1) * (D // 2)])
             for i in range(2):
                 m_raw[2 * h + i, c] = m_half[:, :, i * P : (i + 1) * P]
@@ -117,7 +117,7 @@ def tile_attend_gnce_w_kernel(tc, xT, wT, y, wt, xm, offs, out):
         load_m(0, 1)
         load_m(1, 1)
 
-        window = [keep.tile([P, T], F32, name=f"window{b}") for b in range(D // P)]
+        window = [keep.tile([P, T], F32, name=f"window{b}", align_bytes=256) for b in range(D // P)]
         for b in range(D // P):
             (nc.vector if b < 2 else nc.gpsimd).memset(window[b][:], 0.0)
 

@@ -22,6 +22,7 @@ K_PASS = P * PACK
 CHUNKS = R // K_PASS
 HALF = N // 2
 UNIT = 64
+DIRECT = (4, 4)
 
 
 def tile_attend_gnce_w_kernel(tc, xT, wT, y, wt, xm, offs, out):
@@ -29,8 +30,7 @@ def tile_attend_gnce_w_kernel(tc, xT, wT, y, wt, xm, offs, out):
     with ExitStack() as ctx:
         lists = ctx.enter_context(tc.tile_pool(name="lists", bufs=1))
         keep = ctx.enter_context(tc.tile_pool(name="keep", bufs=1))
-        score_banks = ctx.enter_context(tc.psum_pool(name="score_banks", bufs=4))
-        grad_banks = ctx.enter_context(tc.psum_pool(name="grad_banks", bufs=1))
+        banks = ctx.enter_context(tc.psum_pool(name="banks", bufs=8))
 
         def copy_on(engine, dst, src):
             if engine == "vector":
@@ -53,10 +53,23 @@ def tile_attend_gnce_w_kernel(tc, xT, wT, y, wt, xm, offs, out):
         for c in range(CHUNKS):
             row = slice(c * apart, c * apart + 1)
             nc.scalar.copy(out=wt_dealt[row, :, :], in_=wt_rows[row, :].rearrange("c (p t) -> c t p", t=PACK))
-        wt_bank = score_banks.tile([P, PACK, P], F32, name="bank")
+        wt_bank = banks.tile([P, PACK, P], F32, name="bank")
         for t in range(PACK):
             nc.tensor.transpose(wt_bank[:, t, :], wt_dealt[:, t, :], identity[:])
         nc.scalar.copy(out=weight[:], in_=wt_bank[:].rearrange("p t (c k) -> p c t k", c=CHUNKS)[:, :, :, 0])
+        spread = keep.tile([P, CHUNKS, PACK, P], F32, name="spread")
+        nc.scalar.activation(
+            out=spread[:].rearrange("p c t k -> p (c t) k"),
+            in_=weight[:].rearrange("p c t -> p (c t)").unsqueeze(2).to_broadcast([P, CHUNKS * PACK, P]),
+            func=ACT.Copy,
+            scale=-1.0,
+        )
+        minus_wt = [keep.tile([P, 2 * P, 2], F32, name=f"minus_wt{c}") for c in range(CHUNKS)]
+        for c in range(CHUNKS):
+            spread_bank = banks.tile([P, 2, 2, P], F32, name="bank")
+            for t in range(PACK):
+                nc.tensor.transpose(spread_bank[:, t % 2, t // 2, :], spread[:, c, t, :], identity[:])
+            nc.scalar.copy(out=minus_wt[c][:], in_=spread_bank[:].rearrange("p e u m -> p (u m) e"))
         offsets = lists.tile([P, N // 16], U16, name="offsets")
         w_rows = wT.rearrange("(p t) c -> p t c", t=PACK)
         table = [keep.tile([P, T], F32, name=f"table{t}", align_bytes=256) for t in range(PACK)]
@@ -93,11 +106,11 @@ def tile_attend_gnce_w_kernel(tc, xT, wT, y, wt, xm, offs, out):
             y_raw[c, u] = keep.tile([P, 2, N], F32, name=f"y_raw{c}{u}", align_bytes=256)
             nc.sync.dma_start(out=y_raw[c, u][:], in_=y_rows[c, :, 2 * u : 2 * u + 2, :])
 
-        def load_m(c, h):
-            m_half = keep.tile([P, PACK, D // 2], F32, name=f"m_half{c}{h}", align_bytes=256)
-            nc.sync.dma_start(out=m_half[:], in_=m_rows[c, :, :, h * (D // 2) : (h + 1) * (D // 2)])
-            for i in range(2):
-                m_raw[2 * h + i, c] = m_half[:, :, i * P : (i + 1) * P]
+        def load_m(c, lo, hi):
+            m_part = keep.tile([P, PACK, (hi - lo) * P], F32, name=f"m_part{c}{lo}", align_bytes=256)
+            nc.sync.dma_start(out=m_part[:], in_=m_rows[c, :, :, lo * P : hi * P])
+            for b in range(lo, hi):
+                m_raw[b, c] = m_part[:, :, (b - lo) * P : (b - lo + 1) * P]
 
         nc.sync.dma_start(out=table[0][:], in_=w_rows[:, 0, :])
         nc.sync.dma_start(offsets[:], offs)
@@ -112,10 +125,12 @@ def tile_attend_gnce_w_kernel(tc, xT, wT, y, wt, xm, offs, out):
         load_y(0, 1)
         load_y(1, 0)
         load_y(1, 1)
-        load_m(0, 0)
-        load_m(1, 0)
-        load_m(0, 1)
-        load_m(1, 1)
+        load_m(0, 0, 1)
+        load_m(1, 0, 1)
+        load_m(0, 1, 2)
+        load_m(1, 1, 2)
+        load_m(0, 2, 4)
+        load_m(1, 2, 4)
 
         window = [keep.tile([P, T], F32, name=f"window{b}", align_bytes=256) for b in range(D // P)]
         for b in range(D // P):
@@ -186,6 +201,8 @@ def tile_attend_gnce_w_kernel(tc, xT, wT, y, wt, xm, offs, out):
 
         sig = [keep.tile([P, PACK, N], F32, name=f"sig{c}") for c in range(CHUNKS)]
 
+        score_bank = {}
+
         def score_product(dst, c, t, cols):
             nc.tensor.matmul_mx(
                 out=dst,
@@ -198,19 +215,20 @@ def tile_attend_gnce_w_kernel(tc, xT, wT, y, wt, xm, offs, out):
             )
 
         def scores(c, t):
-            bank = score_banks.tile([P, N], F32, name="bank")
+            bank = banks.tile([P, N], F32, name="bank")
+            score_bank[c, t] = bank
             score_product(bank[:], c, t, slots(0, 8))
-            nc.scalar.activation(out=sig[c][:, t, :], in_=bank[:], func=ACT.Sigmoid)
+            nc.scalar.activation(out=sig[c][:, t, :], in_=bank[:], func=ACT.Sigmoid, scale=-1.0)
 
         def scores_half(c, u, h):
-            bank = score_banks.tile([P, 2, HALF], F32, name="bank")
+            bank = banks.tile([P, 2, HALF], F32, name="bank")
             cols = slots(4 * h, 4 * h + 4)
             for i in range(2):
                 score_product(bank[:, i, :], c, 2 * u + i, cols)
             nc.scalar.activation(out=sig[c][:, 2 * u : 2 * u + 2, cols], in_=bank[:], func=ACT.Sigmoid)
 
         def scores_narrow(c, t, h):
-            bank = score_banks.tile([P, HALF], F32, name="bank")
+            bank = banks.tile([P, HALF], F32, name="bank")
             cols = slots(4 * h, 4 * h + 4)
             score_product(bank[:], c, t, cols)
             nc.scalar.activation(out=sig[c][:, t, cols], in_=bank[:], func=ACT.Sigmoid)
@@ -221,29 +239,41 @@ def tile_attend_gnce_w_kernel(tc, xT, wT, y, wt, xm, offs, out):
             src = y_raw["row", c, t][:, slots(lo, hi)] if ("row", c, t) in y_raw else y_raw[c, t // 2][:, t % 2, slots(lo, hi)]
             dst = yw[c][:, t, slots(lo, hi)]
             if engine == "vector":
-                nc.vector.tensor_scalar(out=dst, in0=src, scalar1=weight[:, c, t : t + 1], scalar2=None, op0=ALU.mult)
+                nc.vector.tensor_scalar(
+                    out=dst, in0=src, scalar1=spread[:, c, t, 0:1], scalar2=weight[:, c, t : t + 1], op0=ALU.mult, op1=ALU.add
+                )
             else:
-                nc.scalar.activation(out=dst, in_=src, func=ACT.Copy, scale=weight[:, c, t : t + 1])
+                nc.scalar.activation(
+                    out=dst, in_=src, func=ACT.Identity, scale=spread[:, c, t, 0:1], bias=weight[:, c, t : t + 1]
+                )
 
         g_codes = [keep.tile([P, N], U32, name=f"g_codes{c}", align_bytes=64) for c in range(CHUNKS)]
         g_scales = [keep.tile([P, N], U8, name=f"g_scales{c}", align_bytes=64) for c in range(CHUNKS)]
         g_rows = [keep.tile([P, PACK, N], BF16, name=f"g_rows{c}") for c in range(CHUNKS)]
-        g_bf = [keep.tile([P, N, PACK], BF16, name=f"g_bf{c}", tag=f"g_bf{c}", align_bytes=64) for c in range(CHUNKS)]
+        g_half = {
+            (c, h): keep.tile([P, HALF, PACK], BF16, name=f"g_bf{c}{h}", tag=f"g_bf{c}{h}", align_bytes=64)
+            for c in range(CHUNKS)
+            for h in range(2)
+        }
+
+        def g_bf(c, lo, hi):
+            h = lo // 4
+            return g_half[c, h][:, slots(lo - 4 * h, hi - 4 * h), :]
 
         def gradient(c, t, lo, hi):
             nc.vector.scalar_tensor_tensor(
                 out=g_rows[c][:, t, slots(lo, hi)],
                 in0=sig[c][:, t, slots(lo, hi)],
-                scalar=weight[:, c, t : t + 1],
+                scalar=spread[:, c, t, 0:1],
                 in1=yw[c][:, t, slots(lo, hi)],
                 op0=ALU.mult,
-                op1=ALU.subtract,
+                op1=ALU.add,
             )
 
         def interleave_gradient(c, lo, hi, engine):
             copy_on(
                 engine,
-                g_bf[c][:, slots(lo, hi), :].rearrange("p (n i) t -> p n t i", i=4),
+                g_bf(c, lo, hi).rearrange("p (n i) t -> p n t i", i=4),
                 g_rows[c][:, :, slots(lo, hi)].rearrange("p t (n i) -> p n t i", i=4),
             )
 
@@ -251,8 +281,47 @@ def tile_attend_gnce_w_kernel(tc, xT, wT, y, wt, xm, offs, out):
             nc.vector.quantize_mx(
                 out=g_codes[c][:, slots(lo, hi)].bitcast(E5M2),
                 scales=g_scales[c][:, slots(lo, hi)],
-                in_=g_bf[c][:, slots(lo, hi), :].rearrange("p n t -> p (n t)"),
+                in_=g_bf(c, lo, hi).rearrange("p n t -> p (n t)"),
             )
+
+        sums, g_turned, word_bank = {}, {}, {}
+
+        def y_of(c, t, cols):
+            return y_raw["row", c, t][:, cols] if ("row", c, t) in y_raw else y_raw[c, t // 2][:, t % 2, cols]
+
+        def reuse(c, s, c2, t2):
+            sums[c, s] = score_bank[c2, t2]
+
+        def warm_in(c, s):
+            score_product(sums[c, s][:], 0, 0, slots(0, 8))
+
+        def turn(c, t, blocks=None):
+            for s in blocks or range(DIRECT[c] // 2, N // P):
+                if (c, s) not in sums:
+                    sums[c, s] = banks.tile([P, N], F32, name="bank")
+                cols = slice(s * P, (s + 1) * P)
+                dst = sums[c, s][:].rearrange("p (e u m) -> p e u m", e=2, u=2)[:, t % 2, t // 2, :]
+                nc.tensor.matmul(dst, lhsT=sig[c][:, t, cols], rhs=identity[:], start=True, stop=False, is_transpose=True)
+                nc.tensor.matmul(dst, lhsT=y_of(c, t, cols), rhs=identity[:], start=False, stop=True, is_transpose=True)
+
+        def close(c, s):
+            g_turned[c, s] = keep.tile([P, 2 * P, 2], BF16, name=f"g_turned{c}{s}")
+            nc.vector.scalar_tensor_tensor(
+                out=g_turned[c, s][:],
+                in0=sums[c, s][:].rearrange("p (e w) -> p w e", e=2),
+                scalar=1.0,
+                in1=minus_wt[c][:],
+                op0=ALU.subtract,
+                op1=ALU.mult,
+            )
+
+        def turn_back(c, s, engine):
+            words = g_turned[c, s][:].rearrange("p w e -> p (w e)").bitcast(F32)
+            bank = banks.tile([P, 2, P], F32, name="bank")
+            for u in range(2):
+                nc.tensor.transpose(bank[:, u, :], words[:, u * P : (u + 1) * P], identity[:])
+            dst = g_bf(c, 2 * s, 2 * s + 2).rearrange("p n t -> p (n t)").bitcast(F32)
+            copy_on(engine, dst.rearrange("p (n u) -> p n u", u=2), bank[:].rearrange("p u n -> p n u"))
 
         m_bf, m_codes, m_scales, acc = {}, {}, {}, {}
 
@@ -261,8 +330,10 @@ def tile_attend_gnce_w_kernel(tc, xT, wT, y, wt, xm, offs, out):
                 m_bf[b, c] = keep.tile([P, P, PACK], BF16, name=f"m_bf{c}", align_bytes=64)
             else:
                 if (b, c) == (1, 0):
-                    m_bf["late"] = keep.tile([P, 6, P, PACK], BF16, name="m_late", tag="g_bf1", align_bytes=64)
-                m_bf[b, c] = m_bf["late"][:, 2 * (b - 1) + c]
+                    m_bf["late"] = keep.tile([P, 2, P, PACK], BF16, name="m_late", tag="g_bf11", align_bytes=64)
+                if (b, c) == (2, 0):
+                    m_bf["later"] = keep.tile([P, 4, P, PACK], BF16, name="m_later", tag="g_bf10", align_bytes=64)
+                m_bf[b, c] = m_bf["late"][:, c] if b == 1 else m_bf["later"][:, 2 * (b - 2) + c]
             copy_on(
                 engine,
                 m_bf[b, c][:].rearrange("p (n i) t -> p n t i", i=4),
@@ -280,7 +351,7 @@ def tile_attend_gnce_w_kernel(tc, xT, wT, y, wt, xm, offs, out):
 
         def product(b, c):
             if c == 0:
-                acc[b] = grad_banks.tile([P, N], F32, name=f"acc{b}")
+                acc[b] = banks.tile([P, N], F32, name="bank")
             nc.tensor.matmul_mx(
                 out=acc[b][:],
                 lhsT=m_codes[b, c][:].bitcast(E4M3),
@@ -292,7 +363,7 @@ def tile_attend_gnce_w_kernel(tc, xT, wT, y, wt, xm, offs, out):
             )
 
         def warm_up(h):
-            spare = score_banks.tile([P, N], F32, name="bank")
+            spare = banks.tile([P, N], F32, name="bank")
             nc.tensor.matmul_mx(
                 out=spare[:],
                 lhsT=g_codes[0][:, h * HALF : h * HALF + P].bitcast(E5M2),
@@ -314,7 +385,7 @@ def tile_attend_gnce_w_kernel(tc, xT, wT, y, wt, xm, offs, out):
             nc.sync.dma_start(out=out[b * P : (b + 1) * P, :], in_=window[b][:])
 
         def output_block(b):
-            dense = keep.tile([P, N], F32, name=f"dense{b}")
+            dense = keep.tile([P, N], F32, name=f"dense{b}", tag=f"dense{b}", align_bytes=64)
             nc.scalar.copy(out=dense[:], in_=acc[b][:])
             nc.vector.tensor_copy(out=window[b][:].indirect(offsets[:]), in_=dense[:])
             nc.sync.dma_start(out=out[b * P : (b + 1) * P, :], in_=window[b][:])
@@ -338,48 +409,62 @@ def tile_attend_gnce_w_kernel(tc, xT, wT, y, wt, xm, offs, out):
         interleave_x_part_pair(6, 8, 1, "vector")
         quantise_x(1, 0, 2)
         quantise_x(1, 2, 4)
-        weighted_targets(0, 0, 0, 8, "vector")
-        weighted_targets(0, 1, 0, 8, "vector")
-        gradient(0, 0, 0, 8)
-        gradient(0, 1, 0, 8)
-        weighted_targets(0, 2, 0, 8, "vector")
-        weighted_targets(0, 3, 0, 8, "vector")
-        gradient(0, 2, 0, 4)
-        gradient(0, 3, 0, 4)
-        gradient(0, 2, 4, 8)
-        gradient(0, 3, 4, 8)
+        reuse(0,2,0,2)
+        reuse(0,3,0,3)
+
         scores(1, 0)
         scores(1, 1)
         scores(1, 2)
         scores(1, 3)
-        weighted_targets(1, 0, 0, 8, "scalar")
-        weighted_targets(1, 1, 0, 8, "vector")
-        weighted_targets(1, 2, 0, 8, "vector")
-        weighted_targets(1, 3, 0, 8, "vector")
+        weighted_targets(0, 0, 0, 4, "vector")
+        weighted_targets(0, 1, 0, 4, "vector")
+        gradient(0, 0, 0, 4)
+        gradient(0, 1, 0, 4)
+        weighted_targets(0, 2, 0, 4, "vector")
+        weighted_targets(0, 3, 0, 4, "vector")
+        gradient(0, 2, 0, 4)
+        gradient(0, 3, 0, 4)
+        for s in (2,3):
+            turn(0,0,[s])
+            turn(0,1,[s])
+            turn(0,2,[s])
+            turn(0,3,[s])
+        weighted_targets(1, 0, 0, 4, "vector")
+        weighted_targets(1, 1, 0, 4, "vector")
         gradient(1, 0, 0, 4)
         gradient(1, 1, 0, 4)
+        close(0,2)
+        close(0,3)
+        turn(1, 0)
+        turn(1, 1)
+        for s in (2,3):
+            turn(1,2,[s])
+            turn(1,3,[s])
+        weighted_targets(1, 2, 0, 4, "vector")
+        weighted_targets(1, 3, 0, 4, "vector")
         gradient(1, 2, 0, 4)
         gradient(1, 3, 0, 4)
-        gradient(1, 0, 4, 8)
+        close(1,2)
+        close(1,3)
         interleave_gradient(0, 0, 4, "scalar")
-        quantise_gradient(0, 0, 4)
-        warm_up(0)
-        warm_up(0)
-        warm_up(0)
-        gradient(1, 1, 4, 8)
-        gradient(1, 2, 4, 8)
-        gradient(1, 3, 4, 8)
-        interleave_gradient(0, 4, 8, "scalar")
-        interleave_m(0, 0, "scalar")
+        turn_back(0, 2, "scalar")
+        turn_back(0, 3, "scalar")
         interleave_gradient(1, 0, 4, "scalar")
-        interleave_m(0, 1, "scalar")
+        turn_back(1, 2, "scalar")
+        turn_back(1, 3, "scalar")
+        warm_in(1,3)
+        warm_in(1,3)
+        interleave_m(0, 0, "scalar")
+        interleave_m(0, 1, "vector")
+        quantise_gradient(0, 0, 4)
         quantise_gradient(0, 4, 8)
         quantise_m(0, 0)
+        warm_in(0,2)
+        warm_in(0,3)
         product(0, 0)
-        interleave_gradient(1, 4, 8, "vector")
         quantise_gradient(1, 0, 4)
-        quantise_gradient(1, 4, 8)
         quantise_m(0, 1)
+        quantise_gradient(1, 4, 8)
         product(0, 1)
         output_block(0)
         interleave_m(1, 0, "vector")

@@ -22,7 +22,8 @@ K_PASS = P * PACK
 CHUNKS = R // K_PASS
 HALF = N // 2
 UNIT = 64
-DIRECT = (4, 4)
+DIRECT = (6, 6)
+M_TAGS = ("m_bf0", "g_rows10")
 
 
 def tile_attend_gnce_w_kernel(tc, xT, wT, y, wt, xm, offs, out):
@@ -249,7 +250,17 @@ def tile_attend_gnce_w_kernel(tc, xT, wT, y, wt, xm, offs, out):
 
         g_codes = [keep.tile([P, N], U32, name=f"g_codes{c}", align_bytes=64) for c in range(CHUNKS)]
         g_scales = [keep.tile([P, N], U8, name=f"g_scales{c}", align_bytes=64) for c in range(CHUNKS)]
-        g_rows = [keep.tile([P, PACK, N], BF16, name=f"g_rows{c}") for c in range(CHUNKS)]
+        rows_first = keep.tile([P, PACK, N], BF16, name="g_rows0")
+        rows_half = [
+            keep.tile([P, PACK, HALF], BF16, name=f"g_rows1{h}", tag=f"g_rows1{h}", align_bytes=64) for h in range(2)
+        ]
+
+        def g_rows(c, lo, hi):
+            if c == 0:
+                return rows_first[:, :, slots(lo, hi)]
+            h = lo // 4
+            return rows_half[h][:, :, slots(lo - 4 * h, hi - 4 * h)]
+
         g_half = {
             (c, h): keep.tile([P, HALF, PACK], BF16, name=f"g_bf{c}{h}", tag=f"g_bf{c}{h}", align_bytes=64)
             for c in range(CHUNKS)
@@ -262,7 +273,7 @@ def tile_attend_gnce_w_kernel(tc, xT, wT, y, wt, xm, offs, out):
 
         def gradient(c, t, lo, hi):
             nc.vector.scalar_tensor_tensor(
-                out=g_rows[c][:, t, slots(lo, hi)],
+                out=g_rows(c, lo, hi)[:, t, :],
                 in0=sig[c][:, t, slots(lo, hi)],
                 scalar=spread[:, c, t, 0:1],
                 in1=yw[c][:, t, slots(lo, hi)],
@@ -274,7 +285,7 @@ def tile_attend_gnce_w_kernel(tc, xT, wT, y, wt, xm, offs, out):
             copy_on(
                 engine,
                 g_bf(c, lo, hi).rearrange("p (n i) t -> p n t i", i=4),
-                g_rows[c][:, :, slots(lo, hi)].rearrange("p t (n i) -> p n t i", i=4),
+                g_rows(c, lo, hi).rearrange("p t (n i) -> p n t i", i=4),
             )
 
         def quantise_gradient(c, lo, hi):
@@ -292,8 +303,8 @@ def tile_attend_gnce_w_kernel(tc, xT, wT, y, wt, xm, offs, out):
         def reuse(c, s, c2, t2):
             sums[c, s] = score_bank[c2, t2]
 
-        def warm_in(c, s):
-            score_product(sums[c, s][:], 0, 0, slots(0, 8))
+        def warm_in(*key):
+            score_product(sums[key][:], 0, 0, slots(0, 8))
 
         def turn(c, t, blocks=None):
             for s in blocks or range(DIRECT[c] // 2, N // P):
@@ -317,17 +328,18 @@ def tile_attend_gnce_w_kernel(tc, xT, wT, y, wt, xm, offs, out):
 
         def turn_back(c, s, engine):
             words = g_turned[c, s][:].rearrange("p w e -> p (w e)").bitcast(F32)
-            bank = banks.tile([P, 2, P], F32, name="bank")
+            sums["wb", c, s] = banks.tile([P, N], F32, name="bank")
+            bank = sums["wb", c, s][:, 0 : 2 * P].rearrange("p (u n) -> p u n", u=2)
             for u in range(2):
                 nc.tensor.transpose(bank[:, u, :], words[:, u * P : (u + 1) * P], identity[:])
             dst = g_bf(c, 2 * s, 2 * s + 2).rearrange("p n t -> p (n t)").bitcast(F32)
-            copy_on(engine, dst.rearrange("p (n u) -> p n u", u=2), bank[:].rearrange("p u n -> p n u"))
+            copy_on(engine, dst.rearrange("p (n u) -> p n u", u=2), bank.rearrange("p u n -> p n u"))
 
         m_bf, m_codes, m_scales, acc = {}, {}, {}, {}
 
         def interleave_m(b, c, engine):
             if b == 0:
-                m_bf[b, c] = keep.tile([P, P, PACK], BF16, name=f"m_bf{c}", align_bytes=64)
+                m_bf[b, c] = keep.tile([P, P, PACK], BF16, name=f"m_bf{c}", tag=M_TAGS[c], align_bytes=64)
             else:
                 if (b, c) == (1, 0):
                     m_bf["late"] = keep.tile([P, 2, P, PACK], BF16, name="m_late", tag="g_bf11", align_bytes=64)
@@ -409,59 +421,52 @@ def tile_attend_gnce_w_kernel(tc, xT, wT, y, wt, xm, offs, out):
         interleave_x_part_pair(6, 8, 1, "vector")
         quantise_x(1, 0, 2)
         quantise_x(1, 2, 4)
-        reuse(0,2,0,2)
         reuse(0,3,0,3)
-
         scores(1, 0)
         scores(1, 1)
         scores(1, 2)
         scores(1, 3)
-        weighted_targets(0, 0, 0, 4, "vector")
-        weighted_targets(0, 1, 0, 4, "vector")
-        gradient(0, 0, 0, 4)
-        gradient(0, 1, 0, 4)
-        weighted_targets(0, 2, 0, 4, "vector")
-        weighted_targets(0, 3, 0, 4, "vector")
-        gradient(0, 2, 0, 4)
-        gradient(0, 3, 0, 4)
-        for s in (2,3):
-            turn(0,0,[s])
-            turn(0,1,[s])
-            turn(0,2,[s])
-            turn(0,3,[s])
-        weighted_targets(1, 0, 0, 4, "vector")
-        weighted_targets(1, 1, 0, 4, "vector")
+        weighted_targets(0, 0, 0, 6, "vector")
+        weighted_targets(0, 1, 0, 6, "vector")
+        gradient(0, 0, 0, 6)
+        gradient(0, 1, 0, 6)
+        weighted_targets(0, 2, 0, 6, "vector")
+        weighted_targets(0, 3, 0, 6, "vector")
+        gradient(0, 2, 0, 6)
+        gradient(0, 3, 0, 6)
+        for t in range(4):
+            turn(0,t)
+        close(0,3)
+        weighted_targets(1, 0, 0, 6, "vector")
+        weighted_targets(1, 1, 0, 6, "vector")
+        weighted_targets(1, 2, 0, 6, "vector")
+        weighted_targets(1, 3, 0, 6, "vector")
+        for t in range(4):
+            turn(1,t)
         gradient(1, 0, 0, 4)
         gradient(1, 1, 0, 4)
-        close(0,2)
-        close(0,3)
-        turn(1, 0)
-        turn(1, 1)
-        for s in (2,3):
-            turn(1,2,[s])
-            turn(1,3,[s])
-        weighted_targets(1, 2, 0, 4, "vector")
-        weighted_targets(1, 3, 0, 4, "vector")
         gradient(1, 2, 0, 4)
         gradient(1, 3, 0, 4)
-        close(1,2)
         close(1,3)
+        gradient(1, 0, 4, 6)
+        gradient(1, 1, 4, 6)
+        gradient(1, 2, 4, 6)
+        gradient(1, 3, 4, 6)
         interleave_gradient(0, 0, 4, "scalar")
-        turn_back(0, 2, "scalar")
+        interleave_gradient(0, 4, 6, "scalar")
         turn_back(0, 3, "scalar")
+        warm_in("wb",0,3)
+        warm_in("wb",0,3)
+        interleave_m(0, 0, "scalar")
         interleave_gradient(1, 0, 4, "scalar")
-        turn_back(1, 2, "scalar")
         turn_back(1, 3, "scalar")
         warm_in(1,3)
-        warm_in(1,3)
-        interleave_m(0, 0, "scalar")
-        interleave_m(0, 1, "vector")
+        interleave_m(0, 1, "scalar")
         quantise_gradient(0, 0, 4)
         quantise_gradient(0, 4, 8)
         quantise_m(0, 0)
-        warm_in(0,2)
-        warm_in(0,3)
         product(0, 0)
+        interleave_gradient(1, 4, 6, "vector")
         quantise_gradient(1, 0, 4)
         quantise_m(0, 1)
         quantise_gradient(1, 4, 8)

@@ -22,8 +22,9 @@ K_PASS = P * PACK
 CHUNKS = R // K_PASS
 HALF = N // 2
 UNIT = 64
-DIRECT = (6, 6)
-M_TAGS = ("m_bf0", "g_rows10")
+DIRECT = (6, 2)
+LATE_TAGS = {(2, 0): "g_turned13", (2, 1): "m_codes01", (3, 0): "dense1", (3, 1): "m_codes11"}
+M_TAGS = ("m_bf0", "m_bf1")
 
 
 def tile_attend_gnce_w_kernel(tc, xT, wT, y, wt, xm, offs, out):
@@ -65,7 +66,7 @@ def tile_attend_gnce_w_kernel(tc, xT, wT, y, wt, xm, offs, out):
             func=ACT.Copy,
             scale=-1.0,
         )
-        minus_wt = [keep.tile([P, 2 * P, 2], F32, name=f"minus_wt{c}") for c in range(CHUNKS)]
+        minus_wt = [keep.tile([P, 2 * P, 2], F32, name=f"minus_wt{c}", tag=f"minus_wt{c}", align_bytes=64) for c in range(CHUNKS)]
         for c in range(CHUNKS):
             spread_bank = banks.tile([P, 2, 2, P], F32, name="bank")
             for t in range(PACK):
@@ -175,6 +176,13 @@ def tile_attend_gnce_w_kernel(tc, xT, wT, y, wt, xm, offs, out):
                 x_raw[c].rearrange("p j (m t) -> p m j t", t=PACK)[:, :, :, 2 * u : 2 * u + 2],
             )
 
+        def interleave_x_cols(c, u, lo, hi, engine):
+            copy_on(
+                engine,
+                x_bf[c][:, 2 * u : 2 * u + 2, lo:hi, :].rearrange("p t m j -> p m j t"),
+                x_raw[c].rearrange("p j (m t) -> p m j t", t=PACK)[:, lo:hi, :, 2 * u : 2 * u + 2],
+            )
+
         def interleave_x_part(lo, hi, engine):
             part, first = x_raw["part", lo]
             copy_on(
@@ -232,7 +240,7 @@ def tile_attend_gnce_w_kernel(tc, xT, wT, y, wt, xm, offs, out):
             bank = banks.tile([P, HALF], F32, name="bank")
             cols = slots(4 * h, 4 * h + 4)
             score_product(bank[:], c, t, cols)
-            nc.scalar.activation(out=sig[c][:, t, cols], in_=bank[:], func=ACT.Sigmoid)
+            nc.scalar.activation(out=sig[c][:, t, cols], in_=bank[:], func=ACT.Sigmoid, scale=-1.0)
 
         yw = [keep.tile([P, PACK, N], F32, name=f"yw{c}") for c in range(CHUNKS)]
 
@@ -316,7 +324,7 @@ def tile_attend_gnce_w_kernel(tc, xT, wT, y, wt, xm, offs, out):
                 nc.tensor.matmul(dst, lhsT=y_of(c, t, cols), rhs=identity[:], start=False, stop=True, is_transpose=True)
 
         def close(c, s):
-            g_turned[c, s] = keep.tile([P, 2 * P, 2], BF16, name=f"g_turned{c}{s}")
+            g_turned[c, s] = keep.tile([P, 2 * P, 2], BF16, name=f"g_turned{c}{s}", tag=f"g_turned{c}{s}", align_bytes=64)
             nc.vector.scalar_tensor_tensor(
                 out=g_turned[c, s][:],
                 in0=sums[c, s][:].rearrange("p (e w) -> p w e", e=2),
@@ -341,11 +349,12 @@ def tile_attend_gnce_w_kernel(tc, xT, wT, y, wt, xm, offs, out):
             if b == 0:
                 m_bf[b, c] = keep.tile([P, P, PACK], BF16, name=f"m_bf{c}", tag=M_TAGS[c], align_bytes=64)
             else:
-                if (b, c) == (1, 0):
-                    m_bf["late"] = keep.tile([P, 2, P, PACK], BF16, name="m_late", tag="g_bf11", align_bytes=64)
-                if (b, c) == (2, 0):
-                    m_bf["later"] = keep.tile([P, 4, P, PACK], BF16, name="m_later", tag="g_bf10", align_bytes=64)
-                m_bf[b, c] = m_bf["late"][:, c] if b == 1 else m_bf["later"][:, 2 * (b - 2) + c]
+                if b == 1:
+                    if c == 0:
+                        m_bf["late"] = keep.tile([P, 2, P, PACK], BF16, name="m_late", tag="g_bf11", align_bytes=64)
+                    m_bf[b, c] = m_bf["late"][:, c]
+                else:
+                    m_bf[b, c] = keep.tile([P, P, PACK], BF16, name=f"m_bf{b}{c}", tag=LATE_TAGS[b, c], align_bytes=64)
             copy_on(
                 engine,
                 m_bf[b, c][:].rearrange("p (n i) t -> p n t i", i=4),
@@ -353,7 +362,7 @@ def tile_attend_gnce_w_kernel(tc, xT, wT, y, wt, xm, offs, out):
             )
 
         def quantise_m(b, c):
-            m_codes[b, c] = keep.tile([P, P], U32, name=f"m_codes{b}{c}", align_bytes=64)
+            m_codes[b, c] = keep.tile([P, P], U32, name=f"m_codes{b}{c}", tag=f"m_codes{b}{c}", align_bytes=64)
             m_scales[b, c] = keep.tile([P, P], U8, name=f"m_scales{b}{c}", align_bytes=64)
             nc.vector.quantize_mx(
                 out=m_codes[b, c][:].bitcast(E4M3),
@@ -407,12 +416,15 @@ def tile_attend_gnce_w_kernel(tc, xT, wT, y, wt, xm, offs, out):
         gather(2, 0, 8)
         gather(3, 0, 8)
         quantise_w(0, 8)
-        interleave_x_pair(0, 0, "vector")
-        interleave_x_pair(0, 1, "scalar")
+        interleave_x_cols(0, 0, 0, 80, "vector")
+        interleave_x_cols(0, 0, 80, 128, "scalar")
+        interleave_x_cols(0, 1, 0, 64, "vector")
+        interleave_x_cols(0, 1, 64, 128, "scalar")
         quantise_x(0, 0, 1)
         quantise_x(0, 1, 2)
         quantise_x(0, 2, 4)
-        scores(0, 0)
+        scores_narrow(0, 0, 0)
+        scores_narrow(0, 0, 1)
         scores(0, 1)
         scores(0, 2)
         scores(0, 3)
@@ -437,39 +449,42 @@ def tile_attend_gnce_w_kernel(tc, xT, wT, y, wt, xm, offs, out):
         for t in range(4):
             turn(0,t)
         close(0,3)
-        weighted_targets(1, 0, 0, 6, "vector")
-        weighted_targets(1, 1, 0, 6, "vector")
-        weighted_targets(1, 2, 0, 6, "vector")
-        weighted_targets(1, 3, 0, 6, "vector")
-        for t in range(4):
-            turn(1,t)
-        gradient(1, 0, 0, 4)
-        gradient(1, 1, 0, 4)
-        gradient(1, 2, 0, 4)
-        gradient(1, 3, 0, 4)
+        turn(1,0)
+        turn(1,1)
+        for s in (1,2,3):
+            turn(1,2,[s])
+            turn(1,3,[s])
+        weighted_targets(1, 0, 0, 2, "vector")
+        weighted_targets(1, 1, 0, 2, "vector")
+        weighted_targets(1, 2, 0, 2, "vector")
+        weighted_targets(1, 3, 0, 2, "vector")
+        gradient(1, 0, 0, 2)
+        gradient(1, 1, 0, 2)
+        gradient(1, 2, 0, 2)
+        gradient(1, 3, 0, 2)
+        close(1,1)
+        close(1,2)
         close(1,3)
-        gradient(1, 0, 4, 6)
-        gradient(1, 1, 4, 6)
-        gradient(1, 2, 4, 6)
-        gradient(1, 3, 4, 6)
         interleave_gradient(0, 0, 4, "scalar")
         interleave_gradient(0, 4, 6, "scalar")
         turn_back(0, 3, "scalar")
-        warm_in("wb",0,3)
-        warm_in("wb",0,3)
+        interleave_gradient(1, 0, 2, "scalar")
         interleave_m(0, 0, "scalar")
-        interleave_gradient(1, 0, 4, "scalar")
+        turn_back(1, 1, "scalar")
+        warm_in(1,1)
+        interleave_m(0, 1, "scalar")
+        turn_back(1, 2, "scalar")
+        warm_in(1,2)
         turn_back(1, 3, "scalar")
         warm_in(1,3)
-        interleave_m(0, 1, "scalar")
         quantise_gradient(0, 0, 4)
         quantise_gradient(0, 4, 8)
         quantise_m(0, 0)
         product(0, 0)
-        interleave_gradient(1, 4, 6, "vector")
         quantise_gradient(1, 0, 4)
         quantise_m(0, 1)
-        quantise_gradient(1, 4, 8)
+        quantise_gradient(1, 4, 6)
+        quantise_gradient(1, 6, 8)
         product(0, 1)
         output_block(0)
         interleave_m(1, 0, "vector")
@@ -479,15 +494,15 @@ def tile_attend_gnce_w_kernel(tc, xT, wT, y, wt, xm, offs, out):
         product(1, 0)
         product(1, 1)
         output_block(1)
-        interleave_m(2, 0, "vector")
-        interleave_m(2, 1, "vector")
+        interleave_m(2, 0, "scalar")
+        interleave_m(2, 1, "scalar")
         quantise_m(2, 0)
         quantise_m(2, 1)
         product(2, 0)
         product(2, 1)
         output_block(2)
         interleave_m(3, 0, "vector")
-        interleave_m(3, 1, "vector")
+        interleave_m(3, 1, "scalar")
         quantise_m(3, 0)
         quantise_m(3, 1)
         product(3, 0)

@@ -20,11 +20,14 @@ P = 128
 PACK = 4
 K_PASS = P * PACK
 CHUNKS = R // K_PASS
+BLOCKS = N // P
 HALF = N // 2
-UNIT = 64
-DIRECT = (6, 2)
-LATE_TAGS = {(2, 0): "g_turned13", (2, 1): "m_codes01", (3, 0): "dense1", (3, 1): "m_codes11"}
-M_TAGS = ("m_bf0", "m_bf1")
+MX_ALIGN = 64
+DMA_ALIGN = 256
+
+DIRECT = (3, 2)
+X_SHARES = (80, 64)
+EARLY_ROWS = 384
 
 
 def tile_attend_gnce_w_kernel(tc, xT, wT, y, wt, xm, offs, out):
@@ -34,15 +37,24 @@ def tile_attend_gnce_w_kernel(tc, xT, wT, y, wt, xm, offs, out):
         keep = ctx.enter_context(tc.tile_pool(name="keep", bufs=1))
         banks = ctx.enter_context(tc.psum_pool(name="banks", bufs=8))
 
+        def new_bank():
+            return banks.tile([P, N], F32, name="bank")
+
         def copy_on(engine, dst, src):
-            if engine == "vector":
+            if engine is nc.vector:
                 nc.vector.tensor_copy(out=dst, in_=src)
             else:
                 nc.scalar.copy(out=dst, in_=src)
 
+        def side_by_side(engine, dst, src):
+            copy_on(engine, dst.rearrange("p (n i) t -> p n t i", i=4), src.rearrange("p t (n i) -> p n t i", i=4))
+
+        def quantise(codes, scales, laid, fmt):
+            nc.vector.quantize_mx(out=codes.bitcast(fmt), scales=scales, in_=laid)
+
         weight = keep.tile([P, CHUNKS, PACK], F32, name="weight")
         apart = P // CHUNKS
-        wt_rows = keep.tile([P, K_PASS], F32, name="wt_rows", align_bytes=256)
+        wt_rows = keep.tile([P, K_PASS], F32, name="wt_rows", align_bytes=DMA_ALIGN)
         nc.scalar.dma_start(out=wt_rows[0:P:apart, :], in_=wt[0].rearrange("(c k) o -> c (k o)", c=CHUNKS))
         warm_in = keep.tile([P, 1], F32, name="warm_in")
         warm_out = keep.tile([P, 1], F32, name="warm_out")
@@ -55,164 +67,83 @@ def tile_attend_gnce_w_kernel(tc, xT, wT, y, wt, xm, offs, out):
         for c in range(CHUNKS):
             row = slice(c * apart, c * apart + 1)
             nc.scalar.copy(out=wt_dealt[row, :, :], in_=wt_rows[row, :].rearrange("c (p t) -> c t p", t=PACK))
-        wt_bank = banks.tile([P, PACK, P], F32, name="bank")
+        wt_bank = new_bank()[:].rearrange("p (t k) -> p t k", t=PACK)
         for t in range(PACK):
             nc.tensor.transpose(wt_bank[:, t, :], wt_dealt[:, t, :], identity[:])
-        nc.scalar.copy(out=weight[:], in_=wt_bank[:].rearrange("p t (c k) -> p c t k", c=CHUNKS)[:, :, :, 0])
-        spread = keep.tile([P, CHUNKS, PACK, P], F32, name="spread")
+        nc.scalar.copy(out=weight[:], in_=wt_bank.rearrange("p t (c k) -> p c t k", c=CHUNKS)[:, :, :, 0])
+
+        def place_of(bank, t):
+            return bank[:].rearrange("p (e u m) -> p e u m", e=2, u=2)[:, t % 2, t // 2, :]
+
+        def by_words(bank):
+            return bank[:].rearrange("p (e w) -> p w e", e=2)
+
+        minus_col = keep.tile([P, CHUNKS, PACK, P], F32, name="minus_col")
         nc.scalar.activation(
-            out=spread[:].rearrange("p c t k -> p (c t) k"),
+            out=minus_col[:].rearrange("p c t k -> p (c t) k"),
             in_=weight[:].rearrange("p c t -> p (c t)").unsqueeze(2).to_broadcast([P, CHUNKS * PACK, P]),
             func=ACT.Copy,
             scale=-1.0,
         )
-        minus_wt = [keep.tile([P, 2 * P, 2], F32, name=f"minus_wt{c}", tag=f"minus_wt{c}", align_bytes=64) for c in range(CHUNKS)]
+        minus_row = [keep.tile([P, 2 * P, 2], F32, name=f"minus_row{c}", align_bytes=MX_ALIGN) for c in range(CHUNKS)]
         for c in range(CHUNKS):
-            spread_bank = banks.tile([P, 2, 2, P], F32, name="bank")
+            bank = new_bank()
             for t in range(PACK):
-                nc.tensor.transpose(spread_bank[:, t % 2, t // 2, :], spread[:, c, t, :], identity[:])
-            nc.scalar.copy(out=minus_wt[c][:], in_=spread_bank[:].rearrange("p e u m -> p (u m) e"))
+                nc.tensor.transpose(place_of(bank, t), minus_col[:, c, t, :], identity[:])
+            nc.scalar.copy(out=minus_row[c][:], in_=by_words(bank))
+
+        def load(name, src):
+            tile = keep.tile(list(src.shape), F32, name=name, align_bytes=DMA_ALIGN)
+            nc.sync.dma_start(out=tile[:], in_=src)
+            return tile
+
         offsets = lists.tile([P, N // 16], U16, name="offsets")
         w_rows = wT.rearrange("(p t) c -> p t c", t=PACK)
-        table = [keep.tile([P, T], F32, name=f"table{t}", align_bytes=256) for t in range(PACK)]
         x_rows = xT[0].rearrange("(p j) r -> p j r", j=PACK)
         y_rows = y[0].rearrange("(c p t) i -> c p t i", c=CHUNKS, t=PACK)
         m_rows = xm[0].rearrange("(c p t) d -> c p t d", c=CHUNKS, t=PACK)
-        x_raw, y_raw, m_raw = {}, {}, {}
 
-        def load_x(c, h):
-            x_half = keep.tile([P, PACK, K_PASS // 2], F32, name=f"x_half{c}{h}")
-            r0 = c * K_PASS + h * (K_PASS // 2)
-            nc.sync.dma_start(out=x_half[:], in_=x_rows[:, :, r0 : r0 + K_PASS // 2])
-            x_raw[c, h] = x_half[:]
-
-        def load_x_whole(c):
-            x_whole = keep.tile([P, PACK, K_PASS], F32, name=f"x_whole{c}", align_bytes=256)
-            nc.sync.dma_start(out=x_whole[:], in_=x_rows[:, :, c * K_PASS : (c + 1) * K_PASS])
-            x_raw[c] = x_whole[:]
-            for h in range(2):
-                x_raw[c, h] = x_whole[:, :, h * (K_PASS // 2) : (h + 1) * (K_PASS // 2)]
-
-        def load_x_part(lo, hi):
-            part = keep.tile([P, PACK, (hi - lo) * UNIT], F32, name=f"x_part{lo}", align_bytes=256)
-            nc.sync.dma_start(out=part[:], in_=x_rows[:, :, K_PASS + lo * UNIT : K_PASS + hi * UNIT])
-            for unit in range(lo, hi):
-                x_raw["part", unit] = (part, lo)
-
-        def load_y_row(c, t):
-            row = keep.tile([P, N], F32, name=f"y_row{c}{t}", align_bytes=256)
-            nc.sync.dma_start(out=row[:], in_=y_rows[c, :, t, :])
-            y_raw["row", c, t] = row
-
-        def load_y(c, u):
-            y_raw[c, u] = keep.tile([P, 2, N], F32, name=f"y_raw{c}{u}", align_bytes=256)
-            nc.sync.dma_start(out=y_raw[c, u][:], in_=y_rows[c, :, 2 * u : 2 * u + 2, :])
-
-        def load_m(c, lo, hi):
-            m_part = keep.tile([P, PACK, (hi - lo) * P], F32, name=f"m_part{c}{lo}", align_bytes=256)
-            nc.sync.dma_start(out=m_part[:], in_=m_rows[c, :, :, lo * P : hi * P])
-            for b in range(lo, hi):
-                m_raw[b, c] = m_part[:, :, (b - lo) * P : (b - lo + 1) * P]
-
-        nc.sync.dma_start(out=table[0][:], in_=w_rows[:, 0, :])
+        table = [load("table0", w_rows[:, 0, :])]
         nc.sync.dma_start(offsets[:], offs)
-        nc.sync.dma_start(out=table[1][:], in_=w_rows[:, 1, :])
-        nc.sync.dma_start(out=table[2][:], in_=w_rows[:, 2, :])
-        nc.sync.dma_start(out=table[3][:], in_=w_rows[:, 3, :])
-        load_x_whole(0)
-        load_x_part(0, 6)
-        load_x_part(6, 8)
-        load_y_row(0, 0)
-        load_y_row(0, 1)
-        load_y(0, 1)
-        load_y(1, 0)
-        load_y(1, 1)
-        load_m(0, 0, 1)
-        load_m(1, 0, 1)
-        load_m(0, 1, 2)
-        load_m(1, 1, 2)
-        load_m(0, 2, 4)
-        load_m(1, 2, 4)
+        table.extend(load(f"table{t}", w_rows[:, t, :]) for t in range(1, PACK))
+        x_first = load("x_first", x_rows[:, :, 0:K_PASS])
+        x_early = load("x_early", x_rows[:, :, K_PASS : K_PASS + EARLY_ROWS])
+        x_late = load("x_late", x_rows[:, :, K_PASS + EARLY_ROWS : R])
+        y_raw = {(0, t): load(f"y0{t}", y_rows[0, :, t, :])[:] for t in range(2)}
+        for c, u in ((0, 1), (1, 0), (1, 1)):
+            pair = load(f"y_pair{c}{u}", y_rows[c, :, 2 * u : 2 * u + 2, :])
+            y_raw.update({(c, 2 * u + e): pair[:, e, :] for e in range(2)})
+        m_raw = {}
+        for lo, hi in ((0, 1), (1, 2), (2, 4)):
+            for c in range(CHUNKS):
+                part = load(f"m_part{c}{lo}", m_rows[c, :, :, lo * P : hi * P])
+                m_raw.update({(b, c): part[:, :, (b - lo) * P : (b - lo + 1) * P] for b in range(lo, hi)})
 
-        window = [keep.tile([P, T], F32, name=f"window{b}", align_bytes=256) for b in range(D // P)]
+        window = [keep.tile([P, T], F32, name=f"window{b}", align_bytes=DMA_ALIGN) for b in range(D // P)]
         for b in range(D // P):
             (nc.vector if b < 2 else nc.gpsimd).memset(window[b][:], 0.0)
 
-        w_bf = keep.tile([P, N, PACK], BF16, name="w_bf", align_bytes=64)
-        w_codes = keep.tile([P, N], U32, name="w_codes", align_bytes=64)
-        w_scales = keep.tile([P, N], U8, name="w_scales", align_bytes=64)
+        w_bf = keep.tile([P, N, PACK], BF16, name="w_bf", align_bytes=MX_ALIGN)
+        w_codes = keep.tile([P, N], U32, name="w_codes", align_bytes=MX_ALIGN)
+        w_scales = keep.tile([P, N], U8, name="w_scales", align_bytes=MX_ALIGN)
+        for t in range(PACK):
+            nc.vector.tensor_copy(out=w_bf[:, :, t], in_=table[t][:].indirect(offsets[:]))
+        quantise(w_codes[:], w_scales[:], w_bf[:].rearrange("p n t -> p (n t)"), E4M3)
 
-        def slots(lo, hi):
-            return slice(lo * UNIT, hi * UNIT)
+        x_bf = [keep.tile([P, PACK, P, PACK], BF16, name=f"x_bf{c}", align_bytes=MX_ALIGN) for c in range(CHUNKS)]
+        x_codes = [keep.tile([P, K_PASS], U32, name=f"x_codes{c}", align_bytes=MX_ALIGN) for c in range(CHUNKS)]
+        x_scales = [keep.tile([P, K_PASS], U8, name=f"x_scales{c}", align_bytes=MX_ALIGN) for c in range(CHUNKS)]
 
-        def gather(t, lo, hi):
-            nc.vector.tensor_copy(
-                out=w_bf[:, slots(lo, hi), t], in_=table[t][:].indirect(offsets[:, lo * UNIT // 16 : hi * UNIT // 16])
-            )
-
-        def quantise_w(lo, hi):
-            nc.vector.quantize_mx(
-                out=w_codes[:, slots(lo, hi)].bitcast(E4M3),
-                scales=w_scales[:, slots(lo, hi)],
-                in_=w_bf[:, slots(lo, hi), :].rearrange("p n t -> p (n t)"),
-            )
-
-        x_bf = [keep.tile([P, PACK, P, PACK], BF16, name=f"x_bf{c}", align_bytes=64) for c in range(CHUNKS)]
-        x_codes = [keep.tile([P, K_PASS], U32, name=f"x_codes{c}", align_bytes=64) for c in range(CHUNKS)]
-        x_scales = [keep.tile([P, K_PASS], U8, name=f"x_scales{c}", align_bytes=64) for c in range(CHUNKS)]
-
-        def interleave_x(c, lo, hi, engine):
-            h = lo // 4
-            copy_on(
-                engine,
-                x_bf[c][:, :, lo * 16 : hi * 16, :].rearrange("p t m j -> p m j t"),
-                x_raw[c, h][:, :, (lo - 4 * h) * UNIT : (hi - 4 * h) * UNIT].rearrange("p j (m t) -> p m j t", t=PACK),
-            )
-
-        def interleave_x_pair(c, u, engine):
-            copy_on(
-                engine,
-                x_bf[c][:, 2 * u : 2 * u + 2, :, :].rearrange("p t m j -> p m j t"),
-                x_raw[c].rearrange("p j (m t) -> p m j t", t=PACK)[:, :, :, 2 * u : 2 * u + 2],
-            )
-
-        def interleave_x_cols(c, u, lo, hi, engine):
-            copy_on(
-                engine,
-                x_bf[c][:, 2 * u : 2 * u + 2, lo:hi, :].rearrange("p t m j -> p m j t"),
-                x_raw[c].rearrange("p j (m t) -> p m j t", t=PACK)[:, lo:hi, :, 2 * u : 2 * u + 2],
-            )
-
-        def interleave_x_part(lo, hi, engine):
-            part, first = x_raw["part", lo]
-            copy_on(
-                engine,
-                x_bf[1][:, :, lo * 16 : hi * 16, :].rearrange("p t m j -> p m j t"),
-                part[:, :, (lo - first) * UNIT : (hi - first) * UNIT].rearrange("p j (m t) -> p m j t", t=PACK),
-            )
-
-        def interleave_x_part_pair(lo, hi, u, engine):
-            part, first = x_raw["part", lo]
-            rows = part[:, :, (lo - first) * UNIT : (hi - first) * UNIT].rearrange("p j (m t) -> p m j t", t=PACK)
-            copy_on(
-                engine,
-                x_bf[1][:, 2 * u : 2 * u + 2, lo * 16 : hi * 16, :].rearrange("p t m j -> p m j t"),
-                rows[:, :, :, 2 * u : 2 * u + 2],
-            )
+        def lay_x(engine, c, raw, first, lo, hi, places):
+            src = raw[:].rearrange("p j (m t) -> p m j t", t=PACK)[:, lo - first : hi - first, :, places]
+            copy_on(engine, x_bf[c][:, places, lo:hi, :].rearrange("p t m j -> p m j t"), src)
 
         def quantise_x(c, lo, hi):
             cols = slice(lo * P, hi * P)
-            nc.vector.quantize_mx(
-                out=x_codes[c][:, cols].bitcast(E4M3),
-                scales=x_scales[c][:, cols],
-                in_=x_bf[c][:, lo:hi, :, :].rearrange("p t m j -> p (t m j)"),
-            )
+            laid = x_bf[c][:, lo:hi, :, :].rearrange("p t m j -> p (t m j)")
+            quantise(x_codes[c][:, cols], x_scales[c][:, cols], laid, E4M3)
 
-        sig = [keep.tile([P, PACK, N], F32, name=f"sig{c}") for c in range(CHUNKS)]
-
-        score_bank = {}
-
-        def score_product(dst, c, t, cols):
+        def score_pass(dst, c, t, cols):
             nc.tensor.matmul_mx(
                 out=dst,
                 lhsT=x_codes[c][:, t * P : (t + 1) * P].bitcast(E4M3),
@@ -223,156 +154,108 @@ def tile_attend_gnce_w_kernel(tc, xT, wT, y, wt, xm, offs, out):
                 stop=True,
             )
 
-        def scores(c, t):
-            bank = banks.tile([P, N], F32, name="bank")
-            score_bank[c, t] = bank
-            score_product(bank[:], c, t, slots(0, 8))
-            nc.scalar.activation(out=sig[c][:, t, :], in_=bank[:], func=ACT.Sigmoid, scale=-1.0)
+        sig = [keep.tile([P, PACK, N], F32, name=f"sig{c}") for c in range(CHUNKS)]
+        score_bank = {}
 
-        def scores_half(c, u, h):
-            bank = banks.tile([P, 2, HALF], F32, name="bank")
-            cols = slots(4 * h, 4 * h + 4)
-            for i in range(2):
-                score_product(bank[:, i, :], c, 2 * u + i, cols)
-            nc.scalar.activation(out=sig[c][:, 2 * u : 2 * u + 2, cols], in_=bank[:], func=ACT.Sigmoid)
+        def scores(c, t, cols=slice(0, N)):
+            score_bank[c, t] = new_bank()
+            score_pass(score_bank[c, t][:, cols], c, t, cols)
+            nc.scalar.activation(out=sig[c][:, t, cols], in_=score_bank[c, t][:, cols], func=ACT.Sigmoid, scale=-1.0)
 
-        def scores_narrow(c, t, h):
-            bank = banks.tile([P, HALF], F32, name="bank")
-            cols = slots(4 * h, 4 * h + 4)
-            score_product(bank[:], c, t, cols)
-            nc.scalar.activation(out=sig[c][:, t, cols], in_=bank[:], func=ACT.Sigmoid, scale=-1.0)
+        def warm_up(bank):
+            score_pass(bank[:], 0, 0, slice(0, N))
 
-        yw = [keep.tile([P, PACK, N], F32, name=f"yw{c}") for c in range(CHUNKS)]
-
-        def weighted_targets(c, t, lo, hi, engine):
-            src = y_raw["row", c, t][:, slots(lo, hi)] if ("row", c, t) in y_raw else y_raw[c, t // 2][:, t % 2, slots(lo, hi)]
-            dst = yw[c][:, t, slots(lo, hi)]
-            if engine == "vector":
-                nc.vector.tensor_scalar(
-                    out=dst, in0=src, scalar1=spread[:, c, t, 0:1], scalar2=weight[:, c, t : t + 1], op0=ALU.mult, op1=ALU.add
-                )
-            else:
-                nc.scalar.activation(
-                    out=dst, in_=src, func=ACT.Identity, scale=spread[:, c, t, 0:1], bias=weight[:, c, t : t + 1]
-                )
-
-        g_codes = [keep.tile([P, N], U32, name=f"g_codes{c}", align_bytes=64) for c in range(CHUNKS)]
-        g_scales = [keep.tile([P, N], U8, name=f"g_scales{c}", align_bytes=64) for c in range(CHUNKS)]
-        rows_first = keep.tile([P, PACK, N], BF16, name="g_rows0")
-        rows_half = [
-            keep.tile([P, PACK, HALF], BF16, name=f"g_rows1{h}", tag=f"g_rows1{h}", align_bytes=64) for h in range(2)
-        ]
-
-        def g_rows(c, lo, hi):
-            if c == 0:
-                return rows_first[:, :, slots(lo, hi)]
-            h = lo // 4
-            return rows_half[h][:, :, slots(lo - 4 * h, hi - 4 * h)]
-
+        g_codes = [keep.tile([P, N], U32, name=f"g_codes{c}", align_bytes=MX_ALIGN) for c in range(CHUNKS)]
+        g_scales = [keep.tile([P, N], U8, name=f"g_scales{c}", align_bytes=MX_ALIGN) for c in range(CHUNKS)]
         g_half = {
-            (c, h): keep.tile([P, HALF, PACK], BF16, name=f"g_bf{c}{h}", tag=f"g_bf{c}{h}", align_bytes=64)
+            (c, h): keep.tile([P, HALF, PACK], BF16, name=f"g_half{c}{h}", tag=f"g_half{c}{h}", align_bytes=MX_ALIGN)
             for c in range(CHUNKS)
             for h in range(2)
         }
 
-        def g_bf(c, lo, hi):
-            h = lo // 4
-            return g_half[c, h][:, slots(lo - 4 * h, hi - 4 * h), :]
+        def g_laid(c, lo, hi):
+            return g_half[c, lo // 2][:, (lo % 2) * P : (lo % 2 + hi - lo) * P, :]
 
-        def gradient(c, t, lo, hi):
-            nc.vector.scalar_tensor_tensor(
-                out=g_rows(c, lo, hi)[:, t, :],
-                in0=sig[c][:, t, slots(lo, hi)],
-                scalar=spread[:, c, t, 0:1],
-                in1=yw[c][:, t, slots(lo, hi)],
+        def quantise_g(c, lo, hi):
+            cols = slice(lo * P, hi * P)
+            quantise(g_codes[c][:, cols], g_scales[c][:, cols], g_laid(c, lo, hi).rearrange("p n t -> p (n t)"), E5M2)
+
+        rest = [keep.tile([P, PACK, DIRECT[c] * P], F32, name=f"rest{c}") for c in range(CHUNKS)]
+        g_rows = [keep.tile([P, PACK, DIRECT[c] * P], BF16, name=f"g_rows{c}") for c in range(CHUNKS)]
+
+        def weigh_targets(c, t):
+            nc.vector.tensor_scalar(
+                out=rest[c][:, t, :],
+                in0=y_raw[c, t][:, 0 : DIRECT[c] * P],
+                scalar1=minus_col[:, c, t, 0:1],
+                scalar2=weight[:, c, t : t + 1],
                 op0=ALU.mult,
                 op1=ALU.add,
             )
 
-        def interleave_gradient(c, lo, hi, engine):
-            copy_on(
-                engine,
-                g_bf(c, lo, hi).rearrange("p (n i) t -> p n t i", i=4),
-                g_rows(c, lo, hi).rearrange("p t (n i) -> p n t i", i=4),
+        def gradient(c, t):
+            nc.vector.scalar_tensor_tensor(
+                out=g_rows[c][:, t, :],
+                in0=sig[c][:, t, 0 : DIRECT[c] * P],
+                scalar=minus_col[:, c, t, 0:1],
+                in1=rest[c][:, t, :],
+                op0=ALU.mult,
+                op1=ALU.add,
             )
 
-        def quantise_gradient(c, lo, hi):
-            nc.vector.quantize_mx(
-                out=g_codes[c][:, slots(lo, hi)].bitcast(E5M2),
-                scales=g_scales[c][:, slots(lo, hi)],
-                in_=g_bf(c, lo, hi).rearrange("p n t -> p (n t)"),
+        def lay_g(c, lo, hi, engine=nc.scalar, part=slice(0, None)):
+            side_by_side(engine, g_laid(c, lo, hi)[:, part, :], g_rows[c][:, :, lo * P : hi * P][:, :, part])
+
+        sums, g_turned = {}, {}
+
+        def turn(c, t, s):
+            if (c, s) not in sums:
+                sums[c, s] = new_bank()
+            cols = slice(s * P, (s + 1) * P)
+            dst = place_of(sums[c, s], t)
+            nc.tensor.matmul(dst, lhsT=sig[c][:, t, cols], rhs=identity[:], start=True, stop=False, is_transpose=True)
+            nc.tensor.matmul(dst, lhsT=y_raw[c, t][:, cols], rhs=identity[:], start=False, stop=True, is_transpose=True)
+
+        def gradient_turned(c, s):
+            g_turned[c, s] = keep.tile(
+                [P, 2 * P, 2], BF16, name=f"g_turned{c}{s}", tag=f"g_turned{c}{s}", align_bytes=MX_ALIGN
             )
-
-        sums, g_turned, word_bank = {}, {}, {}
-
-        def y_of(c, t, cols):
-            return y_raw["row", c, t][:, cols] if ("row", c, t) in y_raw else y_raw[c, t // 2][:, t % 2, cols]
-
-        def reuse(c, s, c2, t2):
-            sums[c, s] = score_bank[c2, t2]
-
-        def warm_in(*key):
-            score_product(sums[key][:], 0, 0, slots(0, 8))
-
-        def turn(c, t, blocks=None):
-            for s in blocks or range(DIRECT[c] // 2, N // P):
-                if (c, s) not in sums:
-                    sums[c, s] = banks.tile([P, N], F32, name="bank")
-                cols = slice(s * P, (s + 1) * P)
-                dst = sums[c, s][:].rearrange("p (e u m) -> p e u m", e=2, u=2)[:, t % 2, t // 2, :]
-                nc.tensor.matmul(dst, lhsT=sig[c][:, t, cols], rhs=identity[:], start=True, stop=False, is_transpose=True)
-                nc.tensor.matmul(dst, lhsT=y_of(c, t, cols), rhs=identity[:], start=False, stop=True, is_transpose=True)
-
-        def close(c, s):
-            g_turned[c, s] = keep.tile([P, 2 * P, 2], BF16, name=f"g_turned{c}{s}", tag=f"g_turned{c}{s}", align_bytes=64)
             nc.vector.scalar_tensor_tensor(
                 out=g_turned[c, s][:],
-                in0=sums[c, s][:].rearrange("p (e w) -> p w e", e=2),
+                in0=by_words(sums[c, s]),
                 scalar=1.0,
-                in1=minus_wt[c][:],
+                in1=minus_row[c][:],
                 op0=ALU.subtract,
                 op1=ALU.mult,
             )
 
-        def turn_back(c, s, engine):
+        def turn_back(c, s):
             words = g_turned[c, s][:].rearrange("p w e -> p (w e)").bitcast(F32)
-            sums["wb", c, s] = banks.tile([P, N], F32, name="bank")
-            bank = sums["wb", c, s][:, 0 : 2 * P].rearrange("p (u n) -> p u n", u=2)
+            whole = new_bank()
+            bank = whole[:, 0 : 2 * P].rearrange("p (u n) -> p u n", u=2)
             for u in range(2):
                 nc.tensor.transpose(bank[:, u, :], words[:, u * P : (u + 1) * P], identity[:])
-            dst = g_bf(c, 2 * s, 2 * s + 2).rearrange("p n t -> p (n t)").bitcast(F32)
-            copy_on(engine, dst.rearrange("p (n u) -> p n u", u=2), bank.rearrange("p u n -> p n u"))
+            dst = g_laid(c, s, s + 1).rearrange("p n t -> p (n t)").bitcast(F32)
+            nc.scalar.copy(out=dst.rearrange("p (n u) -> p n u", u=2), in_=bank.rearrange("p u n -> p n u"))
+            return whole
 
         m_bf, m_codes, m_scales, acc = {}, {}, {}, {}
 
-        def interleave_m(b, c, engine):
-            if b == 0:
-                m_bf[b, c] = keep.tile([P, P, PACK], BF16, name=f"m_bf{c}", tag=M_TAGS[c], align_bytes=64)
-            else:
-                if b == 1:
-                    if c == 0:
-                        m_bf["late"] = keep.tile([P, 2, P, PACK], BF16, name="m_late", tag="g_bf11", align_bytes=64)
-                    m_bf[b, c] = m_bf["late"][:, c]
-                else:
-                    m_bf[b, c] = keep.tile([P, P, PACK], BF16, name=f"m_bf{b}{c}", tag=LATE_TAGS[b, c], align_bytes=64)
-            copy_on(
-                engine,
-                m_bf[b, c][:].rearrange("p (n i) t -> p n t i", i=4),
-                m_raw[b, c].rearrange("p t (n i) -> p n t i", i=4),
-            )
+        def lay_m(engine, b, c, dst):
+            m_bf[b, c] = dst
+            side_by_side(engine, dst, m_raw[b, c])
+
+        def m_tile(name, tag, pieces=1):
+            return keep.tile([P, pieces, P, PACK], BF16, name=name, tag=tag, align_bytes=MX_ALIGN)
 
         def quantise_m(b, c):
-            m_codes[b, c] = keep.tile([P, P], U32, name=f"m_codes{b}{c}", tag=f"m_codes{b}{c}", align_bytes=64)
-            m_scales[b, c] = keep.tile([P, P], U8, name=f"m_scales{b}{c}", align_bytes=64)
-            nc.vector.quantize_mx(
-                out=m_codes[b, c][:].bitcast(E4M3),
-                scales=m_scales[b, c][:],
-                in_=m_bf[b, c][:].rearrange("p n t -> p (n t)"),
-            )
+            m_codes[b, c] = keep.tile([P, P], U32, name=f"m_codes{b}{c}", tag=f"m_codes{b}{c}", align_bytes=MX_ALIGN)
+            m_scales[b, c] = keep.tile([P, P], U8, name=f"m_scales{b}{c}", align_bytes=MX_ALIGN)
+            quantise(m_codes[b, c][:], m_scales[b, c][:], m_bf[b, c].rearrange("p n t -> p (n t)"), E4M3)
 
         def product(b, c):
-            if c == 0:
-                acc[b] = banks.tile([P, N], F32, name="bank")
+            if b not in acc:
+                acc[b] = new_bank()
             nc.tensor.matmul_mx(
                 out=acc[b][:],
                 lhsT=m_codes[b, c][:].bitcast(E4M3),
@@ -383,128 +266,98 @@ def tile_attend_gnce_w_kernel(tc, xT, wT, y, wt, xm, offs, out):
                 stop=(c == CHUNKS - 1),
             )
 
-        def warm_up(h):
-            spare = banks.tile([P, N], F32, name="bank")
-            nc.tensor.matmul_mx(
-                out=spare[:],
-                lhsT=g_codes[0][:, h * HALF : h * HALF + P].bitcast(E5M2),
-                lhsT_scale=g_scales[0][:, h * HALF : h * HALF + P],
-                rhs=w_codes[:].bitcast(E4M3),
-                rhs_scale=w_scales[:],
-                start=True,
-                stop=True,
-            )
-
-        def output_block_halves(b):
-            dense = keep.tile([P, N], F32, name=f"dense{b}")
-            for h in range(2):
-                nc.scalar.copy(out=dense[:, slots(4 * h, 4 * h + 4)], in_=acc[b][:, slots(4 * h, 4 * h + 4)])
-                nc.vector.tensor_copy(
-                    out=window[b][:].indirect(offsets[:, h * HALF // 16 : (h + 1) * HALF // 16]),
-                    in_=dense[:, slots(4 * h, 4 * h + 4)],
-                )
-            nc.sync.dma_start(out=out[b * P : (b + 1) * P, :], in_=window[b][:])
-
         def output_block(b):
-            dense = keep.tile([P, N], F32, name=f"dense{b}", tag=f"dense{b}", align_bytes=64)
+            dense = keep.tile([P, N], F32, name=f"dense{b}", tag=f"dense{b}", align_bytes=MX_ALIGN)
             nc.scalar.copy(out=dense[:], in_=acc[b][:])
             nc.vector.tensor_copy(out=window[b][:].indirect(offsets[:]), in_=dense[:])
             nc.sync.dma_start(out=out[b * P : (b + 1) * P, :], in_=window[b][:])
 
-        gather(0, 0, 8)
-        gather(1, 0, 8)
-        gather(2, 0, 8)
-        gather(3, 0, 8)
-        quantise_w(0, 8)
-        interleave_x_cols(0, 0, 0, 80, "vector")
-        interleave_x_cols(0, 0, 80, 128, "scalar")
-        interleave_x_cols(0, 1, 0, 64, "vector")
-        interleave_x_cols(0, 1, 64, 128, "scalar")
-        quantise_x(0, 0, 1)
-        quantise_x(0, 1, 2)
-        quantise_x(0, 2, 4)
-        scores_narrow(0, 0, 0)
-        scores_narrow(0, 0, 1)
-        scores(0, 1)
-        scores(0, 2)
-        scores(0, 3)
-        interleave_x_part(0, 6, "vector")
-        interleave_x_part_pair(6, 8, 0, "vector")
-        interleave_x_part_pair(6, 8, 1, "vector")
-        quantise_x(1, 0, 2)
-        quantise_x(1, 2, 4)
-        reuse(0,3,0,3)
-        scores(1, 0)
-        scores(1, 1)
-        scores(1, 2)
-        scores(1, 3)
-        weighted_targets(0, 0, 0, 6, "vector")
-        weighted_targets(0, 1, 0, 6, "vector")
-        gradient(0, 0, 0, 6)
-        gradient(0, 1, 0, 6)
-        weighted_targets(0, 2, 0, 6, "vector")
-        weighted_targets(0, 3, 0, 6, "vector")
-        gradient(0, 2, 0, 6)
-        gradient(0, 3, 0, 6)
-        for t in range(4):
-            turn(0,t)
-        close(0,3)
-        turn(1,0)
-        turn(1,1)
-        for s in (1,2,3):
-            turn(1,2,[s])
-            turn(1,3,[s])
-        weighted_targets(1, 0, 0, 2, "vector")
-        weighted_targets(1, 1, 0, 2, "vector")
-        weighted_targets(1, 2, 0, 2, "vector")
-        weighted_targets(1, 3, 0, 2, "vector")
-        gradient(1, 0, 0, 2)
-        gradient(1, 1, 0, 2)
-        gradient(1, 2, 0, 2)
-        gradient(1, 3, 0, 2)
-        close(1,1)
-        close(1,2)
-        close(1,3)
-        interleave_gradient(0, 0, 4, "scalar")
-        interleave_gradient(0, 4, 6, "scalar")
-        turn_back(0, 3, "scalar")
-        interleave_gradient(1, 0, 2, "scalar")
-        interleave_m(0, 0, "scalar")
-        turn_back(1, 1, "scalar")
-        warm_in(1,1)
-        interleave_m(0, 1, "scalar")
-        turn_back(1, 2, "scalar")
-        warm_in(1,2)
-        turn_back(1, 3, "scalar")
-        warm_in(1,3)
-        quantise_gradient(0, 0, 4)
-        quantise_gradient(0, 4, 8)
+        pairs = (slice(0, 2), slice(2, PACK))
+        for places, share in zip(pairs, X_SHARES):
+            lay_x(nc.vector, 0, x_first, 0, 0, share, places)
+            lay_x(nc.scalar, 0, x_first, 0, share, P, places)
+        for lo, hi in ((0, 1), (1, 2), (2, PACK)):
+            quantise_x(0, lo, hi)
+        for h in range(2):
+            scores(0, 0, slice(h * HALF, (h + 1) * HALF))
+        for t in range(1, PACK):
+            scores(0, t)
+
+        early = EARLY_ROWS // PACK
+        lay_x(nc.vector, 1, x_early, 0, 0, early, slice(0, PACK))
+        for places in pairs:
+            lay_x(nc.vector, 1, x_late, early, early, P, places)
+        for places in pairs:
+            quantise_x(1, places.start, places.stop)
+        for t in range(PACK):
+            scores(1, t)
+
+        for places in pairs:
+            for t in range(places.start, places.stop):
+                weigh_targets(0, t)
+            for t in range(places.start, places.stop):
+                gradient(0, t)
+        last = BLOCKS - 1
+        sums[0, last] = score_bank[0, PACK - 1]
+        for t in range(PACK):
+            turn(0, t, last)
+        gradient_turned(0, last)
+        lay_g(0, 2, last, nc.vector, slice(P // 2, P))
+
+        turned = range(DIRECT[1], BLOCKS)
+        for t in range(2):
+            for s in turned:
+                turn(1, t, s)
+        for s in turned:
+            for t in range(2, PACK):
+                turn(1, t, s)
+        for t in range(PACK):
+            weigh_targets(1, t)
+        for t in range(PACK):
+            gradient(1, t)
+        for s in turned:
+            gradient_turned(1, s)
+
+        lay_g(0, 0, 2)
+        lay_g(0, 2, last, nc.scalar, slice(0, P // 2))
+        words_bank = turn_back(0, last)
+        for h in range(2):
+            warm_up(words_bank)
+        lay_g(1, 0, DIRECT[1])
+        lay_m(nc.scalar, 0, 0, m_tile("m_bf00", "m_bf00")[:, 0])
+        lay_m(nc.scalar, 0, 1, m_tile("m_bf01", "m_bf01")[:, 0])
+        turn_back(1, 2)
+        turn_back(1, last)
+        warm_up(sums[1, last])
+
+        for h in range(2):
+            quantise_g(0, 2 * h, 2 * h + 2)
         quantise_m(0, 0)
+        acc[0] = sums[0, last]
         product(0, 0)
-        quantise_gradient(1, 0, 4)
+        quantise_g(1, 0, 2)
         quantise_m(0, 1)
-        quantise_gradient(1, 4, 6)
-        quantise_gradient(1, 6, 8)
+        for s in (2, last):
+            quantise_g(1, s, s + 1)
         product(0, 1)
         output_block(0)
-        interleave_m(1, 0, "vector")
-        interleave_m(1, 1, "vector")
-        quantise_m(1, 0)
-        quantise_m(1, 1)
-        product(1, 0)
-        product(1, 1)
-        output_block(1)
-        interleave_m(2, 0, "scalar")
-        interleave_m(2, 1, "scalar")
-        quantise_m(2, 0)
-        quantise_m(2, 1)
-        product(2, 0)
-        product(2, 1)
-        output_block(2)
-        interleave_m(3, 0, "vector")
-        interleave_m(3, 1, "scalar")
-        quantise_m(3, 0)
-        quantise_m(3, 1)
-        product(3, 0)
-        product(3, 1)
-        output_block(3)
+
+        first_late = m_tile("m_bf1", "g_half11", pieces=CHUNKS)
+        held = {
+            (2, 0): (nc.scalar, f"g_turned1{last}"),
+            (2, 1): (nc.scalar, "m_codes01"),
+            (3, 0): (nc.vector, "dense1"),
+            (3, 1): (nc.scalar, "m_codes11"),
+        }
+        for b in range(1, D // P):
+            for c in range(CHUNKS):
+                if b == 1:
+                    lay_m(nc.vector, b, c, first_late[:, c])
+                else:
+                    engine, tag = held[b, c]
+                    lay_m(engine, b, c, m_tile(f"m_bf{b}{c}", tag)[:, 0])
+            for c in range(CHUNKS):
+                quantise_m(b, c)
+            for c in range(CHUNKS):
+                product(b, c)
+            output_block(b)

@@ -25,7 +25,7 @@ HALF = N // 2
 MX_ALIGN = 64
 DMA_ALIGN = 256
 
-DIRECT = (3, 2)
+DIRECT = (3, 3)
 X_SHARES = (80, 64)
 EARLY_ROWS = 384
 
@@ -126,9 +126,14 @@ def tile_attend_gnce_w_kernel(tc, xT, wT, y, wt, xm, offs, out):
         w_bf = keep.tile([P, N, PACK], BF16, name="w_bf", align_bytes=MX_ALIGN)
         w_codes = keep.tile([P, N], U32, name="w_codes", align_bytes=MX_ALIGN)
         w_scales = keep.tile([P, N], U8, name="w_scales", align_bytes=MX_ALIGN)
-        for t in range(PACK):
+        for t in range(PACK - 1):
             nc.vector.tensor_copy(out=w_bf[:, :, t], in_=table[t][:].indirect(offsets[:]))
-        quantise(w_codes[:], w_scales[:], w_bf[:].rearrange("p n t -> p (n t)"), E4M3)
+        slot_halves = [slice(h * HALF, (h + 1) * HALF) for h in range(2)]
+        for h, cols in enumerate(slot_halves):
+            half_list = offsets[:, h * HALF // 16 : (h + 1) * HALF // 16]
+            nc.vector.tensor_copy(out=w_bf[:, cols, PACK - 1], in_=table[PACK - 1][:].indirect(half_list))
+        for cols in slot_halves:
+            quantise(w_codes[:, cols], w_scales[:, cols], w_bf[:, cols, :].rearrange("p n t -> p (n t)"), E4M3)
 
         x_bf = [keep.tile([P, PACK, P, PACK], BF16, name=f"x_bf{c}", align_bytes=MX_ALIGN) for c in range(CHUNKS)]
         x_codes = [keep.tile([P, K_PASS], U32, name=f"x_codes{c}", align_bytes=MX_ALIGN) for c in range(CHUNKS)]
@@ -181,7 +186,10 @@ def tile_attend_gnce_w_kernel(tc, xT, wT, y, wt, xm, offs, out):
             quantise(g_codes[c][:, cols], g_scales[c][:, cols], g_laid(c, lo, hi).rearrange("p n t -> p (n t)"), E5M2)
 
         rest = [keep.tile([P, PACK, DIRECT[c] * P], F32, name=f"rest{c}") for c in range(CHUNKS)]
-        g_rows = [keep.tile([P, PACK, DIRECT[c] * P], BF16, name=f"g_rows{c}") for c in range(CHUNKS)]
+        g_rows = {
+            (c, lo): keep.tile([P, PACK, (hi - lo) * P], BF16, name=f"g_rows{c}{lo}", tag=f"g_rows{c}{lo}", align_bytes=MX_ALIGN)
+            for c, lo, hi in ((0, 0, 3), (1, 0, 2), (1, 2, 3))
+        }
 
         def weigh_targets(c, t):
             nc.vector.tensor_scalar(
@@ -193,18 +201,20 @@ def tile_attend_gnce_w_kernel(tc, xT, wT, y, wt, xm, offs, out):
                 op1=ALU.add,
             )
 
-        def gradient(c, t):
+        def gradient(c, t, lo, hi):
+            cols = slice(lo * P, hi * P)
             nc.vector.scalar_tensor_tensor(
-                out=g_rows[c][:, t, :],
-                in0=sig[c][:, t, 0 : DIRECT[c] * P],
+                out=g_rows[c, lo][:, t, :],
+                in0=sig[c][:, t, cols],
                 scalar=minus_col[:, c, t, 0:1],
-                in1=rest[c][:, t, :],
+                in1=rest[c][:, t, cols],
                 op0=ALU.mult,
                 op1=ALU.add,
             )
 
         def lay_g(c, lo, hi, engine=nc.scalar, part=slice(0, None)):
-            side_by_side(engine, g_laid(c, lo, hi)[:, part, :], g_rows[c][:, :, lo * P : hi * P][:, :, part])
+            rows = g_rows[0, 0][:, :, lo * P : hi * P] if c == 0 else g_rows[c, lo][:]
+            side_by_side(engine, g_laid(c, lo, hi)[:, part, :], rows[:, :, part])
 
         sums, g_turned = {}, {}
 
@@ -292,53 +302,47 @@ def tile_attend_gnce_w_kernel(tc, xT, wT, y, wt, xm, offs, out):
         for t in range(PACK):
             scores(1, t)
 
+        last = BLOCKS - 1
         for places in pairs:
             for t in range(places.start, places.stop):
                 weigh_targets(0, t)
             for t in range(places.start, places.stop):
-                gradient(0, t)
-        last = BLOCKS - 1
+                gradient(0, t, 0, last)
         sums[0, last] = score_bank[0, PACK - 1]
         for t in range(PACK):
             turn(0, t, last)
         gradient_turned(0, last)
-        lay_g(0, 2, last, nc.vector, slice(P // 2, P))
 
-        turned = range(DIRECT[1], BLOCKS)
-        for t in range(2):
-            for s in turned:
-                turn(1, t, s)
-        for s in turned:
-            for t in range(2, PACK):
-                turn(1, t, s)
         for t in range(PACK):
             weigh_targets(1, t)
         for t in range(PACK):
-            gradient(1, t)
-        for s in turned:
-            gradient_turned(1, s)
+            turn(1, t, last)
+        for t in range(PACK):
+            gradient(1, t, 0, 2)
+        gradient_turned(1, last)
+        for t in range(PACK):
+            gradient(1, t, 2, last)
 
         lay_g(0, 0, 2)
-        lay_g(0, 2, last, nc.scalar, slice(0, P // 2))
+        lay_g(0, 2, last)
         words_bank = turn_back(0, last)
         for h in range(2):
             warm_up(words_bank)
-        lay_g(1, 0, DIRECT[1])
         lay_m(nc.scalar, 0, 0, m_tile("m_bf00", "m_bf00")[:, 0])
-        lay_m(nc.scalar, 0, 1, m_tile("m_bf01", "m_bf01")[:, 0])
-        turn_back(1, 2)
+        lay_g(1, 0, 2)
         turn_back(1, last)
         warm_up(sums[1, last])
+        lay_m(nc.scalar, 0, 1, m_tile("m_bf01", "g_rows10")[:, 0])
 
         for h in range(2):
             quantise_g(0, 2 * h, 2 * h + 2)
         quantise_m(0, 0)
         acc[0] = sums[0, last]
         product(0, 0)
+        lay_g(1, 2, last, nc.vector)
         quantise_g(1, 0, 2)
         quantise_m(0, 1)
-        for s in (2, last):
-            quantise_g(1, s, s + 1)
+        quantise_g(1, 2, BLOCKS)
         product(0, 1)
         output_block(0)
 

@@ -25,9 +25,33 @@ HALF = N // 2
 MX_ALIGN = 64
 DMA_ALIGN = 256
 
-DIRECT = (3, 3)
+DIRECT = (3, 2)
+SUM_BANK = {(0, 3): 3, (1, 2): 5, (1, 3): 1}
+WORD_BANK = {(0, 3): 5, (1, 2): 6, (1, 3): 0}
+ACC_BANK = (2, 7, 4, 3)
+SCORES0 = ((0, 4, 0, 256), (0, 0, 256, 512), (1, 5, 0, 256), (1, 1, 256, 512), (2, 2, 0, 512), (3, 3, 0, 512))
+TURN1 = (("s", (0,)), ("s", (1,)), ("y", (0, 1, 2, 3)), ("s", (2,)), ("s", (3,)))
+M_TAG = {(0, 0): "minus_row0", (0, 1): "g_turned13"}
+M01 = "s"
+G_TAG = ("y10", "g_codes1")
+M01_TAG = "g_rows10"
 X_SHARES = (80, 64)
-EARLY_ROWS = 384
+TABLE_LOADS = ((0, 1), (1, 2), (2, 3), (3, 4))
+X_LOADS = (((0, 64), (64, 128)), ((0, 64), (64, 96), (96, 128)))
+X_LAY = (
+    (("s", 0, 0, 64, 0, 4), ("v", 64, 64, 108, 0, 2), ("s", 64, 108, 128, 0, 2), ("v", 64, 64, 108, 2, 4), ("s", 64, 108, 128, 2, 4)),
+    (("v", 0, 0, 64, 0, 4), ("v", 64, 64, 96, 0, 4), ("v", 96, 96, 128, 0, 2), ("v", 96, 96, 128, 2, 4)),
+)
+PRE = 0
+XQ1 = ((0, 64), (64, 128))
+REST_TAG = {(0, 0): ("x_bf1", 2), (0, 2): ("x_bf1", 2), (1, 0): ("minus_row0", 4)}
+Y_LOADS = ((0, 0, 2), (0, 2, 4), (1, 0, 4))
+ORD0 = (("u", 0), ("u", 1), ("g", 0), ("g", 1), ("u", 2), ("u", 3), ("g", 2), ("g", 3))
+US = ()
+G02 = "v"
+G12 = "v"
+WARM_A = 0
+WARM_B = 2
 
 
 def tile_attend_gnce_w_kernel(tc, xT, wT, y, wt, xm, offs, out):
@@ -35,10 +59,10 @@ def tile_attend_gnce_w_kernel(tc, xT, wT, y, wt, xm, offs, out):
     with ExitStack() as ctx:
         lists = ctx.enter_context(tc.tile_pool(name="lists", bufs=1))
         keep = ctx.enter_context(tc.tile_pool(name="keep", bufs=1))
-        banks = ctx.enter_context(tc.psum_pool(name="banks", bufs=8))
+        banks = ctx.enter_context(tc.psum_pool(name="banks", bufs=1))
 
-        def new_bank():
-            return banks.tile([P, N], F32, name="bank")
+        def new_bank(k):
+            return banks.tile([P, N], F32, name=f"bank{k}", tag=f"bank{k}")
 
         def copy_on(engine, dst, src):
             if engine is nc.vector:
@@ -67,7 +91,7 @@ def tile_attend_gnce_w_kernel(tc, xT, wT, y, wt, xm, offs, out):
         for c in range(CHUNKS):
             row = slice(c * apart, c * apart + 1)
             nc.scalar.copy(out=wt_dealt[row, :, :], in_=wt_rows[row, :].rearrange("c (p t) -> c t p", t=PACK))
-        wt_bank = new_bank()[:].rearrange("p (t k) -> p t k", t=PACK)
+        wt_bank = new_bank(7)[:].rearrange("p (t k) -> p t k", t=PACK)
         for t in range(PACK):
             nc.tensor.transpose(wt_bank[:, t, :], wt_dealt[:, t, :], identity[:])
         nc.scalar.copy(out=weight[:], in_=wt_bank.rearrange("p t (c k) -> p c t k", c=CHUNKS)[:, :, :, 0])
@@ -85,15 +109,15 @@ def tile_attend_gnce_w_kernel(tc, xT, wT, y, wt, xm, offs, out):
             func=ACT.Copy,
             scale=-1.0,
         )
-        minus_row = [keep.tile([P, 2 * P, 2], F32, name=f"minus_row{c}", align_bytes=MX_ALIGN) for c in range(CHUNKS)]
+        minus_row = [keep.tile([P, 2 * P, 2], F32, name=f"minus_row{c}", tag=f"minus_row{c}", align_bytes=DMA_ALIGN) for c in range(CHUNKS)]
         for c in range(CHUNKS):
-            bank = new_bank()
+            bank = new_bank(5 + c)
             for t in range(PACK):
                 nc.tensor.transpose(place_of(bank, t), minus_col[:, c, t, :], identity[:])
             nc.scalar.copy(out=minus_row[c][:], in_=by_words(bank))
 
         def load(name, src):
-            tile = keep.tile(list(src.shape), F32, name=name, align_bytes=DMA_ALIGN)
+            tile = keep.tile(list(src.shape), F32, name=name, tag=name, align_bytes=DMA_ALIGN)
             nc.sync.dma_start(out=tile[:], in_=src)
             return tile
 
@@ -103,16 +127,23 @@ def tile_attend_gnce_w_kernel(tc, xT, wT, y, wt, xm, offs, out):
         y_rows = y[0].rearrange("(c p t) i -> c p t i", c=CHUNKS, t=PACK)
         m_rows = xm[0].rearrange("(c p t) d -> c p t d", c=CHUNKS, t=PACK)
 
-        table = [load("table0", w_rows[:, 0, :])]
-        nc.sync.dma_start(offsets[:], offs)
-        table.extend(load(f"table{t}", w_rows[:, t, :]) for t in range(1, PACK))
-        x_first = load("x_first", x_rows[:, :, 0:K_PASS])
-        x_early = load("x_early", x_rows[:, :, K_PASS : K_PASS + EARLY_ROWS])
-        x_late = load("x_late", x_rows[:, :, K_PASS + EARLY_ROWS : R])
-        y_raw = {(0, t): load(f"y0{t}", y_rows[0, :, t, :])[:] for t in range(2)}
-        for c, u in ((0, 1), (1, 0), (1, 1)):
-            pair = load(f"y_pair{c}{u}", y_rows[c, :, 2 * u : 2 * u + 2, :])
-            y_raw.update({(c, 2 * u + e): pair[:, e, :] for e in range(2)})
+        table = []
+        for lo, hi in TABLE_LOADS:
+            planes = load(f"table{lo}", w_rows[:, lo:hi, :])
+            table.extend(planes[:, t, :] for t in range(hi - lo))
+            if lo == 0:
+                nc.sync.dma_start(offsets[:], offs)
+        x_raw = {}
+        for c in range(CHUNKS):
+            for lo, hi in X_LOADS[c]:
+                x_raw[c, lo] = load(f"x{c}_{lo}", x_rows[:, :, c * K_PASS + PACK * lo : c * K_PASS + PACK * hi])
+        y_raw = {}
+        for c, lo, hi in Y_LOADS:
+            for h in ((1, 0) if c == 1 else (None,)):
+                cols = slice(0, N) if h is None else slice(h * HALF, (h + 1) * HALF)
+                part = load(f"y{c}{lo}" + ("t" if h == 1 else ""), y_rows[c, :, lo:hi, cols])
+                for s in range(cols.start // P, cols.stop // P):
+                    y_raw.update({(c, t, s): part[:, t - lo, s * P - cols.start :] for t in range(lo, hi)})
         m_raw = {}
         for lo, hi in ((0, 1), (1, 2), (2, 4)):
             for c in range(CHUNKS):
@@ -127,15 +158,15 @@ def tile_attend_gnce_w_kernel(tc, xT, wT, y, wt, xm, offs, out):
         w_codes = keep.tile([P, N], U32, name="w_codes", align_bytes=MX_ALIGN)
         w_scales = keep.tile([P, N], U8, name="w_scales", align_bytes=MX_ALIGN)
         for t in range(PACK - 1):
-            nc.vector.tensor_copy(out=w_bf[:, :, t], in_=table[t][:].indirect(offsets[:]))
+            nc.vector.tensor_copy(out=w_bf[:, :, t], in_=table[t].indirect(offsets[:]))
         slot_halves = [slice(h * HALF, (h + 1) * HALF) for h in range(2)]
         for h, cols in enumerate(slot_halves):
             half_list = offsets[:, h * HALF // 16 : (h + 1) * HALF // 16]
-            nc.vector.tensor_copy(out=w_bf[:, cols, PACK - 1], in_=table[PACK - 1][:].indirect(half_list))
+            nc.vector.tensor_copy(out=w_bf[:, cols, PACK - 1], in_=table[PACK - 1].indirect(half_list))
         for cols in slot_halves:
             quantise(w_codes[:, cols], w_scales[:, cols], w_bf[:, cols, :].rearrange("p n t -> p (n t)"), E4M3)
 
-        x_bf = [keep.tile([P, PACK, P, PACK], BF16, name=f"x_bf{c}", align_bytes=MX_ALIGN) for c in range(CHUNKS)]
+        x_bf = [keep.tile([P, PACK, P, PACK], BF16, name=f"x_bf{c}", tag=f"x_bf{c}", align_bytes=DMA_ALIGN) for c in range(CHUNKS)]
         x_codes = [keep.tile([P, K_PASS], U32, name=f"x_codes{c}", align_bytes=MX_ALIGN) for c in range(CHUNKS)]
         x_scales = [keep.tile([P, K_PASS], U8, name=f"x_scales{c}", align_bytes=MX_ALIGN) for c in range(CHUNKS)]
 
@@ -160,41 +191,59 @@ def tile_attend_gnce_w_kernel(tc, xT, wT, y, wt, xm, offs, out):
             )
 
         sig = [keep.tile([P, PACK, N], F32, name=f"sig{c}") for c in range(CHUNKS)]
-        score_bank = {}
 
-        def scores(c, t, cols=slice(0, N)):
-            score_bank[c, t] = new_bank()
-            score_pass(score_bank[c, t][:, cols], c, t, cols)
-            nc.scalar.activation(out=sig[c][:, t, cols], in_=score_bank[c, t][:, cols], func=ACT.Sigmoid, scale=-1.0)
+        def scores(c, t, k, cols=slice(0, N)):
+            bank = new_bank(k)
+            score_pass(bank[:, cols], c, t, cols)
+            nc.scalar.activation(out=sig[c][:, t, cols], in_=bank[:, cols], func=ACT.Sigmoid, scale=-1.0)
 
         def warm_up(bank):
             score_pass(bank[:], 0, 0, slice(0, N))
 
-        g_codes = [keep.tile([P, N], U32, name=f"g_codes{c}", align_bytes=MX_ALIGN) for c in range(CHUNKS)]
+        g_codes = {}
         g_scales = [keep.tile([P, N], U8, name=f"g_scales{c}", align_bytes=MX_ALIGN) for c in range(CHUNKS)]
         g_half = {
-            (c, h): keep.tile([P, HALF, PACK], BF16, name=f"g_half{c}{h}", tag=f"g_half{c}{h}", align_bytes=MX_ALIGN)
+            (c, h): keep.tile([P, HALF, PACK], BF16, name=f"g_half{c}{h}", tag="m_part10" if (c, h) == (1, 1) else f"g_half{c}{h}", align_bytes=DMA_ALIGN)
             for c in range(CHUNKS)
             for h in range(2)
         }
 
         def g_laid(c, lo, hi):
+            if (c, lo) == (0, 3):
+                if "words" not in g_half:
+                    g_half["words"] = keep.tile([P, P, PACK], BF16, name="g_words", tag="m_part00", align_bytes=DMA_ALIGN)
+                return g_half["words"][:]
             return g_half[c, lo // 2][:, (lo % 2) * P : (lo % 2 + hi - lo) * P, :]
 
         def quantise_g(c, lo, hi):
             cols = slice(lo * P, hi * P)
+            if c not in g_codes:
+                g_codes[c] = keep.tile([P, N], U32, name=f"g_codes{c}", tag=G_TAG[c], align_bytes=DMA_ALIGN)
             quantise(g_codes[c][:, cols], g_scales[c][:, cols], g_laid(c, lo, hi).rearrange("p n t -> p (n t)"), E5M2)
 
-        rest = [keep.tile([P, PACK, DIRECT[c] * P], F32, name=f"rest{c}") for c in range(CHUNKS)]
+        rest = {}
         g_rows = {
-            (c, lo): keep.tile([P, PACK, (hi - lo) * P], BF16, name=f"g_rows{c}{lo}", tag=f"g_rows{c}{lo}", align_bytes=MX_ALIGN)
-            for c, lo, hi in ((0, 0, 3), (1, 0, 2), (1, 2, 3))
+            (c, lo): keep.tile([P, PACK, (hi - lo) * P], BF16, name=f"g_rows{c}{lo}", tag="minus_row1" if c == 1 else "g_rows00", align_bytes=DMA_ALIGN)
+            for c, lo, hi in ((0, 0, 3), (1, 0, 2))
         }
 
         def weigh_targets(c, t):
+            if (c, t) in REST_TAG:
+                tag, places = REST_TAG[c, t]
+                part = keep.tile([P, places, DIRECT[c] * P], F32, name=f"rest{c}{t}", tag=tag, align_bytes=DMA_ALIGN)
+                rest.update({(c, t + k): part[:, k, :] for k in range(places)})
+            if (c, t) in US:
+                nc.scalar.activation(
+                    out=rest[c, t],
+                    in_=sig[c][:, t, 0 : DIRECT[c] * P],
+                    func=ACT.Identity,
+                    scale=minus_col[:, c, t, 0:1],
+                    bias=weight[:, c, t : t + 1],
+                )
+                return
             nc.vector.tensor_scalar(
-                out=rest[c][:, t, :],
-                in0=y_raw[c, t][:, 0 : DIRECT[c] * P],
+                out=rest[c, t],
+                in0=sig[c][:, t, 0 : DIRECT[c] * P],
                 scalar1=minus_col[:, c, t, 0:1],
                 scalar2=weight[:, c, t : t + 1],
                 op0=ALU.mult,
@@ -205,30 +254,38 @@ def tile_attend_gnce_w_kernel(tc, xT, wT, y, wt, xm, offs, out):
             cols = slice(lo * P, hi * P)
             nc.vector.scalar_tensor_tensor(
                 out=g_rows[c, lo][:, t, :],
-                in0=sig[c][:, t, cols],
+                in0=y_raw[c, t, lo][:, 0 : (hi - lo) * P],
                 scalar=minus_col[:, c, t, 0:1],
-                in1=rest[c][:, t, cols],
+                in1=rest[c, t][:, cols],
                 op0=ALU.mult,
                 op1=ALU.add,
             )
 
         def lay_g(c, lo, hi, engine=nc.scalar, part=slice(0, None)):
-            rows = g_rows[0, 0][:, :, lo * P : hi * P] if c == 0 else g_rows[c, lo][:]
+            rows = g_rows[c, 0][:, :, lo * P : hi * P]
             side_by_side(engine, g_laid(c, lo, hi)[:, part, :], rows[:, :, part])
 
-        sums, g_turned = {}, {}
+        sums, turned, g_turned = {}, {}, {}
 
-        def turn(c, t, s):
+        def turn(c, s, what, places):
             if (c, s) not in sums:
-                sums[c, s] = new_bank()
-            cols = slice(s * P, (s + 1) * P)
-            dst = place_of(sums[c, s], t)
-            nc.tensor.matmul(dst, lhsT=sig[c][:, t, cols], rhs=identity[:], start=True, stop=False, is_transpose=True)
-            nc.tensor.matmul(dst, lhsT=y_raw[c, t][:, cols], rhs=identity[:], start=False, stop=True, is_transpose=True)
+                sums[c, s] = new_bank(SUM_BANK[c, s])
+                turned[c, s] = 0
+            for t in places:
+                src = sig[c][:, t, s * P :] if what == "s" else y_raw[c, t, s]
+                turned[c, s] = turned[c, s] + 1
+                nc.tensor.matmul(
+                    place_of(sums[c, s], t),
+                    lhsT=src[:, 0:P],
+                    rhs=identity[:],
+                    start=turned[c, s] == 1,
+                    stop=turned[c, s] == 2 * PACK,
+                    is_transpose=True,
+                )
 
         def gradient_turned(c, s):
             g_turned[c, s] = keep.tile(
-                [P, 2 * P, 2], BF16, name=f"g_turned{c}{s}", tag=f"g_turned{c}{s}", align_bytes=MX_ALIGN
+                [P, 2 * P, 2], BF16, name=f"g_turned{c}{s}", tag=f"g_turned{c}{s}", align_bytes=DMA_ALIGN
             )
             nc.vector.scalar_tensor_tensor(
                 out=g_turned[c, s][:],
@@ -241,7 +298,7 @@ def tile_attend_gnce_w_kernel(tc, xT, wT, y, wt, xm, offs, out):
 
         def turn_back(c, s):
             words = g_turned[c, s][:].rearrange("p w e -> p (w e)").bitcast(F32)
-            whole = new_bank()
+            whole = new_bank(WORD_BANK[c, s])
             bank = whole[:, 0 : 2 * P].rearrange("p (u n) -> p u n", u=2)
             for u in range(2):
                 nc.tensor.transpose(bank[:, u, :], words[:, u * P : (u + 1) * P], identity[:])
@@ -256,16 +313,16 @@ def tile_attend_gnce_w_kernel(tc, xT, wT, y, wt, xm, offs, out):
             side_by_side(engine, dst, m_raw[b, c])
 
         def m_tile(name, tag, pieces=1):
-            return keep.tile([P, pieces, P, PACK], BF16, name=name, tag=tag, align_bytes=MX_ALIGN)
+            return keep.tile([P, pieces, P, PACK], BF16, name=name, tag=tag, align_bytes=DMA_ALIGN)
 
         def quantise_m(b, c):
-            m_codes[b, c] = keep.tile([P, P], U32, name=f"m_codes{b}{c}", tag=f"m_codes{b}{c}", align_bytes=MX_ALIGN)
+            m_codes[b, c] = keep.tile([P, P], U32, name=f"m_codes{b}{c}", tag=M_TAG.get((b, c), f"m_codes{b}{c}"), align_bytes=DMA_ALIGN)
             m_scales[b, c] = keep.tile([P, P], U8, name=f"m_scales{b}{c}", align_bytes=MX_ALIGN)
             quantise(m_codes[b, c][:], m_scales[b, c][:], m_bf[b, c].rearrange("p n t -> p (n t)"), E4M3)
 
         def product(b, c):
             if b not in acc:
-                acc[b] = new_bank()
+                acc[b] = new_bank(ACC_BANK[b])
             nc.tensor.matmul_mx(
                 out=acc[b][:],
                 lhsT=m_codes[b, c][:].bitcast(E4M3),
@@ -283,85 +340,93 @@ def tile_attend_gnce_w_kernel(tc, xT, wT, y, wt, xm, offs, out):
             nc.sync.dma_start(out=out[b * P : (b + 1) * P, :], in_=window[b][:])
 
         pairs = (slice(0, 2), slice(2, PACK))
-        for places, share in zip(pairs, X_SHARES):
-            lay_x(nc.vector, 0, x_first, 0, 0, share, places)
-            lay_x(nc.scalar, 0, x_first, 0, share, P, places)
+        engines = {"v": nc.vector, "s": nc.scalar}
+        for k in range(PRE):
+            spare = new_bank(7)
+            nc.tensor.matmul_mx(
+                out=spare[:, 0:HALF],
+                lhsT=w_codes[:, 0:P].bitcast(E4M3),
+                lhsT_scale=w_scales[:, 0:P],
+                rhs=w_codes[:, 0:HALF].bitcast(E4M3),
+                rhs_scale=w_scales[:, 0:HALF],
+                start=True,
+                stop=True,
+            )
+        for e, first, lo, hi, a, z in X_LAY[0]:
+            lay_x(engines[e], 0, x_raw[0, first], first, lo, hi, slice(a, z))
         for lo, hi in ((0, 1), (1, 2), (2, PACK)):
             quantise_x(0, lo, hi)
-        for h in range(2):
-            scores(0, 0, slice(h * HALF, (h + 1) * HALF))
-        for t in range(1, PACK):
-            scores(0, t)
+        for t, k, lo, hi in SCORES0:
+            scores(0, t, k, slice(lo, hi))
 
-        early = EARLY_ROWS // PACK
-        lay_x(nc.vector, 1, x_early, 0, 0, early, slice(0, PACK))
-        for places in pairs:
-            lay_x(nc.vector, 1, x_late, early, early, P, places)
-        for places in pairs:
-            quantise_x(1, places.start, places.stop)
-        for t in range(PACK):
-            scores(1, t)
+        for e, first, lo, hi, a, z in X_LAY[1]:
+            lay_x(engines[e], 1, x_raw[1, first], first, lo, hi, slice(a, z))
+        for lo, hi in XQ1:
+            if hi - lo == P:
+                for places in pairs:
+                    quantise_x(1, places.start, places.stop)
+            else:
+                for t in range(PACK):
+                    cols = slice(t * P + lo, t * P + hi)
+                    laid = x_bf[1][:, t, lo:hi, :].rearrange("p m j -> p (m j)")
+                    quantise(x_codes[1][:, cols], x_scales[1][:, cols], laid, E4M3)
+        for t, k in enumerate((6, 7, 4, 0)):
+            scores(1, t, k)
 
         last = BLOCKS - 1
-        for places in pairs:
-            for t in range(places.start, places.stop):
+        for kind, t in ORD0:
+            if kind == "u":
                 weigh_targets(0, t)
-            for t in range(places.start, places.stop):
+            else:
                 gradient(0, t, 0, last)
-        sums[0, last] = score_bank[0, PACK - 1]
-        for t in range(PACK):
-            turn(0, t, last)
+        for what, places in (("y", (2, 3, 0, 1)), ("s", (0, 1, 2, 3))):
+            turn(0, last, what, places)
         gradient_turned(0, last)
 
         for t in range(PACK):
             weigh_targets(1, t)
-        for t in range(PACK):
-            turn(1, t, last)
+        for s in (2, 3):
+            for what in "ys":
+                turn(1, s, what, range(PACK))
+        for s in (2, 3):
+            gradient_turned(1, s)
         for t in range(PACK):
             gradient(1, t, 0, 2)
-        gradient_turned(1, last)
-        for t in range(PACK):
-            gradient(1, t, 2, last)
 
         lay_g(0, 0, 2)
         lay_g(0, 2, last)
-        words_bank = turn_back(0, last)
-        for h in range(2):
-            warm_up(words_bank)
         lay_m(nc.scalar, 0, 0, m_tile("m_bf00", "m_bf00")[:, 0])
-        lay_g(1, 0, 2)
-        turn_back(1, last)
-        warm_up(sums[1, last])
-        lay_m(nc.scalar, 0, 1, m_tile("m_bf01", "g_rows10")[:, 0])
+        turn_back(0, last)
+        lay_m(nc.scalar, 0, 1, m_tile("m_bf01", "m_bf01")[:, 0])
+        for s in (2, 3):
+            turn_back(1, s)
+        for h in range(WARM_B):
+            warm_up(sums[1, last])
+        lay_g(1, 0, 1)
+        quantise_g(0, 0, 2)
+        lay_g(1, 1, 2, nc.vector)
 
-        for h in range(2):
-            quantise_g(0, 2 * h, 2 * h + 2)
+        quantise_g(0, 2, 3)
+        quantise_g(0, 3, 4)
         quantise_m(0, 0)
-        acc[0] = sums[0, last]
         product(0, 0)
-        lay_g(1, 2, last, nc.vector)
-        quantise_g(1, 0, 2)
+        quantise_g(1, 2, 4)
         quantise_m(0, 1)
-        quantise_g(1, 2, BLOCKS)
+        quantise_g(1, 0, 2)
         product(0, 1)
         output_block(0)
 
-        first_late = m_tile("m_bf1", "g_half11", pieces=CHUNKS)
-        held = {
-            (2, 0): (nc.scalar, f"g_turned1{last}"),
-            (2, 1): (nc.scalar, "m_codes01"),
-            (3, 0): (nc.vector, "dense1"),
-            (3, 1): (nc.scalar, "m_codes11"),
-        }
-        for b in range(1, D // P):
+        def prepare(b, engine, tag):
+            laid = m_tile(f"m_bf{b}", tag, pieces=CHUNKS)
             for c in range(CHUNKS):
-                if b == 1:
-                    lay_m(nc.vector, b, c, first_late[:, c])
-                else:
-                    engine, tag = held[b, c]
-                    lay_m(engine, b, c, m_tile(f"m_bf{b}{c}", tag)[:, 0])
+                lay_m(engine, b, c, laid[:, c])
             for c in range(CHUNKS):
                 quantise_m(b, c)
+
+        prepare(1, nc.vector, "g_half10")
+        for b in range(1, D // P):
             for c in range(CHUNKS):
                 product(b, c)
+            if b + 1 < D // P:
+                prepare(b + 1, nc.scalar, f"m_codes{b}0")
             output_block(b)

@@ -31,22 +31,22 @@ WORD_BANK = {(0, 3): 5, (1, 2): 6, (1, 3): 0}
 ACC_BANK = (2, 7, 4, 3)
 SCORES0 = ((0, 4, 0, 256), (0, 0, 256, 512), (1, 5, 0, 256), (1, 1, 256, 512), (2, 2, 0, 512), (3, 3, 0, 512))
 TURN1 = (("s", (0,)), ("s", (1,)), ("y", (0, 1, 2, 3)), ("s", (2,)), ("s", (3,)))
-M_TAG = {(0, 0): "minus_row0", (0, 1): "g_turned13"}
+M_TAG = {(0, 0): "rest03", (0, 1): "g_turned12"}
 M01 = "s"
-G_TAG = ("y10", "g_codes1")
+G_TAG = ("x1_96", "g_codes1")
 M01_TAG = "g_rows10"
 X_SHARES = (80, 64)
 TABLE_LOADS = ((0, 1), (1, 2), (2, 3), (3, 4))
-X_LOADS = (((0, 64), (64, 128)), ((0, 64), (64, 96), (96, 128)))
+X_LOADS = (((0, 128),), ((0, 96), (96, 128)))
 X_LAY = (
-    (("s", 0, 0, 64, 0, 4), ("v", 64, 64, 108, 0, 2), ("s", 64, 108, 128, 0, 2), ("v", 64, 64, 108, 2, 4), ("s", 64, 108, 128, 2, 4)),
-    (("v", 0, 0, 64, 0, 4), ("v", 64, 64, 96, 0, 4), ("v", 96, 96, 128, 0, 2), ("v", 96, 96, 128, 2, 4)),
+    (("v", 0, 0, 80, 0, 2), ("s", 0, 80, 128, 0, 2), ("v", 0, 0, 64, 2, 4), ("s", 0, 64, 128, 2, 4)),
+    (("v", 0, 0, 96, 0, 4), ("v", 96, 96, 128, 0, 2), ("v", 96, 96, 128, 2, 4)),
 )
 PRE = 0
-XQ1 = ((0, 64), (64, 128))
-REST_TAG = {(0, 0): ("x_bf1", 2), (0, 2): ("x_bf1", 2), (1, 0): ("minus_row0", 4)}
+XQ1 = ((0, 128),)
+REST_TAG = {(0, 0): ("x1_96", 3), (0, 3): ("rest03", 1), (1, 0): ("x1_96", 3), (1, 3): ("rest03", 1)}
 Y_LOADS = ((0, 0, 2), (0, 2, 4), (1, 0, 4))
-ORD0 = (("u", 0), ("u", 1), ("g", 0), ("g", 1), ("u", 2), ("u", 3), ("g", 2), ("g", 3))
+ORD0 = (("u", 0), ("u", 1), ("u", 2), ("g", 0), ("g", 1), ("u", 3), ("g", 2), ("g", 3))
 US = ()
 G02 = "v"
 G12 = "v"
@@ -137,18 +137,25 @@ def tile_attend_gnce_w_kernel(tc, xT, wT, y, wt, xm, offs, out):
         for c in range(CHUNKS):
             for lo, hi in X_LOADS[c]:
                 x_raw[c, lo] = load(f"x{c}_{lo}", x_rows[:, :, c * K_PASS + PACK * lo : c * K_PASS + PACK * hi])
-        y_raw = {}
-        for c, lo, hi in Y_LOADS:
-            for h in ((1, 0) if c == 1 else (None,)):
-                cols = slice(0, N) if h is None else slice(h * HALF, (h + 1) * HALF)
-                part = load(f"y{c}{lo}" + ("t" if h == 1 else ""), y_rows[c, :, lo:hi, cols])
-                for s in range(cols.start // P, cols.stop // P):
-                    y_raw.update({(c, t, s): part[:, t - lo, s * P - cols.start :] for t in range(lo, hi)})
-        m_raw = {}
-        for lo, hi in ((0, 1), (1, 2), (2, 4)):
+        y_raw, m_raw = {}, {}
+
+        def load_y(name, c, lo, hi, first, end):
+            part = load(name, y_rows[c, :, lo:hi, first * P : end * P])
+            for s in range(first, end):
+                y_raw.update({(c, t, s): part[:, t - lo, (s - first) * P :] for t in range(lo, hi)})
+
+        def load_m(lo, hi):
             for c in range(CHUNKS):
                 part = load(f"m_part{c}{lo}", m_rows[c, :, :, lo * P : hi * P])
                 m_raw.update({(b, c): part[:, :, (b - lo) * P : (b - lo + 1) * P] for b in range(lo, hi)})
+
+        load_y("y00", 0, 0, 2, 0, BLOCKS)
+        load_y("y02", 0, 2, PACK, 0, BLOCKS)
+        load_y("y1_turned", 1, 0, PACK, 2, BLOCKS)
+        load_y("y1_direct", 1, 0, PACK, 0, 2)
+        load_m(0, 1)
+        load_m(1, 2)
+        load_m(2, 4)
 
         window = [keep.tile([P, T], F32, name=f"window{b}", align_bytes=DMA_ALIGN) for b in range(D // P)]
         for b in range(D // P):
@@ -213,6 +220,10 @@ def tile_attend_gnce_w_kernel(tc, xT, wT, y, wt, xm, offs, out):
                 if "words" not in g_half:
                     g_half["words"] = keep.tile([P, P, PACK], BF16, name="g_words", tag="m_part00", align_bytes=DMA_ALIGN)
                 return g_half["words"][:]
+            if (c, lo) == (1, 0):
+                if "last" not in g_half:
+                    g_half["last"] = keep.tile([P, P, PACK], BF16, name="g_last", tag="g_turned13", align_bytes=DMA_ALIGN)
+                return g_half["last"][:]
             return g_half[c, lo // 2][:, (lo % 2) * P : (lo % 2 + hi - lo) * P, :]
 
         def quantise_g(c, lo, hi):
@@ -223,7 +234,7 @@ def tile_attend_gnce_w_kernel(tc, xT, wT, y, wt, xm, offs, out):
 
         rest = {}
         g_rows = {
-            (c, lo): keep.tile([P, PACK, (hi - lo) * P], BF16, name=f"g_rows{c}{lo}", tag="minus_row1" if c == 1 else "g_rows00", align_bytes=DMA_ALIGN)
+            (c, lo): keep.tile([P, PACK, (hi - lo) * P], BF16, name=f"g_rows{c}{lo}", tag=f"g_rows{c}{lo}", align_bytes=DMA_ALIGN)
             for c, lo, hi in ((0, 0, 3), (1, 0, 2))
         }
 
@@ -316,16 +327,21 @@ def tile_attend_gnce_w_kernel(tc, xT, wT, y, wt, xm, offs, out):
             return keep.tile([P, pieces, P, PACK], BF16, name=name, tag=tag, align_bytes=DMA_ALIGN)
 
         def quantise_m(b, c):
-            m_codes[b, c] = keep.tile([P, P], U32, name=f"m_codes{b}{c}", tag=M_TAG.get((b, c), f"m_codes{b}{c}"), align_bytes=DMA_ALIGN)
+            if b == 0:
+                if "first" not in m_codes:
+                    m_codes["first"] = keep.tile([P, CHUNKS, P], U32, name="m_codes0", tag="rest03", align_bytes=DMA_ALIGN)
+                m_codes[b, c] = m_codes["first"][:, c]
+            else:
+                m_codes[b, c] = keep.tile([P, P], U32, name=f"m_codes{b}{c}", tag=f"m_codes{b}{c}", align_bytes=DMA_ALIGN)[:]
             m_scales[b, c] = keep.tile([P, P], U8, name=f"m_scales{b}{c}", align_bytes=MX_ALIGN)
-            quantise(m_codes[b, c][:], m_scales[b, c][:], m_bf[b, c].rearrange("p n t -> p (n t)"), E4M3)
+            quantise(m_codes[b, c], m_scales[b, c][:], m_bf[b, c].rearrange("p n t -> p (n t)"), E4M3)
 
         def product(b, c):
             if b not in acc:
                 acc[b] = new_bank(ACC_BANK[b])
             nc.tensor.matmul_mx(
                 out=acc[b][:],
-                lhsT=m_codes[b, c][:].bitcast(E4M3),
+                lhsT=m_codes[b, c].bitcast(E4M3),
                 lhsT_scale=m_scales[b, c][:],
                 rhs=g_codes[c][:].bitcast(E5M2),
                 rhs_scale=g_scales[c][:],
@@ -404,29 +420,38 @@ def tile_attend_gnce_w_kernel(tc, xT, wT, y, wt, xm, offs, out):
             warm_up(sums[1, last])
         lay_g(1, 0, 1)
         quantise_g(0, 0, 2)
+        quantise_g(0, 2, 3)
         lay_g(1, 1, 2, nc.vector)
 
-        quantise_g(0, 2, 3)
         quantise_g(0, 3, 4)
         quantise_m(0, 0)
         product(0, 0)
         quantise_g(1, 2, 4)
         quantise_m(0, 1)
-        quantise_g(1, 0, 2)
+        quantise_g(1, 1, 2)
+        quantise_g(1, 0, 1)
         product(0, 1)
         output_block(0)
 
-        def prepare(b, engine, tag):
-            laid = m_tile(f"m_bf{b}", tag, pieces=CHUNKS)
-            for c in range(CHUNKS):
-                lay_m(engine, b, c, laid[:, c])
-            for c in range(CHUNKS):
-                quantise_m(b, c)
-
-        prepare(1, nc.vector, "g_half10")
-        for b in range(1, D // P):
-            for c in range(CHUNKS):
-                product(b, c)
-            if b + 1 < D // P:
-                prepare(b + 1, nc.scalar, f"m_codes{b}0")
-            output_block(b)
+        behind_g = m_tile("m_behind_g", "g_turned13", pieces=3)
+        for c in range(CHUNKS):
+            lay_m(nc.vector, 1, c, behind_g[:, c])
+        lay_m(nc.scalar, 2, 0, behind_g[:, 2])
+        for b, c in ((1, 0), (2, 0), (1, 1)):
+            quantise_m(b, c)
+        for c in range(CHUNKS):
+            product(1, c)
+        lay_m(nc.scalar, 2, 1, m_tile("m_bf21", "m_codes10")[:, 0])
+        quantise_m(2, 1)
+        output_block(1)
+        for c in range(CHUNKS):
+            product(2, c)
+        third = m_tile("m_bf3", "m_codes11", pieces=CHUNKS)
+        for c in range(CHUNKS):
+            lay_m(nc.scalar, 3, c, third[:, c])
+        for c in range(CHUNKS):
+            quantise_m(3, c)
+        output_block(2)
+        for c in range(CHUNKS):
+            product(3, c)
+        output_block(3)

@@ -151,9 +151,10 @@ def tile_attend_gnce_w_kernel(tc, xT, wT, y, wt, xm, offs, out):
 
         load_y("y00", 0, 0, 2, 0, BLOCKS)
         load_y("y02", 0, 2, PACK, 0, BLOCKS)
-        load_y("y1_turned", 1, 0, PACK, 2, BLOCKS)
-        load_y("y1_direct", 1, 0, PACK, 0, 2)
+        for s in (2, 3):
+            load_y(f"y1_turned{s}", 1, 0, PACK, s, s + 1)
         load_m(0, 1)
+        load_y("y1_direct", 1, 0, PACK, 0, 2)
         load_m(1, 2)
         load_m(2, 4)
 
@@ -402,8 +403,11 @@ def tile_attend_gnce_w_kernel(tc, xT, wT, y, wt, xm, offs, out):
         for t in range(PACK):
             weigh_targets(1, t)
         for s in (2, 3):
-            for what in "ys":
-                turn(1, s, what, range(PACK))
+            turn(1, s, "y", range(PACK))
+            turn(1, s, "s", (0, 1))
+        for t in (2, 3):
+            for s in (2, 3):
+                turn(1, s, "s", (t,))
         for s in (2, 3):
             gradient_turned(1, s)
         for t in range(PACK):

@@ -33,25 +33,25 @@ SCORES0 = ((0, 4, 0, 256), (0, 0, 256, 512), (1, 5, 0, 256), (1, 1, 256, 512), (
 TURN1 = (("s", (0,)), ("s", (1,)), ("y", (0, 1, 2, 3)), ("s", (2,)), ("s", (3,)))
 M_TAG = {(0, 0): "rest03", (0, 1): "g_turned12"}
 M01 = "s"
-G_TAG = ("x1_96", "g_codes1")
+G_TAG = ("x1_80", "g_codes1")
 M01_TAG = "g_rows10"
 X_SHARES = (80, 64)
 TABLE_LOADS = ((0, 1), (1, 2), (2, 3), (3, 4))
-X_LOADS = (((0, 128),), ((0, 96), (96, 128)))
+X_LOADS = (((0, 128),), ((0, 80), (80, 128)))
 X_LAY = (
     (("v", 0, 0, 80, 0, 2), ("s", 0, 80, 128, 0, 2), ("v", 0, 0, 64, 2, 4), ("s", 0, 64, 128, 2, 4)),
-    (("v", 0, 0, 96, 0, 4), ("v", 96, 96, 128, 0, 2), ("v", 96, 96, 128, 2, 4)),
+    (("v", 0, 0, 80, 0, 4), ("v", 80, 80, 128, 0, 2), ("v", 80, 80, 128, 2, 4)),
 )
-PRE = 0
+PRE = 2
 XQ1 = ((0, 128),)
-REST_TAG = {(0, 0): ("x1_96", 3), (0, 3): ("rest03", 1), (1, 0): ("x1_96", 3), (1, 3): ("rest03", 1)}
+REST_TAG = {(0, 0): ("x1_80", 3), (0, 3): ("rest03", 1), (1, 0): ("x1_80", 3), (1, 3): ("rest03", 1)}
 Y_LOADS = ((0, 0, 2), (0, 2, 4), (1, 0, 4))
 ORD0 = (("u", 0), ("u", 1), ("u", 2), ("g", 0), ("g", 1), ("u", 3), ("g", 2), ("g", 3))
 US = ()
 G02 = "v"
 G12 = "v"
 WARM_A = 0
-WARM_B = 2
+WARM_B = 3
 
 
 def tile_attend_gnce_w_kernel(tc, xT, wT, y, wt, xm, offs, out):
@@ -144,8 +144,8 @@ def tile_attend_gnce_w_kernel(tc, xT, wT, y, wt, xm, offs, out):
             for s in range(first, end):
                 y_raw.update({(c, t, s): part[:, t - lo, (s - first) * P :] for t in range(lo, hi)})
 
-        def load_m(lo, hi):
-            for c in range(CHUNKS):
+        def load_m(lo, hi, chunks=range(CHUNKS)):
+            for c in chunks:
                 part = load(f"m_part{c}{lo}", m_rows[c, :, :, lo * P : hi * P])
                 m_raw.update({(b, c): part[:, :, (b - lo) * P : (b - lo + 1) * P] for b in range(lo, hi)})
 
@@ -153,8 +153,9 @@ def tile_attend_gnce_w_kernel(tc, xT, wT, y, wt, xm, offs, out):
         load_y("y02", 0, 2, PACK, 0, BLOCKS)
         for s in (2, 3):
             load_y(f"y1_turned{s}", 1, 0, PACK, s, s + 1)
-        load_m(0, 1)
+        load_m(0, 1, (0,))
         load_y("y1_direct", 1, 0, PACK, 0, 2)
+        load_m(0, 1, (1,))
         load_m(1, 2)
         load_m(2, 4)
 
@@ -217,10 +218,6 @@ def tile_attend_gnce_w_kernel(tc, xT, wT, y, wt, xm, offs, out):
         }
 
         def g_laid(c, lo, hi):
-            if (c, lo) == (0, 3):
-                if "words" not in g_half:
-                    g_half["words"] = keep.tile([P, P, PACK], BF16, name="g_words", tag="m_part00", align_bytes=DMA_ALIGN)
-                return g_half["words"][:]
             if (c, lo) == (1, 0):
                 if "last" not in g_half:
                     g_half["last"] = keep.tile([P, P, PACK], BF16, name="g_last", tag="g_turned13", align_bytes=DMA_ALIGN)
@@ -424,10 +421,9 @@ def tile_attend_gnce_w_kernel(tc, xT, wT, y, wt, xm, offs, out):
             warm_up(sums[1, last])
         lay_g(1, 0, 1)
         quantise_g(0, 0, 2)
-        quantise_g(0, 2, 3)
+        quantise_g(0, 2, 4)
         lay_g(1, 1, 2, nc.vector)
 
-        quantise_g(0, 3, 4)
         quantise_m(0, 0)
         product(0, 0)
         quantise_g(1, 2, 4)
@@ -437,10 +433,10 @@ def tile_attend_gnce_w_kernel(tc, xT, wT, y, wt, xm, offs, out):
         product(0, 1)
         output_block(0)
 
-        behind_g = m_tile("m_behind_g", "g_turned13", pieces=3)
+        behind_g = m_tile("m_behind_g", "g_turned13", pieces=2)
         for c in range(CHUNKS):
             lay_m(nc.vector, 1, c, behind_g[:, c])
-        lay_m(nc.scalar, 2, 0, behind_g[:, 2])
+        lay_m(nc.scalar, 2, 0, m_tile("m_bf20", "m_part10")[:, 0])
         for b, c in ((1, 0), (2, 0), (1, 1)):
             quantise_m(b, c)
         for c in range(CHUNKS):

@@ -399,12 +399,8 @@ def tile_attend_gnce_w_kernel(tc, xT, wT, y, wt, xm, offs, out):
 
         for t in range(PACK):
             weigh_targets(1, t)
-        for s in (2, 3):
-            turn(1, s, "y", range(PACK))
-            turn(1, s, "s", (0, 1))
-        for t in (2, 3):
-            for s in (2, 3):
-                turn(1, s, "s", (t,))
+        for s, what, places in ((2, "y", range(PACK)), (2, "s", (0, 1)), (3, "y", range(PACK)), (2, "s", (2, 3)), (3, "s", range(PACK))):
+            turn(1, s, what, places)
         for s in (2, 3):
             gradient_turned(1, s)
         for t in range(PACK):

@@ -26,32 +26,8 @@ MX_ALIGN = 64
 DMA_ALIGN = 256
 
 DIRECT = (3, 2)
-SUM_BANK = {(0, 3): 3, (1, 2): 5, (1, 3): 1}
-WORD_BANK = {(0, 3): 5, (1, 2): 6, (1, 3): 0}
-ACC_BANK = (2, 7, 4, 3)
-SCORES0 = ((0, 4, 0, 256), (0, 0, 256, 512), (1, 5, 0, 256), (1, 1, 256, 512), (2, 2, 0, 512), (3, 3, 0, 512))
-TURN1 = (("s", (0,)), ("s", (1,)), ("y", (0, 1, 2, 3)), ("s", (2,)), ("s", (3,)))
-M_TAG = {(0, 0): "rest03", (0, 1): "g_turned12"}
-M01 = "s"
-G_TAG = ("x1_80", "g_codes1")
-M01_TAG = "g_rows10"
 X_SHARES = (80, 64)
-TABLE_LOADS = ((0, 1), (1, 2), (2, 3), (3, 4))
-X_LOADS = (((0, 128),), ((0, 80), (80, 128)))
-X_LAY = (
-    (("v", 0, 0, 80, 0, 2), ("s", 0, 80, 128, 0, 2), ("v", 0, 0, 64, 2, 4), ("s", 0, 64, 128, 2, 4)),
-    (("v", 0, 0, 80, 0, 4), ("v", 80, 80, 128, 0, 2), ("v", 80, 80, 128, 2, 4)),
-)
-PRE = 2
-XQ1 = ((0, 128),)
-REST_TAG = {(0, 0): ("x1_80", 3), (0, 3): ("rest03", 1), (1, 0): ("x1_80", 3), (1, 3): ("rest03", 1)}
-Y_LOADS = ((0, 0, 2), (0, 2, 4), (1, 0, 4))
-ORD0 = (("u", 0), ("u", 1), ("u", 2), ("g", 0), ("g", 1), ("u", 3), ("g", 2), ("g", 3))
-US = ()
-G02 = "v"
-G12 = "v"
-WARM_A = 0
-WARM_B = 3
+EARLY = 80
 
 
 def tile_attend_gnce_w_kernel(tc, xT, wT, y, wt, xm, offs, out):
@@ -109,7 +85,7 @@ def tile_attend_gnce_w_kernel(tc, xT, wT, y, wt, xm, offs, out):
             func=ACT.Copy,
             scale=-1.0,
         )
-        minus_row = [keep.tile([P, 2 * P, 2], F32, name=f"minus_row{c}", tag=f"minus_row{c}", align_bytes=DMA_ALIGN) for c in range(CHUNKS)]
+        minus_row = [keep.tile([P, 2 * P, 2], F32, name=f"minus_row{c}", align_bytes=DMA_ALIGN) for c in range(CHUNKS)]
         for c in range(CHUNKS):
             bank = new_bank(5 + c)
             for t in range(PACK):
@@ -127,37 +103,34 @@ def tile_attend_gnce_w_kernel(tc, xT, wT, y, wt, xm, offs, out):
         y_rows = y[0].rearrange("(c p t) i -> c p t i", c=CHUNKS, t=PACK)
         m_rows = xm[0].rearrange("(c p t) d -> c p t d", c=CHUNKS, t=PACK)
 
-        table = []
-        for lo, hi in TABLE_LOADS:
-            planes = load(f"table{lo}", w_rows[:, lo:hi, :])
-            table.extend(planes[:, t, :] for t in range(hi - lo))
-            if lo == 0:
-                nc.sync.dma_start(offsets[:], offs)
-        x_raw = {}
-        for c in range(CHUNKS):
-            for lo, hi in X_LOADS[c]:
-                x_raw[c, lo] = load(f"x{c}_{lo}", x_rows[:, :, c * K_PASS + PACK * lo : c * K_PASS + PACK * hi])
+        table = [load("table0", w_rows[:, 0, :])]
+        nc.sync.dma_start(offsets[:], offs)
+        table.extend(load(f"table{t}", w_rows[:, t, :]) for t in range(1, PACK))
+        x_first = load("x_first", x_rows[:, :, 0:K_PASS])
+        x_early = load("x_early", x_rows[:, :, K_PASS : K_PASS + PACK * EARLY])
+        x_late = load("x_late", x_rows[:, :, K_PASS + PACK * EARLY : R])
         y_raw, m_raw = {}, {}
 
-        def load_y(name, c, lo, hi, first, end):
-            part = load(name, y_rows[c, :, lo:hi, first * P : end * P])
-            for s in range(first, end):
-                y_raw.update({(c, t, s): part[:, t - lo, (s - first) * P :] for t in range(lo, hi)})
+        def load_y(name, c, places, blocks):
+            part = load(name, y_rows[c, :, places.start : places.stop, blocks.start * P : blocks.stop * P])
+            for t in places:
+                y_raw.update({(c, t, s): part[:, t - places.start, (s - blocks.start) * P :] for s in blocks})
 
-        def load_m(lo, hi, chunks=range(CHUNKS)):
-            for c in chunks:
-                part = load(f"m_part{c}{lo}", m_rows[c, :, :, lo * P : hi * P])
-                m_raw.update({(b, c): part[:, :, (b - lo) * P : (b - lo + 1) * P] for b in range(lo, hi)})
+        def load_m(c, blocks):
+            part = load(f"m_part{c}{blocks.start}", m_rows[c, :, :, blocks.start * P : blocks.stop * P])
+            for b in blocks:
+                m_raw[b, c] = part[:, :, (b - blocks.start) * P : (b - blocks.start + 1) * P]
 
-        load_y("y00", 0, 0, 2, 0, BLOCKS)
-        load_y("y02", 0, 2, PACK, 0, BLOCKS)
-        for s in (2, 3):
-            load_y(f"y1_turned{s}", 1, 0, PACK, s, s + 1)
-        load_m(0, 1, (0,))
-        load_y("y1_direct", 1, 0, PACK, 0, 2)
-        load_m(0, 1, (1,))
-        load_m(1, 2)
-        load_m(2, 4)
+        for u in range(2):
+            load_y(f"y0_pair{u}", 0, range(2 * u, 2 * u + 2), range(BLOCKS))
+        for s in range(DIRECT[1], BLOCKS):
+            load_y(f"y1_turned{s}", 1, range(PACK), range(s, s + 1))
+        load_m(0, range(1))
+        load_y("y1_direct", 1, range(PACK), range(DIRECT[1]))
+        load_m(1, range(1))
+        for blocks in (range(1, 2), range(2, D // P)):
+            for c in range(CHUNKS):
+                load_m(c, blocks)
 
         window = [keep.tile([P, T], F32, name=f"window{b}", align_bytes=DMA_ALIGN) for b in range(D // P)]
         for b in range(D // P):
@@ -167,15 +140,15 @@ def tile_attend_gnce_w_kernel(tc, xT, wT, y, wt, xm, offs, out):
         w_codes = keep.tile([P, N], U32, name="w_codes", align_bytes=MX_ALIGN)
         w_scales = keep.tile([P, N], U8, name="w_scales", align_bytes=MX_ALIGN)
         for t in range(PACK - 1):
-            nc.vector.tensor_copy(out=w_bf[:, :, t], in_=table[t].indirect(offsets[:]))
+            nc.vector.tensor_copy(out=w_bf[:, :, t], in_=table[t][:].indirect(offsets[:]))
         slot_halves = [slice(h * HALF, (h + 1) * HALF) for h in range(2)]
         for h, cols in enumerate(slot_halves):
             half_list = offsets[:, h * HALF // 16 : (h + 1) * HALF // 16]
-            nc.vector.tensor_copy(out=w_bf[:, cols, PACK - 1], in_=table[PACK - 1].indirect(half_list))
+            nc.vector.tensor_copy(out=w_bf[:, cols, PACK - 1], in_=table[PACK - 1][:].indirect(half_list))
         for cols in slot_halves:
             quantise(w_codes[:, cols], w_scales[:, cols], w_bf[:, cols, :].rearrange("p n t -> p (n t)"), E4M3)
 
-        x_bf = [keep.tile([P, PACK, P, PACK], BF16, name=f"x_bf{c}", tag=f"x_bf{c}", align_bytes=DMA_ALIGN) for c in range(CHUNKS)]
+        x_bf = [keep.tile([P, PACK, P, PACK], BF16, name=f"x_bf{c}", align_bytes=DMA_ALIGN) for c in range(CHUNKS)]
         x_codes = [keep.tile([P, K_PASS], U32, name=f"x_codes{c}", align_bytes=MX_ALIGN) for c in range(CHUNKS)]
         x_scales = [keep.tile([P, K_PASS], U8, name=f"x_scales{c}", align_bytes=MX_ALIGN) for c in range(CHUNKS)]
 
@@ -209,76 +182,72 @@ def tile_attend_gnce_w_kernel(tc, xT, wT, y, wt, xm, offs, out):
         def warm_up(bank):
             score_pass(bank[:], 0, 0, slice(0, N))
 
-        g_codes = {}
+        g_codes, g_laid = {}, {}
         g_scales = [keep.tile([P, N], U8, name=f"g_scales{c}", align_bytes=MX_ALIGN) for c in range(CHUNKS)]
-        g_half = {
-            (c, h): keep.tile([P, HALF, PACK], BF16, name=f"g_half{c}{h}", tag="m_part10" if (c, h) == (1, 1) else f"g_half{c}{h}", align_bytes=DMA_ALIGN)
-            for c in range(CHUNKS)
-            for h in range(2)
+        g_runs = {
+            (0, 0): (2, "g00"),
+            (0, 2): (BLOCKS, "g02"),
+            (1, 0): (1, "g_turned13"),
+            (1, 1): (2, "g11"),
+            (1, 2): (BLOCKS, "m_part10"),
         }
 
-        def g_laid(c, lo, hi):
-            if (c, lo) == (1, 0):
-                if "last" not in g_half:
-                    g_half["last"] = keep.tile([P, P, PACK], BF16, name="g_last", tag="g_turned13", align_bytes=DMA_ALIGN)
-                return g_half["last"][:]
-            return g_half[c, lo // 2][:, (lo % 2) * P : (lo % 2 + hi - lo) * P, :]
-
-        def quantise_g(c, lo, hi):
-            cols = slice(lo * P, hi * P)
-            if c not in g_codes:
-                g_codes[c] = keep.tile([P, N], U32, name=f"g_codes{c}", tag=G_TAG[c], align_bytes=DMA_ALIGN)
-            quantise(g_codes[c][:, cols], g_scales[c][:, cols], g_laid(c, lo, hi).rearrange("p n t -> p (n t)"), E5M2)
-
-        rest = {}
-        g_rows = {
-            (c, lo): keep.tile([P, PACK, (hi - lo) * P], BF16, name=f"g_rows{c}{lo}", tag=f"g_rows{c}{lo}", align_bytes=DMA_ALIGN)
-            for c, lo, hi in ((0, 0, 3), (1, 0, 2))
-        }
-
-        def weigh_targets(c, t):
-            if (c, t) in REST_TAG:
-                tag, places = REST_TAG[c, t]
-                part = keep.tile([P, places, DIRECT[c] * P], F32, name=f"rest{c}{t}", tag=tag, align_bytes=DMA_ALIGN)
-                rest.update({(c, t + k): part[:, k, :] for k in range(places)})
-            if (c, t) in US:
-                nc.scalar.activation(
-                    out=rest[c, t],
-                    in_=sig[c][:, t, 0 : DIRECT[c] * P],
-                    func=ACT.Identity,
-                    scale=minus_col[:, c, t, 0:1],
-                    bias=weight[:, c, t : t + 1],
+        def laid_blocks(c, lo, hi):
+            first = max(start for chunk, start in g_runs if chunk == c and start <= lo)
+            if (c, first) not in g_laid:
+                end, tag = g_runs[c, first]
+                g_laid[c, first] = keep.tile(
+                    [P, (end - first) * P, PACK], BF16, name=f"g_laid{c}{first}", tag=tag, align_bytes=DMA_ALIGN
                 )
-                return
-            nc.vector.tensor_scalar(
-                out=rest[c, t],
-                in0=sig[c][:, t, 0 : DIRECT[c] * P],
-                scalar1=minus_col[:, c, t, 0:1],
-                scalar2=weight[:, c, t : t + 1],
-                op0=ALU.mult,
-                op1=ALU.add,
-            )
+            return g_laid[c, first][:, (lo - first) * P : (hi - first) * P, :]
 
-        def gradient(c, t, lo, hi):
-            cols = slice(lo * P, hi * P)
+        def quantise_g(c, first):
+            end = g_runs[c, first][0]
+            if c not in g_codes:
+                tag = ("x_late", "g_codes1")[c]
+                g_codes[c] = keep.tile([P, N], U32, name=f"g_codes{c}", tag=tag, align_bytes=DMA_ALIGN)
+            cols = slice(first * P, end * P)
+            quantise(g_codes[c][:, cols], g_scales[c][:, cols], g_laid[c, first][:].rearrange("p n t -> p (n t)"), E5M2)
+
+        weighted = {}
+        g_rows = [
+            keep.tile([P, PACK, DIRECT[c] * P], BF16, name=f"g_rows{c}", align_bytes=DMA_ALIGN) for c in range(CHUNKS)
+        ]
+
+        def weigh(c, places, tag):
+            shape = [P, len(places), DIRECT[c] * P]
+            part = keep.tile(shape, F32, name=f"weighted{c}{places.start}", tag=tag, align_bytes=DMA_ALIGN)
+            for t in places:
+                weighted[c, t] = part[:, t - places.start, :]
+                nc.vector.tensor_scalar(
+                    out=weighted[c, t],
+                    in0=sig[c][:, t, 0 : DIRECT[c] * P],
+                    scalar1=minus_col[:, c, t, 0:1],
+                    scalar2=weight[:, c, t : t + 1],
+                    op0=ALU.mult,
+                    op1=ALU.add,
+                )
+
+        def gradient(c, t):
             nc.vector.scalar_tensor_tensor(
-                out=g_rows[c, lo][:, t, :],
-                in0=y_raw[c, t, lo][:, 0 : (hi - lo) * P],
+                out=g_rows[c][:, t, :],
+                in0=y_raw[c, t, 0][:, 0 : DIRECT[c] * P],
                 scalar=minus_col[:, c, t, 0:1],
-                in1=rest[c, t][:, cols],
+                in1=weighted[c, t],
                 op0=ALU.mult,
                 op1=ALU.add,
             )
 
-        def lay_g(c, lo, hi, engine=nc.scalar, part=slice(0, None)):
-            rows = g_rows[c, 0][:, :, lo * P : hi * P]
-            side_by_side(engine, g_laid(c, lo, hi)[:, part, :], rows[:, :, part])
+        def lay_g(engine, c, lo, hi):
+            side_by_side(engine, laid_blocks(c, lo, hi), g_rows[c][:, :, lo * P : hi * P])
 
+        sum_bank = {(0, 3): 3, (1, 2): 5, (1, 3): 1}
+        word_bank = {(0, 3): 5, (1, 2): 6, (1, 3): 0}
         sums, turned, g_turned = {}, {}, {}
 
         def turn(c, s, what, places):
             if (c, s) not in sums:
-                sums[c, s] = new_bank(SUM_BANK[c, s])
+                sums[c, s] = new_bank(sum_bank[c, s])
                 turned[c, s] = 0
             for t in places:
                 src = sig[c][:, t, s * P :] if what == "s" else y_raw[c, t, s]
@@ -307,15 +276,14 @@ def tile_attend_gnce_w_kernel(tc, xT, wT, y, wt, xm, offs, out):
 
         def turn_back(c, s):
             words = g_turned[c, s][:].rearrange("p w e -> p (w e)").bitcast(F32)
-            whole = new_bank(WORD_BANK[c, s])
-            bank = whole[:, 0 : 2 * P].rearrange("p (u n) -> p u n", u=2)
+            bank = new_bank(word_bank[c, s])[:, 0 : 2 * P].rearrange("p (u n) -> p u n", u=2)
             for u in range(2):
                 nc.tensor.transpose(bank[:, u, :], words[:, u * P : (u + 1) * P], identity[:])
-            dst = g_laid(c, s, s + 1).rearrange("p n t -> p (n t)").bitcast(F32)
+            dst = laid_blocks(c, s, s + 1).rearrange("p n t -> p (n t)").bitcast(F32)
             nc.scalar.copy(out=dst.rearrange("p (n u) -> p n u", u=2), in_=bank.rearrange("p u n -> p n u"))
-            return whole
 
         m_bf, m_codes, m_scales, acc = {}, {}, {}, {}
+        acc_bank = (2, 7, 4, 3)
 
         def lay_m(engine, b, c, dst):
             m_bf[b, c] = dst
@@ -325,18 +293,15 @@ def tile_attend_gnce_w_kernel(tc, xT, wT, y, wt, xm, offs, out):
             return keep.tile([P, pieces, P, PACK], BF16, name=name, tag=tag, align_bytes=DMA_ALIGN)
 
         def quantise_m(b, c):
-            if b == 0:
-                if "first" not in m_codes:
-                    m_codes["first"] = keep.tile([P, CHUNKS, P], U32, name="m_codes0", tag="rest03", align_bytes=DMA_ALIGN)
-                m_codes[b, c] = m_codes["first"][:, c]
-            else:
-                m_codes[b, c] = keep.tile([P, P], U32, name=f"m_codes{b}{c}", tag=f"m_codes{b}{c}", align_bytes=DMA_ALIGN)[:]
+            if (b, c) not in m_codes:
+                name = f"m_codes{b}{c}"
+                m_codes[b, c] = keep.tile([P, P], U32, name=name, tag=name, align_bytes=DMA_ALIGN)[:]
             m_scales[b, c] = keep.tile([P, P], U8, name=f"m_scales{b}{c}", align_bytes=MX_ALIGN)
             quantise(m_codes[b, c], m_scales[b, c][:], m_bf[b, c].rearrange("p n t -> p (n t)"), E4M3)
 
         def product(b, c):
             if b not in acc:
-                acc[b] = new_bank(ACC_BANK[b])
+                acc[b] = new_bank(acc_bank[b])
             nc.tensor.matmul_mx(
                 out=acc[b][:],
                 lhsT=m_codes[b, c].bitcast(E4M3),
@@ -348,88 +313,80 @@ def tile_attend_gnce_w_kernel(tc, xT, wT, y, wt, xm, offs, out):
             )
 
         def output_block(b):
-            dense = keep.tile([P, N], F32, name=f"dense{b}", tag=f"dense{b}", align_bytes=MX_ALIGN)
+            dense = keep.tile([P, N], F32, name=f"dense{b}", align_bytes=MX_ALIGN)
             nc.scalar.copy(out=dense[:], in_=acc[b][:])
             nc.vector.tensor_copy(out=window[b][:].indirect(offsets[:]), in_=dense[:])
             nc.sync.dma_start(out=out[b * P : (b + 1) * P, :], in_=window[b][:])
 
         pairs = (slice(0, 2), slice(2, PACK))
-        engines = {"v": nc.vector, "s": nc.scalar}
-        for k in range(PRE):
-            spare = new_bank(7)
-            nc.tensor.matmul_mx(
-                out=spare[:, 0:HALF],
-                lhsT=w_codes[:, 0:P].bitcast(E4M3),
-                lhsT_scale=w_scales[:, 0:P],
-                rhs=w_codes[:, 0:HALF].bitcast(E4M3),
-                rhs_scale=w_scales[:, 0:HALF],
-                start=True,
-                stop=True,
-            )
-        for e, first, lo, hi, a, z in X_LAY[0]:
-            lay_x(engines[e], 0, x_raw[0, first], first, lo, hi, slice(a, z))
+        for places, share in zip(pairs, X_SHARES):
+            lay_x(nc.vector, 0, x_first, 0, 0, share, places)
+            lay_x(nc.scalar, 0, x_first, 0, share, P, places)
         for lo, hi in ((0, 1), (1, 2), (2, PACK)):
             quantise_x(0, lo, hi)
-        for t, k, lo, hi in SCORES0:
-            scores(0, t, k, slice(lo, hi))
+        for t in range(2):
+            for cols, bank in zip(slot_halves, (PACK + t, t)):
+                scores(0, t, bank, cols)
+        for t in range(2, PACK):
+            scores(0, t, t)
 
-        for e, first, lo, hi, a, z in X_LAY[1]:
-            lay_x(engines[e], 1, x_raw[1, first], first, lo, hi, slice(a, z))
-        for lo, hi in XQ1:
-            if hi - lo == P:
-                for places in pairs:
-                    quantise_x(1, places.start, places.stop)
-            else:
-                for t in range(PACK):
-                    cols = slice(t * P + lo, t * P + hi)
-                    laid = x_bf[1][:, t, lo:hi, :].rearrange("p m j -> p (m j)")
-                    quantise(x_codes[1][:, cols], x_scales[1][:, cols], laid, E4M3)
-        for t, k in enumerate((6, 7, 4, 0)):
-            scores(1, t, k)
+        lay_x(nc.vector, 1, x_early, 0, 0, EARLY, slice(0, PACK))
+        for places in pairs:
+            lay_x(nc.vector, 1, x_late, EARLY, EARLY, P, places)
+        for places in pairs:
+            quantise_x(1, places.start, places.stop)
+        for t, bank in enumerate((6, 7, 4, 0)):
+            scores(1, t, bank)
 
         last = BLOCKS - 1
-        for kind, t in ORD0:
-            if kind == "u":
-                weigh_targets(0, t)
-            else:
-                gradient(0, t, 0, last)
-        for what, places in (("y", (2, 3, 0, 1)), ("s", (0, 1, 2, 3))):
-            turn(0, last, what, places)
+        weigh(0, range(3), "x_late")
+        for t in range(2):
+            gradient(0, t)
+        weigh(0, range(3, PACK), "last_place")
+        for t in range(2, PACK):
+            gradient(0, t)
+        turn(0, last, "y", (2, 3, 0, 1))
+        turn(0, last, "s", range(PACK))
         gradient_turned(0, last)
 
-        for t in range(PACK):
-            weigh_targets(1, t)
-        for s, what, places in ((2, "y", range(PACK)), (2, "s", (0, 1)), (3, "y", range(PACK)), (2, "s", (2, 3)), (3, "s", range(PACK))):
-            turn(1, s, what, places)
-        for s in (2, 3):
+        weigh(1, range(3), "x_late")
+        weigh(1, range(3, PACK), "last_place")
+        turn(1, 2, "y", range(PACK))
+        turn(1, 2, "s", range(2))
+        turn(1, last, "y", range(PACK))
+        turn(1, 2, "s", range(2, PACK))
+        turn(1, last, "s", range(PACK))
+        for s in (2, last):
             gradient_turned(1, s)
         for t in range(PACK):
-            gradient(1, t, 0, 2)
+            gradient(1, t)
 
-        lay_g(0, 0, 2)
-        lay_g(0, 2, last)
+        lay_g(nc.scalar, 0, 0, 2)
+        lay_g(nc.scalar, 0, 2, last)
         lay_m(nc.scalar, 0, 0, m_tile("m_bf00", "m_bf00")[:, 0])
         turn_back(0, last)
         lay_m(nc.scalar, 0, 1, m_tile("m_bf01", "m_bf01")[:, 0])
-        for s in (2, 3):
+        for s in (2, last):
             turn_back(1, s)
-        for h in range(WARM_B):
+        for _ in range(2):
             warm_up(sums[1, last])
-        lay_g(1, 0, 1)
-        quantise_g(0, 0, 2)
-        quantise_g(0, 2, 4)
-        lay_g(1, 1, 2, nc.vector)
+        lay_g(nc.scalar, 1, 0, 1)
+        quantise_g(0, 0)
+        quantise_g(0, 2)
+        lay_g(nc.vector, 1, 1, 2)
 
+        first_codes = keep.tile([P, CHUNKS, P], U32, name="m_codes0", tag="last_place", align_bytes=DMA_ALIGN)
+        m_codes.update({(0, c): first_codes[:, c] for c in range(CHUNKS)})
         quantise_m(0, 0)
         product(0, 0)
-        quantise_g(1, 2, 4)
+        quantise_g(1, 2)
         quantise_m(0, 1)
-        quantise_g(1, 1, 2)
-        quantise_g(1, 0, 1)
+        quantise_g(1, 1)
+        quantise_g(1, 0)
         product(0, 1)
         output_block(0)
 
-        behind_g = m_tile("m_behind_g", "g_turned13", pieces=2)
+        behind_g = m_tile("m_bf1", "g_turned13", pieces=CHUNKS)
         for c in range(CHUNKS):
             lay_m(nc.vector, 1, c, behind_g[:, c])
         lay_m(nc.scalar, 2, 0, m_tile("m_bf20", "m_part10")[:, 0])
@@ -442,9 +399,9 @@ def tile_attend_gnce_w_kernel(tc, xT, wT, y, wt, xm, offs, out):
         output_block(1)
         for c in range(CHUNKS):
             product(2, c)
-        third = m_tile("m_bf3", "m_codes11", pieces=CHUNKS)
+        behind_first = m_tile("m_bf3", "m_codes11", pieces=CHUNKS)
         for c in range(CHUNKS):
-            lay_m(nc.scalar, 3, c, third[:, c])
+            lay_m(nc.scalar, 3, c, behind_first[:, c])
         for c in range(CHUNKS):
             quantise_m(3, c)
         output_block(2)

@@ -27,7 +27,7 @@ DMA_ALIGN = 256
 
 DIRECT = (3, 2)
 X_SHARES = (80, 64)
-EARLY = 80
+EARLY = 64
 
 
 def tile_attend_gnce_w_kernel(tc, xT, wT, y, wt, xm, offs, out):

@@ -125,9 +125,9 @@ def tile_attend_gnce_w_kernel(tc, xT, wT, y, wt, xm, offs, out):
             load_y(f"y0_pair{u}", 0, range(2 * u, 2 * u + 2), range(BLOCKS))
         for s in range(DIRECT[1], BLOCKS):
             load_y(f"y1_turned{s}", 1, range(PACK), range(s, s + 1))
-        load_m(0, range(1))
+        for c in range(CHUNKS):
+            load_m(c, range(1))
         load_y("y1_direct", 1, range(PACK), range(DIRECT[1]))
-        load_m(1, range(1))
         for blocks in (range(1, 2), range(2, D // P)):
             for c in range(CHUNKS):
                 load_m(c, blocks)
@@ -182,14 +182,21 @@ def tile_attend_gnce_w_kernel(tc, xT, wT, y, wt, xm, offs, out):
         def warm_up(bank):
             score_pass(bank[:], 0, 0, slice(0, N))
 
-        g_codes, g_laid = {}, {}
-        g_scales = [keep.tile([P, N], U8, name=f"g_scales{c}", align_bytes=MX_ALIGN) for c in range(CHUNKS)]
+        g_laid, g_scales = {}, []
+        g_start = (0, N + HALF)
+        g_width = CHUNKS * (N + HALF)
+
+        def padding(plane):
+            return plane.rearrange("p (c w) -> p c w", c=CHUNKS)[:, :, plane.shape[1] // 3 :]
+
+        g_codes = keep.tile([P, g_width], U32, name="g_codes", align_bytes=DMA_ALIGN)
+        nc.gpsimd.memset(padding(g_codes[:]), 0)
         g_runs = {
             (0, 0): (2, "g00"),
             (0, 2): (BLOCKS, "g02"),
             (1, 0): (1, "g_turned13"),
             (1, 1): (2, "g11"),
-            (1, 2): (BLOCKS, "m_part10"),
+            (1, 2): (BLOCKS, "g12"),
         }
 
         def laid_blocks(c, lo, hi):
@@ -203,11 +210,11 @@ def tile_attend_gnce_w_kernel(tc, xT, wT, y, wt, xm, offs, out):
 
         def quantise_g(c, first):
             end = g_runs[c, first][0]
-            if c not in g_codes:
-                tag = ("x_late", "g_codes1")[c]
-                g_codes[c] = keep.tile([P, N], U32, name=f"g_codes{c}", tag=tag, align_bytes=DMA_ALIGN)
-            cols = slice(first * P, end * P)
-            quantise(g_codes[c][:, cols], g_scales[c][:, cols], g_laid[c, first][:].rearrange("p n t -> p (n t)"), E5M2)
+            if not g_scales:
+                g_scales.append(keep.tile([P, g_width], U8, name="g_scales", tag="x_late", align_bytes=DMA_ALIGN))
+                nc.gpsimd.memset(padding(g_scales[0][:].bitcast(U32)), 0)
+            cols = slice(g_start[c] + first * P, g_start[c] + end * P)
+            quantise(g_codes[:, cols], g_scales[0][:, cols], g_laid[c, first][:].rearrange("p n t -> p (n t)"), E5M2)
 
         weighted = {}
         g_rows = [
@@ -299,24 +306,39 @@ def tile_attend_gnce_w_kernel(tc, xT, wT, y, wt, xm, offs, out):
             m_scales[b, c] = keep.tile([P, P], U8, name=f"m_scales{b}{c}", align_bytes=MX_ALIGN)
             quantise(m_codes[b, c], m_scales[b, c][:], m_bf[b, c].rearrange("p n t -> p (n t)"), E4M3)
 
-        def product(b, c):
-            if b not in acc:
-                acc[b] = new_bank(acc_bank[b])
+        def product(b, c, first=0):
+            opens = (b, first) not in acc
+            if opens:
+                acc[b, first] = new_bank(acc_bank[-1] if first else acc_bank[b])
+            cols = slice(g_start[c] + first, g_start[c] + first + N)
             nc.tensor.matmul_mx(
-                out=acc[b][:],
+                out=acc[b, first][:],
                 lhsT=m_codes[b, c].bitcast(E4M3),
                 lhsT_scale=m_scales[b, c][:],
-                rhs=g_codes[c][:].bitcast(E5M2),
-                rhs_scale=g_scales[c][:],
-                start=(c == 0),
-                stop=(c == CHUNKS - 1),
+                rhs=g_codes[:, cols].bitcast(E5M2),
+                rhs_scale=g_scales[0][:, cols],
+                start=opens,
+                stop=not opens,
             )
 
-        def output_block(b):
-            dense = keep.tile([P, N], F32, name=f"dense{b}", align_bytes=MX_ALIGN)
-            nc.scalar.copy(out=dense[:], in_=acc[b][:])
-            nc.vector.tensor_copy(out=window[b][:].indirect(offsets[:]), in_=dense[:])
+        dense = {}
+
+        def copy_out(b, first=0, width=N):
+            name = f"dense{b}_{first}"
+            dense[b, first] = keep.tile([P, width], F32, name=name, tag=name, align_bytes=DMA_ALIGN)
+            nc.scalar.copy(out=dense[b, first][:], in_=acc[b, first][:, 0:width])
+
+        def scatter(b, first=0, width=N):
+            listed = offsets[:, first // 16 : (first + width) // 16]
+            nc.vector.tensor_copy(out=window[b][:].indirect(listed), in_=dense[b, first][:])
+
+        def store(b):
             nc.sync.dma_start(out=out[b * P : (b + 1) * P, :], in_=window[b][:])
+
+        def output_block(b):
+            copy_out(b)
+            scatter(b)
+            store(b)
 
         pairs = (slice(0, 2), slice(2, PACK))
         for places, share in zip(pairs, X_SHARES):
@@ -361,7 +383,6 @@ def tile_attend_gnce_w_kernel(tc, xT, wT, y, wt, xm, offs, out):
         for t in range(PACK):
             gradient(1, t)
 
-        lay_g(nc.scalar, 0, 0, 2)
         lay_g(nc.scalar, 0, 2, last)
         lay_m(nc.scalar, 0, 0, m_tile("m_bf00", "m_bf00")[:, 0])
         turn_back(0, last)
@@ -370,38 +391,45 @@ def tile_attend_gnce_w_kernel(tc, xT, wT, y, wt, xm, offs, out):
             turn_back(1, s)
         for _ in range(2):
             warm_up(sums[1, last])
+        for s in range(2):
+            lay_g(nc.scalar, 0, s, s + 1)
         lay_g(nc.scalar, 1, 0, 1)
-        quantise_g(0, 0)
         quantise_g(0, 2)
-        lay_g(nc.vector, 1, 1, 2)
 
         first_codes = keep.tile([P, CHUNKS, P], U32, name="m_codes0", tag="last_place", align_bytes=DMA_ALIGN)
         m_codes.update({(0, c): first_codes[:, c] for c in range(CHUNKS)})
         quantise_m(0, 0)
-        product(0, 0)
-        quantise_g(1, 2)
+        product(0, 0, HALF)
         quantise_m(0, 1)
+        quantise_g(1, 2)
+        product(0, 1, HALF)
+        lay_g(nc.vector, 1, 1, 2)
+        quantise_g(0, 0)
+        product(0, 0)
         quantise_g(1, 1)
         quantise_g(1, 0)
         product(0, 1)
-        output_block(0)
-
-        behind_g = m_tile("m_bf1", "g_turned13", pieces=CHUNKS)
+        copy_out(0, HALF, HALF)
+        lay_m(nc.scalar, 1, 1, m_tile("m_bf11", "g_turned13")[:, 0])
+        lay_m(nc.vector, 1, 0, m_tile("m_bf10", "g11")[:, 0])
+        scatter(0, HALF, HALF)
+        copy_out(0, 0, HALF)
         for c in range(CHUNKS):
-            lay_m(nc.vector, 1, c, behind_g[:, c])
-        lay_m(nc.scalar, 2, 0, m_tile("m_bf20", "m_part10")[:, 0])
-        for b, c in ((1, 0), (2, 0), (1, 1)):
-            quantise_m(b, c)
+            quantise_m(1, c)
+        scatter(0, 0, HALF)
+        store(0)
+
         for c in range(CHUNKS):
             product(1, c)
-        lay_m(nc.scalar, 2, 1, m_tile("m_bf21", "m_codes10")[:, 0])
-        quantise_m(2, 1)
+        lay_m(nc.scalar, 2, 0, m_tile("m_bf20", "last_place")[:, 0])
+        lay_m(nc.vector, 2, 1, m_tile("m_bf21", "dense0_0")[:, 0])
+        for c in range(CHUNKS):
+            quantise_m(2, c)
         output_block(1)
         for c in range(CHUNKS):
             product(2, c)
-        behind_first = m_tile("m_bf3", "m_codes11", pieces=CHUNKS)
-        for c in range(CHUNKS):
-            lay_m(nc.scalar, 3, c, behind_first[:, c])
+        lay_m(nc.scalar, 3, 0, m_tile("m_bf30", "m_codes11")[:, 0])
+        lay_m(nc.vector, 3, 1, m_tile("m_bf31", "dense1_0")[:, 0])
         for c in range(CHUNKS):
             quantise_m(3, c)
         output_block(2)

@@ -125,9 +125,9 @@ def tile_attend_gnce_w_kernel(tc, xT, wT, y, wt, xm, offs, out):
             load_y(f"y0_pair{u}", 0, range(2 * u, 2 * u + 2), range(BLOCKS))
         for s in range(DIRECT[1], BLOCKS):
             load_y(f"y1_turned{s}", 1, range(PACK), range(s, s + 1))
-        for c in range(CHUNKS):
-            load_m(c, range(1))
+        load_m(0, range(1))
         load_y("y1_direct", 1, range(PACK), range(DIRECT[1]))
+        load_m(1, range(1))
         for blocks in (range(1, 2), range(2, D // P)):
             for c in range(CHUNKS):
                 load_m(c, blocks)
@@ -212,7 +212,7 @@ def tile_attend_gnce_w_kernel(tc, xT, wT, y, wt, xm, offs, out):
             end = g_runs[c, first][0]
             if not g_scales:
                 g_scales.append(keep.tile([P, g_width], U8, name="g_scales", tag="x_late", align_bytes=DMA_ALIGN))
-                nc.gpsimd.memset(padding(g_scales[0][:].bitcast(U32)), 0)
+                nc.vector.memset(padding(g_scales[0][:].bitcast(U32)), 0)
             cols = slice(g_start[c] + first * P, g_start[c] + end * P)
             quantise(g_codes[:, cols], g_scales[0][:, cols], g_laid[c, first][:].rearrange("p n t -> p (n t)"), E5M2)
 
@@ -248,8 +248,8 @@ def tile_attend_gnce_w_kernel(tc, xT, wT, y, wt, xm, offs, out):
         def lay_g(engine, c, lo, hi):
             side_by_side(engine, laid_blocks(c, lo, hi), g_rows[c][:, :, lo * P : hi * P])
 
-        sum_bank = {(0, 3): 3, (1, 2): 5, (1, 3): 1}
-        word_bank = {(0, 3): 5, (1, 2): 6, (1, 3): 0}
+        sum_bank = {(0, 3): 5, (1, 2): 4, (1, 3): 6}
+        word_bank = {(0, 3): 4, (1, 2): 0, (1, 3): 3}
         sums, turned, g_turned = {}, {}, {}
 
         def turn(c, s, what, places):
@@ -290,7 +290,7 @@ def tile_attend_gnce_w_kernel(tc, xT, wT, y, wt, xm, offs, out):
             nc.scalar.copy(out=dst.rearrange("p (n u) -> p n u", u=2), in_=bank.rearrange("p u n -> p n u"))
 
         m_bf, m_codes, m_scales, acc = {}, {}, {}, {}
-        acc_bank = (2, 7, 4, 3)
+        acc_bank = (7, 1, 2, 5)
 
         def lay_m(engine, b, c, dst):
             m_bf[b, c] = dst
@@ -346,18 +346,16 @@ def tile_attend_gnce_w_kernel(tc, xT, wT, y, wt, xm, offs, out):
             lay_x(nc.scalar, 0, x_first, 0, share, P, places)
         for lo, hi in ((0, 1), (1, 2), (2, PACK)):
             quantise_x(0, lo, hi)
-        for t in range(2):
-            for cols, bank in zip(slot_halves, (PACK + t, t)):
-                scores(0, t, bank, cols)
-        for t in range(2, PACK):
-            scores(0, t, t)
+        for t in range(PACK):
+            for h, cols in enumerate(slot_halves):
+                scores(0, t, 2 * t + h, cols)
 
         lay_x(nc.vector, 1, x_early, 0, 0, EARLY, slice(0, PACK))
         for places in pairs:
             lay_x(nc.vector, 1, x_late, EARLY, EARLY, P, places)
         for places in pairs:
             quantise_x(1, places.start, places.stop)
-        for t, bank in enumerate((6, 7, 4, 0)):
+        for t, bank in enumerate(range(PACK)):
             scores(1, t, bank)
 
         last = BLOCKS - 1
@@ -385,14 +383,13 @@ def tile_attend_gnce_w_kernel(tc, xT, wT, y, wt, xm, offs, out):
 
         lay_g(nc.scalar, 0, 2, last)
         lay_m(nc.scalar, 0, 0, m_tile("m_bf00", "m_bf00")[:, 0])
+        lay_g(nc.scalar, 0, 0, 2)
         turn_back(0, last)
         lay_m(nc.scalar, 0, 1, m_tile("m_bf01", "m_bf01")[:, 0])
         for s in (2, last):
             turn_back(1, s)
         for _ in range(2):
             warm_up(sums[1, last])
-        for s in range(2):
-            lay_g(nc.scalar, 0, s, s + 1)
         lay_g(nc.scalar, 1, 0, 1)
         quantise_g(0, 2)
 
@@ -400,18 +397,20 @@ def tile_attend_gnce_w_kernel(tc, xT, wT, y, wt, xm, offs, out):
         m_codes.update({(0, c): first_codes[:, c] for c in range(CHUNKS)})
         quantise_m(0, 0)
         product(0, 0, HALF)
+        lay_g(nc.vector, 1, 1, 2)
         quantise_m(0, 1)
         quantise_g(1, 2)
         product(0, 1, HALF)
-        lay_g(nc.vector, 1, 1, 2)
         quantise_g(0, 0)
         product(0, 0)
         quantise_g(1, 1)
         quantise_g(1, 0)
         product(0, 1)
         copy_out(0, HALF, HALF)
-        lay_m(nc.scalar, 1, 1, m_tile("m_bf11", "g_turned13")[:, 0])
-        lay_m(nc.vector, 1, 0, m_tile("m_bf10", "g11")[:, 0])
+        lay_m(nc.vector, 1, 0, m_tile("m_bf10", "g00")[:, 0])
+        m_bf[1, 1] = m_tile("m_bf11", "g_turned13")[:, 0]
+        for engine, cols in ((nc.scalar, slice(0, P // 2)), (nc.vector, slice(P // 2, P))):
+            side_by_side(engine, m_bf[1, 1][:, cols, :], m_raw[1, 1][:, :, cols])
         scatter(0, HALF, HALF)
         copy_out(0, 0, HALF)
         for c in range(CHUNKS):

@@ -27,7 +27,7 @@ DMA_ALIGN = 256
 
 DIRECT = (3, 2)
 X_SHARES = (80, 64)
-EARLY = 64
+EARLY = 80
 
 
 def tile_attend_gnce_w_kernel(tc, xT, wT, y, wt, xm, offs, out):
@@ -123,8 +123,7 @@ def tile_attend_gnce_w_kernel(tc, xT, wT, y, wt, xm, offs, out):
 
         for u in range(2):
             load_y(f"y0_pair{u}", 0, range(2 * u, 2 * u + 2), range(BLOCKS))
-        for s in range(DIRECT[1], BLOCKS):
-            load_y(f"y1_turned{s}", 1, range(PACK), range(s, s + 1))
+        load_y("y1_turned", 1, range(PACK), range(DIRECT[1], BLOCKS))
         load_m(0, range(1))
         load_y("y1_direct", 1, range(PACK), range(DIRECT[1]))
         load_m(1, range(1))
@@ -248,8 +247,8 @@ def tile_attend_gnce_w_kernel(tc, xT, wT, y, wt, xm, offs, out):
         def lay_g(engine, c, lo, hi):
             side_by_side(engine, laid_blocks(c, lo, hi), g_rows[c][:, :, lo * P : hi * P])
 
-        sum_bank = {(0, 3): 5, (1, 2): 4, (1, 3): 6}
-        word_bank = {(0, 3): 4, (1, 2): 0, (1, 3): 3}
+        sum_bank = {(0, 3): 5, (1, 2): 7, (1, 3): 6}
+        word_bank = {(0, 3): 7, (1, 2): 0, (1, 3): 3}
         sums, turned, g_turned = {}, {}, {}
 
         def turn(c, s, what, places):
@@ -353,10 +352,12 @@ def tile_attend_gnce_w_kernel(tc, xT, wT, y, wt, xm, offs, out):
         lay_x(nc.vector, 1, x_early, 0, 0, EARLY, slice(0, PACK))
         for places in pairs:
             lay_x(nc.vector, 1, x_late, EARLY, EARLY, P, places)
-        for places in pairs:
-            quantise_x(1, places.start, places.stop)
-        for t, bank in enumerate(range(PACK)):
-            scores(1, t, bank)
+        for lo, hi in ((0, 1), (1, 2), (2, PACK)):
+            quantise_x(1, lo, hi)
+        for h, cols in enumerate(slot_halves):
+            scores(1, 0, h, cols)
+        for t in range(1, PACK):
+            scores(1, t, t + 1)
 
         last = BLOCKS - 1
         weigh(0, range(3), "x_late")

@@ -210,7 +210,7 @@ def tile_attend_gnce_w_kernel(tc, xT, wT, y, wt, xm, offs, out):
         def quantise_g(c, first):
             end = g_runs[c, first][0]
             if not g_scales:
-                g_scales.append(keep.tile([P, g_width], U8, name="g_scales", tag="x_late", align_bytes=DMA_ALIGN))
+                g_scales.append(keep.tile([P, g_width], U8, name="g_scales", tag="last_place", align_bytes=DMA_ALIGN))
                 nc.vector.memset(padding(g_scales[0][:].bitcast(U32)), 0)
             cols = slice(g_start[c] + first * P, g_start[c] + end * P)
             quantise(g_codes[:, cols], g_scales[0][:, cols], g_laid[c, first][:].rearrange("p n t -> p (n t)"), E5M2)
@@ -385,21 +385,21 @@ def tile_attend_gnce_w_kernel(tc, xT, wT, y, wt, xm, offs, out):
         lay_g(nc.scalar, 0, 2, last)
         lay_m(nc.scalar, 0, 0, m_tile("m_bf00", "m_bf00")[:, 0])
         lay_g(nc.scalar, 0, 0, 2)
-        turn_back(0, last)
         lay_m(nc.scalar, 0, 1, m_tile("m_bf01", "m_bf01")[:, 0])
+        turn_back(0, last)
         for s in (2, last):
             turn_back(1, s)
         for _ in range(2):
             warm_up(sums[1, last])
         lay_g(nc.scalar, 1, 0, 1)
-        quantise_g(0, 2)
 
-        first_codes = keep.tile([P, CHUNKS, P], U32, name="m_codes0", tag="last_place", align_bytes=DMA_ALIGN)
+        first_codes = keep.tile([P, CHUNKS, P], U32, name="m_codes0", tag="x_late", align_bytes=DMA_ALIGN)
         m_codes.update({(0, c): first_codes[:, c] for c in range(CHUNKS)})
-        quantise_m(0, 0)
+        for c in range(CHUNKS):
+            quantise_m(0, c)
+        quantise_g(0, 2)
         product(0, 0, HALF)
         lay_g(nc.vector, 1, 1, 2)
-        quantise_m(0, 1)
         quantise_g(1, 2)
         product(0, 1, HALF)
         quantise_g(0, 0)
@@ -421,7 +421,7 @@ def tile_attend_gnce_w_kernel(tc, xT, wT, y, wt, xm, offs, out):
 
         for c in range(CHUNKS):
             product(1, c)
-        lay_m(nc.scalar, 2, 0, m_tile("m_bf20", "last_place")[:, 0])
+        lay_m(nc.scalar, 2, 0, m_tile("m_bf20", "x_late")[:, 0])
         lay_m(nc.vector, 2, 1, m_tile("m_bf21", "dense0_0")[:, 0])
         for c in range(CHUNKS):
             quantise_m(2, c)

@@ -20,14 +20,12 @@ P = 128
 PACK = 4
 K_PASS = P * PACK
 CHUNKS = R // K_PASS
-BLOCKS = N // P
 HALF = N // 2
-MX_ALIGN = 64
-DMA_ALIGN = 256
-
-DIRECT = (3, 2)
+LOW, HIGH = 0, 1
+ALIGN = 256
 X_SHARES = (80, 64)
 EARLY = 80
+G_SPLIT = 160
 
 
 def tile_attend_gnce_w_kernel(tc, xT, wT, y, wt, xm, offs, out):
@@ -35,10 +33,14 @@ def tile_attend_gnce_w_kernel(tc, xT, wT, y, wt, xm, offs, out):
     with ExitStack() as ctx:
         lists = ctx.enter_context(tc.tile_pool(name="lists", bufs=1))
         keep = ctx.enter_context(tc.tile_pool(name="keep", bufs=1))
+        reuse = ctx.enter_context(tc.tile_pool(name="reuse", bufs=1))
         banks = ctx.enter_context(tc.psum_pool(name="banks", bufs=1))
 
         def new_bank(k):
             return banks.tile([P, N], F32, name=f"bank{k}", tag=f"bank{k}")
+
+        def new_tile(name, shape, dtype, tag=None):
+            return keep.tile(shape, dtype, name=name, tag=tag or name, align_bytes=ALIGN)
 
         def copy_on(engine, dst, src):
             if engine is nc.vector:
@@ -52,9 +54,11 @@ def tile_attend_gnce_w_kernel(tc, xT, wT, y, wt, xm, offs, out):
         def quantise(codes, scales, laid, fmt):
             nc.vector.quantize_mx(out=codes.bitcast(fmt), scales=scales, in_=laid)
 
-        weight = keep.tile([P, CHUNKS, PACK], F32, name="weight")
+        def half(h):
+            return slice(h * HALF, (h + 1) * HALF)
+
         apart = P // CHUNKS
-        wt_rows = keep.tile([P, K_PASS], F32, name="wt_rows", align_bytes=DMA_ALIGN)
+        wt_rows = new_tile("wt_rows", [P, K_PASS], F32)
         nc.scalar.dma_start(out=wt_rows[0:P:apart, :], in_=wt[0].rearrange("(c k) o -> c (k o)", c=CHUNKS))
         warm_in = keep.tile([P, 1], F32, name="warm_in")
         warm_out = keep.tile([P, 1], F32, name="warm_out")
@@ -66,11 +70,17 @@ def tile_attend_gnce_w_kernel(tc, xT, wT, y, wt, xm, offs, out):
         nc.gpsimd.memset(wt_dealt[:], 0.0)
         for c in range(CHUNKS):
             row = slice(c * apart, c * apart + 1)
-            nc.scalar.copy(out=wt_dealt[row, :, :], in_=wt_rows[row, :].rearrange("c (p t) -> c t p", t=PACK))
+            nc.scalar.activation(
+                out=wt_dealt[row, :, :],
+                in_=wt_rows[row, :].rearrange("c (p t) -> c t p", t=PACK),
+                func=ACT.Copy,
+                scale=-1.0,
+            )
         wt_bank = new_bank(7)[:].rearrange("p (t k) -> p t k", t=PACK)
         for t in range(PACK):
             nc.tensor.transpose(wt_bank[:, t, :], wt_dealt[:, t, :], identity[:])
-        nc.scalar.copy(out=weight[:], in_=wt_bank.rearrange("p t (c k) -> p c t k", c=CHUNKS)[:, :, :, 0])
+        minus = keep.tile([P, CHUNKS, PACK], F32, name="minus")
+        nc.scalar.copy(out=minus[:], in_=wt_bank.rearrange("p t (c k) -> p c t k", c=CHUNKS)[:, :, :, 0])
 
         def place_of(bank, t):
             return bank[:].rearrange("p (e u m) -> p e u m", e=2, u=2)[:, t % 2, t // 2, :]
@@ -78,24 +88,19 @@ def tile_attend_gnce_w_kernel(tc, xT, wT, y, wt, xm, offs, out):
         def by_words(bank):
             return bank[:].rearrange("p (e w) -> p w e", e=2)
 
-        minus_col = keep.tile([P, CHUNKS, PACK, P], F32, name="minus_col")
-        nc.scalar.activation(
-            out=minus_col[:].rearrange("p c t k -> p (c t) k"),
-            in_=weight[:].rearrange("p c t -> p (c t)").unsqueeze(2).to_broadcast([P, CHUNKS * PACK, P]),
-            func=ACT.Copy,
-            scale=-1.0,
-        )
-        minus_row = [keep.tile([P, 2 * P, 2], F32, name=f"minus_row{c}", align_bytes=DMA_ALIGN) for c in range(CHUNKS)]
+        minus_row = [new_tile(f"minus_row{c}", [P, 2 * P, 2], F32) for c in range(CHUNKS)]
         for c in range(CHUNKS):
             bank = new_bank(5 + c)
             for t in range(PACK):
-                nc.tensor.transpose(place_of(bank, t), minus_col[:, c, t, :], identity[:])
-            nc.scalar.copy(out=minus_row[c][:], in_=by_words(bank))
+                nc.tensor.transpose(place_of(bank, t), minus[:, c, t : t + 1].to_broadcast([P, P]), identity[:])
+            nc.vector.tensor_copy(out=minus_row[c][:], in_=by_words(bank))
 
-        def load(name, src):
-            tile = keep.tile(list(src.shape), F32, name=name, tag=name, align_bytes=DMA_ALIGN)
+        def load(tile, src):
             nc.sync.dma_start(out=tile[:], in_=src)
             return tile
+
+        def load_new(name, src):
+            return load(new_tile(name, list(src.shape), F32), src)
 
         offsets = lists.tile([P, N // 16], U16, name="offsets")
         w_rows = wT.rearrange("(p t) c -> p t c", t=PACK)
@@ -103,174 +108,121 @@ def tile_attend_gnce_w_kernel(tc, xT, wT, y, wt, xm, offs, out):
         y_rows = y[0].rearrange("(c p t) i -> c p t i", c=CHUNKS, t=PACK)
         m_rows = xm[0].rearrange("(c p t) d -> c p t d", c=CHUNKS, t=PACK)
 
-        table = [load("table0", w_rows[:, 0, :])]
+        table = [load_new("table0", w_rows[:, 0, :])]
         nc.sync.dma_start(offsets[:], offs)
-        table.extend(load(f"table{t}", w_rows[:, t, :]) for t in range(1, PACK))
-        x_first = load("x_first", x_rows[:, :, 0:K_PASS])
-        x_early = load("x_early", x_rows[:, :, K_PASS : K_PASS + PACK * EARLY])
-        x_late = load("x_late", x_rows[:, :, K_PASS + PACK * EARLY : R])
+        table.extend(load_new(f"table{t}", w_rows[:, t, :]) for t in range(1, PACK))
+        x_first = load_new("x_first", x_rows[:, :, 0:K_PASS])
+        x_early = load_new("x_early", x_rows[:, :, K_PASS : K_PASS + PACK * EARLY])
+        x_last = reuse.tile([P, PACK, PACK * (P - EARLY)], F32, name="x_last", align_bytes=ALIGN, offset=0)
+        load(x_last, x_rows[:, :, K_PASS + PACK * EARLY : R])
         y_raw, m_raw = {}, {}
 
-        def load_y(name, c, places, blocks):
-            part = load(name, y_rows[c, :, places.start : places.stop, blocks.start * P : blocks.stop * P])
-            for t in places:
-                y_raw.update({(c, t, s): part[:, t - places.start, (s - blocks.start) * P :] for s in blocks})
+        def load_y(c, h):
+            y_raw[c, h] = load_new(f"y{c}{h}", y_rows[c, :, :, half(h)])
 
         def load_m(c, blocks):
-            part = load(f"m_part{c}{blocks.start}", m_rows[c, :, :, blocks.start * P : blocks.stop * P])
+            part = load_new(f"m_part{c}{blocks.start}", m_rows[c, :, :, blocks.start * P : blocks.stop * P])
             for b in blocks:
                 m_raw[b, c] = part[:, :, (b - blocks.start) * P : (b - blocks.start + 1) * P]
 
-        for u in range(2):
-            load_y(f"y0_pair{u}", 0, range(2 * u, 2 * u + 2), range(BLOCKS))
-        load_y("y1_turned", 1, range(PACK), range(DIRECT[1], BLOCKS))
-        load_m(0, range(1))
-        load_y("y1_direct", 1, range(PACK), range(DIRECT[1]))
-        load_m(1, range(1))
+        load_y(0, LOW)
+        load_y(0, HIGH)
+        y_blocks = [load_new(f"y_block{s}", y_rows[1, :, :, HALF + s * P : HALF + (s + 1) * P]) for s in range(2)]
+        for c in range(CHUNKS):
+            load_m(c, range(1))
+        load_y(1, LOW)
         for blocks in (range(1, 2), range(2, D // P)):
             for c in range(CHUNKS):
                 load_m(c, blocks)
 
-        window = [keep.tile([P, T], F32, name=f"window{b}", align_bytes=DMA_ALIGN) for b in range(D // P)]
+        window = [new_tile(f"window{b}", [P, T], F32) for b in range(D // P)]
         for b in range(D // P):
             (nc.vector if b < 2 else nc.gpsimd).memset(window[b][:], 0.0)
 
-        w_bf = keep.tile([P, N, PACK], BF16, name="w_bf", align_bytes=MX_ALIGN)
-        w_codes = keep.tile([P, N], U32, name="w_codes", align_bytes=MX_ALIGN)
-        w_scales = keep.tile([P, N], U8, name="w_scales", align_bytes=MX_ALIGN)
-        for t in range(PACK - 1):
-            nc.vector.tensor_copy(out=w_bf[:, :, t], in_=table[t][:].indirect(offsets[:]))
-        slot_halves = [slice(h * HALF, (h + 1) * HALF) for h in range(2)]
-        for h, cols in enumerate(slot_halves):
-            half_list = offsets[:, h * HALF // 16 : (h + 1) * HALF // 16]
-            nc.vector.tensor_copy(out=w_bf[:, cols, PACK - 1], in_=table[PACK - 1][:].indirect(half_list))
-        for cols in slot_halves:
-            quantise(w_codes[:, cols], w_scales[:, cols], w_bf[:, cols, :].rearrange("p n t -> p (n t)"), E4M3)
+        def listed(h):
+            return offsets[:, h * HALF // 16 : (h + 1) * HALF // 16]
 
-        x_bf = [keep.tile([P, PACK, P, PACK], BF16, name=f"x_bf{c}", align_bytes=DMA_ALIGN) for c in range(CHUNKS)]
-        x_codes = [keep.tile([P, K_PASS], U32, name=f"x_codes{c}", align_bytes=MX_ALIGN) for c in range(CHUNKS)]
-        x_scales = [keep.tile([P, K_PASS], U8, name=f"x_scales{c}", align_bytes=MX_ALIGN) for c in range(CHUNKS)]
+        w_bf = [new_tile(f"w_bf{h}", [P, HALF, PACK], BF16) for h in range(2)]
+        for t in range(PACK):
+            nc.scalar.activation(out=w_bf[HIGH][:, :, t], in_=table[t][:].indirect(listed(HIGH)), func=ACT.Copy)
+            nc.vector.tensor_copy(out=w_bf[LOW][:, :, t], in_=table[t][:].indirect(listed(LOW)))
+        w_codes = [new_tile(f"w_codes{h}", [P, HALF], U32) for h in range(2)]
+        w_scales = {HIGH: new_tile("w_scales1", [P, HALF], U8), LOW: new_tile("w_scales0", [P, HALF], U8, "table3")}
+        for h in (HIGH, LOW):
+            quantise(w_codes[h][:], w_scales[h][:], w_bf[h][:].rearrange("p n t -> p (n t)"), E4M3)
+
+        x_bf = [new_tile(f"x_bf{c}", [P, PACK, P, PACK], BF16) for c in range(CHUNKS)]
+        x_codes = [new_tile(f"x_codes{c}", [P, K_PASS], U32) for c in range(CHUNKS)]
+        x_scales = [new_tile(f"x_scales{c}", [P, K_PASS], U8) for c in range(CHUNKS)]
 
         def lay_x(engine, c, raw, first, lo, hi, places):
             src = raw[:].rearrange("p j (m t) -> p m j t", t=PACK)[:, lo - first : hi - first, :, places]
             copy_on(engine, x_bf[c][:, places, lo:hi, :].rearrange("p t m j -> p m j t"), src)
 
-        def quantise_x(c, lo, hi):
-            cols = slice(lo * P, hi * P)
-            laid = x_bf[c][:, lo:hi, :, :].rearrange("p t m j -> p (t m j)")
-            quantise(x_codes[c][:, cols], x_scales[c][:, cols], laid, E4M3)
+        def quantise_x(c):
+            for lo, hi in ((0, 1), (1, 2), (2, PACK)):
+                cols = slice(lo * P, hi * P)
+                laid = x_bf[c][:, lo:hi, :, :].rearrange("p t m j -> p (t m j)")
+                quantise(x_codes[c][:, cols], x_scales[c][:, cols], laid, E4M3)
 
-        def score_pass(dst, c, t, cols):
+        def score_pass(dst, c, t, h):
             nc.tensor.matmul_mx(
                 out=dst,
                 lhsT=x_codes[c][:, t * P : (t + 1) * P].bitcast(E4M3),
                 lhsT_scale=x_scales[c][:, t * P : (t + 1) * P],
-                rhs=w_codes[:, cols].bitcast(E4M3),
-                rhs_scale=w_scales[:, cols],
+                rhs=w_codes[h][:].bitcast(E4M3),
+                rhs_scale=w_scales[h][:],
                 start=True,
                 stop=True,
             )
 
         sig = [keep.tile([P, PACK, N], F32, name=f"sig{c}") for c in range(CHUNKS)]
 
-        def scores(c, t, k, cols=slice(0, N)):
+        def scores(c, t, k, halves):
             bank = new_bank(k)
-            score_pass(bank[:, cols], c, t, cols)
+            for h in halves:
+                score_pass(bank[:, half(h)], c, t, h)
+            cols = slice(min(halves) * HALF, (max(halves) + 1) * HALF)
             nc.scalar.activation(out=sig[c][:, t, cols], in_=bank[:, cols], func=ACT.Sigmoid, scale=-1.0)
 
-        def warm_up(bank):
-            score_pass(bank[:], 0, 0, slice(0, N))
+        pairs = (slice(0, 2), slice(2, PACK))
+        for places, share in zip(pairs, X_SHARES):
+            lay_x(nc.vector, 0, x_first, 0, 0, share, places)
+            lay_x(nc.scalar, 0, x_first, 0, share, P, places)
+        quantise_x(0)
+        for t in range(PACK):
+            for i, h in enumerate((LOW, HIGH)):
+                scores(0, t, 2 * t + i, (h,))
+        lay_x(nc.vector, 1, x_early, 0, 0, EARLY, slice(0, PACK))
+        for places in pairs:
+            lay_x(nc.vector, 1, x_last, EARLY, EARLY, P, places)
+        quantise_x(1)
 
-        g_laid, g_scales = {}, []
-        g_start = (0, N + HALF)
-        g_width = CHUNKS * (N + HALF)
-
-        def padding(plane):
-            return plane.rearrange("p (c w) -> p c w", c=CHUNKS)[:, :, plane.shape[1] // 3 :]
-
-        g_codes = keep.tile([P, g_width], U32, name="g_codes", align_bytes=DMA_ALIGN)
-        nc.gpsimd.memset(padding(g_codes[:]), 0)
-        g_runs = {
-            (0, 0): (2, "g00"),
-            (0, 2): (BLOCKS, "g02"),
-            (1, 0): (1, "g_turned13"),
-            (1, 1): (2, "g11"),
-            (1, 2): (BLOCKS, "g12"),
-        }
-
-        def laid_blocks(c, lo, hi):
-            first = max(start for chunk, start in g_runs if chunk == c and start <= lo)
-            if (c, first) not in g_laid:
-                end, tag = g_runs[c, first]
-                g_laid[c, first] = keep.tile(
-                    [P, (end - first) * P, PACK], BF16, name=f"g_laid{c}{first}", tag=tag, align_bytes=DMA_ALIGN
-                )
-            return g_laid[c, first][:, (lo - first) * P : (hi - first) * P, :]
-
-        def quantise_g(c, first):
-            end = g_runs[c, first][0]
-            if not g_scales:
-                g_scales.append(keep.tile([P, g_width], U8, name="g_scales", tag="last_place", align_bytes=DMA_ALIGN))
-                nc.vector.memset(padding(g_scales[0][:].bitcast(U32)), 0)
-            cols = slice(g_start[c] + first * P, g_start[c] + end * P)
-            quantise(g_codes[:, cols], g_scales[0][:, cols], g_laid[c, first][:].rearrange("p n t -> p (n t)"), E5M2)
-
-        weighted = {}
-        g_rows = [
-            keep.tile([P, PACK, DIRECT[c] * P], BF16, name=f"g_rows{c}", align_bytes=DMA_ALIGN) for c in range(CHUNKS)
-        ]
-
-        def weigh(c, places, tag):
-            shape = [P, len(places), DIRECT[c] * P]
-            part = keep.tile(shape, F32, name=f"weighted{c}{places.start}", tag=tag, align_bytes=DMA_ALIGN)
-            for t in places:
-                weighted[c, t] = part[:, t - places.start, :]
-                nc.vector.tensor_scalar(
-                    out=weighted[c, t],
-                    in0=sig[c][:, t, 0 : DIRECT[c] * P],
-                    scalar1=minus_col[:, c, t, 0:1],
-                    scalar2=weight[:, c, t : t + 1],
-                    op0=ALU.mult,
-                    op1=ALU.add,
-                )
-
-        def gradient(c, t):
-            nc.vector.scalar_tensor_tensor(
-                out=g_rows[c][:, t, :],
-                in0=y_raw[c, t, 0][:, 0 : DIRECT[c] * P],
-                scalar=minus_col[:, c, t, 0:1],
-                in1=weighted[c, t],
-                op0=ALU.mult,
-                op1=ALU.add,
-            )
-
-        def lay_g(engine, c, lo, hi):
-            side_by_side(engine, laid_blocks(c, lo, hi), g_rows[c][:, :, lo * P : hi * P])
-
-        sum_bank = {(0, 3): 5, (1, 2): 7, (1, 3): 6}
-        word_bank = {(0, 3): 7, (1, 2): 0, (1, 3): 3}
         sums, turned, g_turned = {}, {}, {}
+        sum_bank = {(0, 0): 6, (0, 1): 7, (1, 0): 0, (1, 1): 1}
 
         def turn(c, s, what, places):
             if (c, s) not in sums:
                 sums[c, s] = new_bank(sum_bank[c, s])
                 turned[c, s] = 0
             for t in places:
-                src = sig[c][:, t, s * P :] if what == "s" else y_raw[c, t, s]
+                cols = slice(s * P, (s + 1) * P)
+                if what == "s":
+                    src = sig[c][:, t, half(HIGH)][:, cols]
+                else:
+                    src = y_blocks[s][:, t, :] if c else y_raw[c, HIGH][:, t, cols]
                 turned[c, s] = turned[c, s] + 1
                 nc.tensor.matmul(
                     place_of(sums[c, s], t),
-                    lhsT=src[:, 0:P],
+                    lhsT=src,
                     rhs=identity[:],
                     start=turned[c, s] == 1,
                     stop=turned[c, s] == 2 * PACK,
                     is_transpose=True,
                 )
 
-        def gradient_turned(c, s):
-            g_turned[c, s] = keep.tile(
-                [P, 2 * P, 2], BF16, name=f"g_turned{c}{s}", tag=f"g_turned{c}{s}", align_bytes=DMA_ALIGN
-            )
+        def gradient_turned(c, s, tag=None):
+            g_turned[c, s] = new_tile(f"g_turned{c}{s}", [P, 2 * P, 2], BF16, tag)
             nc.vector.scalar_tensor_tensor(
                 out=g_turned[c, s][:],
                 in0=by_words(sums[c, s]),
@@ -280,159 +232,178 @@ def tile_attend_gnce_w_kernel(tc, xT, wT, y, wt, xm, offs, out):
                 op1=ALU.mult,
             )
 
-        def turn_back(c, s):
-            words = g_turned[c, s][:].rearrange("p w e -> p (w e)").bitcast(F32)
-            bank = new_bank(word_bank[c, s])[:, 0 : 2 * P].rearrange("p (u n) -> p u n", u=2)
-            for u in range(2):
-                nc.tensor.transpose(bank[:, u, :], words[:, u * P : (u + 1) * P], identity[:])
-            dst = laid_blocks(c, s, s + 1).rearrange("p n t -> p (n t)").bitcast(F32)
-            nc.scalar.copy(out=dst.rearrange("p (n u) -> p n u", u=2), in_=bank.rearrange("p u n -> p n u"))
+        g_laid = {}
 
-        m_bf, m_codes, m_scales, acc = {}, {}, {}, {}
-        acc_bank = (7, 1, 2, 5)
+        def turn_back(c, k, order):
+            bank = new_bank(k)[:].rearrange("p (s u n) -> p s u n", s=2, u=2)
+            for s in order:
+                words = g_turned[c, s][:].rearrange("p w e -> p (w e)").bitcast(F32)
+                for u in range(2):
+                    nc.tensor.transpose(bank[:, s, u, :], words[:, u * P : (u + 1) * P], identity[:])
+            g_laid[c, HIGH] = new_tile(f"g_laid{c}1", [P, HALF, PACK], BF16)
+            dst = g_laid[c, HIGH][:].rearrange("p n t -> p (n t)").bitcast(F32)
+            nc.scalar.copy(out=dst.rearrange("p (s n u) -> p s n u", s=2, u=2), in_=bank.rearrange("p s u n -> p s n u"))
+
+        weighted = {}
+        g_rows = {}
+
+        def weigh(c, u, part):
+            for t in (2 * u, 2 * u + 1):
+                weighted[c, t] = part[:, t % 2, :]
+                nc.vector.tensor_scalar(
+                    out=weighted[c, t],
+                    in0=sig[c][:, t, half(LOW)],
+                    scalar1=1.0,
+                    scalar2=minus[:, c, t : t + 1],
+                    op0=ALU.subtract,
+                    op1=ALU.mult,
+                )
+
+        def on_x_last(name, shape, dtype, u):
+            return reuse.tile(shape, dtype, name=name, tag=f"x_last{u}", align_bytes=ALIGN, offset=u * 2 * HALF * 4)
+
+        def gradient(c, tag=None):
+            g_rows[c] = new_tile(f"g_rows{c}", [P, PACK, HALF], BF16, tag)
+            for t in range(PACK):
+                nc.vector.scalar_tensor_tensor(
+                    out=g_rows[c][:, t, :],
+                    in0=y_raw[c, LOW][:, t, :],
+                    scalar=minus[:, c, t : t + 1],
+                    in1=weighted[c, t],
+                    op0=ALU.mult,
+                    op1=ALU.add,
+                )
+
+        def lay_g(engine, c, cols):
+            if (c, LOW) not in g_laid:
+                g_laid[c, LOW] = new_tile(f"g_laid{c}0", [P, HALF, PACK], BF16, "g_turned11" if c else None)
+            side_by_side(engine, g_laid[c, LOW][:, cols, :], g_rows[c][:, :, cols])
+
+        g_codes, g_scales = {}, {}
+
+        def quantise_g(c, h, scales, tag=None):
+            g_codes[c, h] = new_tile(f"g_codes{c}{h}", [P, HALF], U32, tag)
+            g_scales[c, h] = scales
+            quantise(g_codes[c, h][:], scales, g_laid[c, h][:].rearrange("p n t -> p (n t)"), E5M2)
+
+        m_bf, m_codes, m_scales, acc, dense = {}, {}, {}, {}, {}
 
         def lay_m(engine, b, c, dst):
             m_bf[b, c] = dst
             side_by_side(engine, dst, m_raw[b, c])
 
-        def m_tile(name, tag, pieces=1):
-            return keep.tile([P, pieces, P, PACK], BF16, name=name, tag=tag, align_bytes=DMA_ALIGN)
+        def quantise_m(b, chunks, codes, laid):
+            scales = new_tile(f"m_scales{b}{chunks.start}", [P, len(chunks) * P], U8)
+            for i, c in enumerate(chunks):
+                m_codes[b, c] = codes[:, i * P : (i + 1) * P]
+                m_scales[b, c] = scales[:, i * P : (i + 1) * P]
+            quantise(codes, scales[:], laid, E4M3)
 
-        def quantise_m(b, c):
-            if (b, c) not in m_codes:
-                name = f"m_codes{b}{c}"
-                m_codes[b, c] = keep.tile([P, P], U32, name=name, tag=name, align_bytes=DMA_ALIGN)[:]
-            m_scales[b, c] = keep.tile([P, P], U8, name=f"m_scales{b}{c}", align_bytes=MX_ALIGN)
-            quantise(m_codes[b, c], m_scales[b, c][:], m_bf[b, c].rearrange("p n t -> p (n t)"), E4M3)
-
-        def product(b, c, first=0):
-            opens = (b, first) not in acc
-            if opens:
-                acc[b, first] = new_bank(acc_bank[-1] if first else acc_bank[b])
-            cols = slice(g_start[c] + first, g_start[c] + first + N)
+        def product(b, c, h, opens):
             nc.tensor.matmul_mx(
-                out=acc[b, first][:],
+                out=acc[b, h],
                 lhsT=m_codes[b, c].bitcast(E4M3),
-                lhsT_scale=m_scales[b, c][:],
-                rhs=g_codes[:, cols].bitcast(E5M2),
-                rhs_scale=g_scales[0][:, cols],
+                lhsT_scale=m_scales[b, c],
+                rhs=g_codes[c, h][:].bitcast(E5M2),
+                rhs_scale=g_scales[c, h],
                 start=opens,
                 stop=not opens,
             )
 
-        dense = {}
+        def copy_out(name, src):
+            dense[name] = new_tile(name, list(src.shape), F32)
+            nc.scalar.copy(out=dense[name][:], in_=src)
 
-        def copy_out(b, first=0, width=N):
-            name = f"dense{b}_{first}"
-            dense[b, first] = keep.tile([P, width], F32, name=name, tag=name, align_bytes=DMA_ALIGN)
-            nc.scalar.copy(out=dense[b, first][:], in_=acc[b, first][:, 0:width])
-
-        def scatter(b, first=0, width=N):
-            listed = offsets[:, first // 16 : (first + width) // 16]
-            nc.vector.tensor_copy(out=window[b][:].indirect(listed), in_=dense[b, first][:])
+        def scatter(b, name, where):
+            nc.vector.tensor_copy(out=window[b][:].indirect(where), in_=dense[name][:])
 
         def store(b):
             nc.sync.dma_start(out=out[b * P : (b + 1) * P, :], in_=window[b][:])
 
-        def output_block(b):
-            copy_out(b)
-            scatter(b)
+        for h in (LOW, HIGH):
+            scores(1, 0, h, (h,))
+        for t in range(1, PACK - 1):
+            scores(1, t, 1 + t, (HIGH, LOW))
+        for h in (LOW, HIGH):
+            scores(1, PACK - 1, 4 + h, (h,))
+        for u in range(2):
+            weigh(0, u, on_x_last(f"weighted0{u}", [P, 2, HALF], F32, u))
+        gradient(0)
+        weigh(1, 0, on_x_last("weighted10", [P, 2, HALF], F32, 0))
+        for s in range(2):
+            turn(0, s, "y", range(PACK))
+            turn(0, s, "s", range(PACK))
+        gradient_turned(0, 0)
+        weigh(1, 1, new_tile("weighted11", [P, 2, HALF], F32, "y01"))
+        lay_g(nc.scalar, 0, slice(0, HALF))
+        turn(1, 0, "y", range(PACK))
+        turn(1, 0, "s", range(PACK))
+        turn(1, 1, "y", range(1))
+        turn(1, 1, "s", range(PACK))
+        turn(1, 1, "y", range(1, PACK))
+        gradient_turned(0, 1, "y_block0")
+        for s in range(2):
+            gradient_turned(1, s)
+        first_m = new_tile("m_bf0", [P, CHUNKS, P, PACK], BF16)
+        for c in range(CHUNKS):
+            lay_m(nc.scalar, 0, c, first_m[:, c])
+        turn_back(0, 2, (1, 0))
+        turn_back(1, 3, (0, 1))
+        gradient(1, "y_block1")
+        lay_g(nc.scalar, 1, slice(0, G_SPLIT))
+        quantise_m(0, range(CHUNKS), on_x_last("m_codes0", [P, CHUNKS * P], U32, 0)[:], first_m[:].rearrange("p c n t -> p (c n t)"))
+        scales = new_tile("g_scales", [P, 2, CHUNKS, HALF], U8, "y01")
+        acc.update({(0, HIGH): new_bank(4)[:, 0:HALF], (0, LOW): new_bank(5)[:, 0:HALF]})
+        for c in range(CHUNKS):
+            quantise_g(c, HIGH, scales[:, HIGH, c])
+            product(0, c, HIGH, c == 0)
+        lay_g(nc.vector, 1, slice(G_SPLIT, HALF))
+        for c in range(CHUNKS):
+            quantise_g(c, LOW, scales[:, LOW, c], None if c else "g_laid11")
+            product(0, c, LOW, c == 0)
+        lay_m(nc.scalar, 1, 1, new_tile("m_bf11", [P, P, PACK], BF16, "y10")[:])
+        copy_out("dense01", acc[0, HIGH])
+
+        def quantise_piece(b, c, tag=None):
+            codes = new_tile(f"m_codes{b}{c}", [P, P], U32, tag)
+            quantise_m(b, range(c, c + 1), codes[:], m_bf[b, c].rearrange("p n t -> p (n t)"))
+
+        acc.update({(1, HIGH): new_bank(6)[:, 0:HALF], (1, LOW): new_bank(7)[:, 0:HALF]})
+        lay_m(nc.vector, 1, 0, new_tile("m_bf10", [P, P, PACK], BF16, "g_laid00")[:])
+        quantise_piece(1, 1, "g_turned11")
+        scatter(0, "dense01", listed(HIGH))
+        copy_out("dense00", acc[0, LOW])
+        quantise_piece(1, 0)
+        scatter(0, "dense00", listed(LOW))
+        store(0)
+        for c in (1, 0):
+            for h in (HIGH, LOW):
+                product(1, c, h, c == 1)
+
+        def products(b, k):
+            bank = new_bank(k)
+            for h in (HIGH, LOW):
+                acc[b, h] = bank[:, half(h)]
+                for c in range(CHUNKS):
+                    product(b, c, h, c == 0)
+            return bank
+
+        def output(b, bank):
+            copy_out(f"dense{b}", bank[:])
+            scatter(b, f"dense{b}", offsets[:])
             store(b)
 
-        pairs = (slice(0, 2), slice(2, PACK))
-        for places, share in zip(pairs, X_SHARES):
-            lay_x(nc.vector, 0, x_first, 0, 0, share, places)
-            lay_x(nc.scalar, 0, x_first, 0, share, P, places)
-        for lo, hi in ((0, 1), (1, 2), (2, PACK)):
-            quantise_x(0, lo, hi)
-        for t in range(PACK):
-            for h, cols in enumerate(slot_halves):
-                scores(0, t, 2 * t + h, cols)
-
-        lay_x(nc.vector, 1, x_early, 0, 0, EARLY, slice(0, PACK))
-        for places in pairs:
-            lay_x(nc.vector, 1, x_late, EARLY, EARLY, P, places)
-        for lo, hi in ((0, 1), (1, 2), (2, PACK)):
-            quantise_x(1, lo, hi)
-        for h, cols in enumerate(slot_halves):
-            scores(1, 0, h, cols)
-        for t in range(1, PACK):
-            scores(1, t, t + 1)
-
-        last = BLOCKS - 1
-        weigh(0, range(3), "x_late")
-        for t in range(2):
-            gradient(0, t)
-        weigh(0, range(3, PACK), "last_place")
-        for t in range(2, PACK):
-            gradient(0, t)
-        turn(0, last, "y", (2, 3, 0, 1))
-        turn(0, last, "s", range(PACK))
-        gradient_turned(0, last)
-
-        weigh(1, range(3), "x_late")
-        weigh(1, range(3, PACK), "last_place")
-        turn(1, 2, "y", range(PACK))
-        turn(1, 2, "s", range(2))
-        turn(1, last, "y", range(PACK))
-        turn(1, 2, "s", range(2, PACK))
-        turn(1, last, "s", range(PACK))
-        for s in (2, last):
-            gradient_turned(1, s)
-        for t in range(PACK):
-            gradient(1, t)
-
-        lay_g(nc.scalar, 0, 2, last)
-        lay_m(nc.scalar, 0, 0, m_tile("m_bf00", "m_bf00")[:, 0])
-        lay_g(nc.scalar, 0, 0, 2)
-        lay_m(nc.scalar, 0, 1, m_tile("m_bf01", "m_bf01")[:, 0])
-        turn_back(0, last)
-        for s in (2, last):
-            turn_back(1, s)
-        for _ in range(2):
-            warm_up(sums[1, last])
-        lay_g(nc.scalar, 1, 0, 1)
-
-        first_codes = keep.tile([P, CHUNKS, P], U32, name="m_codes0", tag="x_late", align_bytes=DMA_ALIGN)
-        m_codes.update({(0, c): first_codes[:, c] for c in range(CHUNKS)})
+        lay_m(nc.scalar, 2, 0, on_x_last("m_bf20", [P, P, PACK], BF16, 0)[:])
+        lay_m(nc.vector, 2, 1, new_tile("m_bf21", [P, P, PACK], BF16, "dense00")[:])
+        for h in (HIGH, LOW):
+            copy_out(f"dense1{h}", acc[1, h])
+            scatter(1, f"dense1{h}", listed(h))
+            quantise_piece(2, h)
+        store(1)
+        bank = products(2, 0)
+        lay_m(nc.scalar, 3, 0, new_tile("m_bf30", [P, P, PACK], BF16, "m_codes10")[:])
+        lay_m(nc.vector, 3, 1, new_tile("m_bf31", [P, P, PACK], BF16, "dense11")[:])
         for c in range(CHUNKS):
-            quantise_m(0, c)
-        quantise_g(0, 2)
-        product(0, 0, HALF)
-        lay_g(nc.vector, 1, 1, 2)
-        quantise_g(1, 2)
-        product(0, 1, HALF)
-        quantise_g(0, 0)
-        product(0, 0)
-        quantise_g(1, 1)
-        quantise_g(1, 0)
-        product(0, 1)
-        copy_out(0, HALF, HALF)
-        lay_m(nc.vector, 1, 0, m_tile("m_bf10", "g00")[:, 0])
-        m_bf[1, 1] = m_tile("m_bf11", "g_turned13")[:, 0]
-        for engine, cols in ((nc.scalar, slice(0, P // 2)), (nc.vector, slice(P // 2, P))):
-            side_by_side(engine, m_bf[1, 1][:, cols, :], m_raw[1, 1][:, :, cols])
-        scatter(0, HALF, HALF)
-        copy_out(0, 0, HALF)
-        for c in range(CHUNKS):
-            quantise_m(1, c)
-        scatter(0, 0, HALF)
-        store(0)
-
-        for c in range(CHUNKS):
-            product(1, c)
-        lay_m(nc.scalar, 2, 0, m_tile("m_bf20", "x_late")[:, 0])
-        lay_m(nc.vector, 2, 1, m_tile("m_bf21", "dense0_0")[:, 0])
-        for c in range(CHUNKS):
-            quantise_m(2, c)
-        output_block(1)
-        for c in range(CHUNKS):
-            product(2, c)
-        lay_m(nc.scalar, 3, 0, m_tile("m_bf30", "m_codes11")[:, 0])
-        lay_m(nc.vector, 3, 1, m_tile("m_bf31", "dense1_0")[:, 0])
-        for c in range(CHUNKS):
-            quantise_m(3, c)
-        output_block(2)
-        for c in range(CHUNKS):
-            product(3, c)
-        output_block(3)
+            quantise_piece(3, c)
+        output(2, bank)
+        output(3, products(3, 1))

@@ -25,7 +25,9 @@ LOW, HIGH = 0, 1
 ALIGN = 256
 X_SHARES = (80, 64)
 EARLY = 80
-G_SPLIT = 160
+Y_LAST = 4096
+Y_HIGH = 8192
+G_SPLIT = 256
 
 
 def tile_attend_gnce_w_kernel(tc, xT, wT, y, wt, xm, offs, out):
@@ -126,11 +128,13 @@ def tile_attend_gnce_w_kernel(tc, xT, wT, y, wt, xm, offs, out):
                 m_raw[b, c] = part[:, :, (b - blocks.start) * P : (b - blocks.start + 1) * P]
 
         load_y(0, LOW)
-        load_y(0, HIGH)
-        y_blocks = [load_new(f"y_block{s}", y_rows[1, :, :, HALF + s * P : HALF + (s + 1) * P]) for s in range(2)]
+        y_high = reuse.tile([P, PACK, HALF], F32, name="y_high", align_bytes=ALIGN, offset=Y_HIGH)
+        y_raw[0, HIGH] = load(y_high, y_rows[0, :, :, half(HIGH)])
+        y_last = reuse.tile([P, PACK, HALF], F32, name="y_last", align_bytes=ALIGN, offset=Y_LAST)
+        y_raw[1, HIGH] = load(y_last, y_rows[1, :, :, half(HIGH)])
+        load_y(1, LOW)
         for c in range(CHUNKS):
             load_m(c, range(1))
-        load_y(1, LOW)
         for blocks in (range(1, 2), range(2, D // P)):
             for c in range(CHUNKS):
                 load_m(c, blocks)
@@ -176,7 +180,7 @@ def tile_attend_gnce_w_kernel(tc, xT, wT, y, wt, xm, offs, out):
                 stop=True,
             )
 
-        sig = [keep.tile([P, PACK, N], F32, name=f"sig{c}") for c in range(CHUNKS)]
+        sig = [new_tile(f"sig{c}", [P, PACK, N], F32) for c in range(CHUNKS)]
 
         def scores(c, t, k, halves):
             bank = new_bank(k)
@@ -210,7 +214,7 @@ def tile_attend_gnce_w_kernel(tc, xT, wT, y, wt, xm, offs, out):
                 if what == "s":
                     src = sig[c][:, t, half(HIGH)][:, cols]
                 else:
-                    src = y_blocks[s][:, t, :] if c else y_raw[c, HIGH][:, t, cols]
+                    src = y_raw[c, HIGH][:, t, cols]
                 turned[c, s] = turned[c, s] + 1
                 nc.tensor.matmul(
                     place_of(sums[c, s], t),
@@ -221,8 +225,8 @@ def tile_attend_gnce_w_kernel(tc, xT, wT, y, wt, xm, offs, out):
                     is_transpose=True,
                 )
 
-        def gradient_turned(c, s, tag=None):
-            g_turned[c, s] = new_tile(f"g_turned{c}{s}", [P, 2 * P, 2], BF16, tag)
+        def gradient_turned(c, s, dst):
+            g_turned[c, s] = dst
             nc.vector.scalar_tensor_tensor(
                 out=g_turned[c, s][:],
                 in0=by_words(sums[c, s]),
@@ -234,15 +238,13 @@ def tile_attend_gnce_w_kernel(tc, xT, wT, y, wt, xm, offs, out):
 
         g_laid = {}
 
-        def turn_back(c, k, order):
-            bank = new_bank(k)[:].rearrange("p (s u n) -> p s u n", s=2, u=2)
-            for s in order:
-                words = g_turned[c, s][:].rearrange("p w e -> p (w e)").bitcast(F32)
-                for u in range(2):
-                    nc.tensor.transpose(bank[:, s, u, :], words[:, u * P : (u + 1) * P], identity[:])
-            g_laid[c, HIGH] = new_tile(f"g_laid{c}1", [P, HALF, PACK], BF16)
-            dst = g_laid[c, HIGH][:].rearrange("p n t -> p (n t)").bitcast(F32)
-            nc.scalar.copy(out=dst.rearrange("p (s n u) -> p s n u", s=2, u=2), in_=bank.rearrange("p s u n -> p s n u"))
+        def turn_back(c, s, k):
+            bank = new_bank(k)[:, 0 : 2 * P].rearrange("p (u n) -> p u n", u=2)
+            words = g_turned[c, s][:].rearrange("p w e -> p (w e)").bitcast(F32)
+            for u in range(2):
+                nc.tensor.transpose(bank[:, u, :], words[:, u * P : (u + 1) * P], identity[:])
+            dst = g_laid[c, HIGH][:, s * P : (s + 1) * P, :].rearrange("p n t -> p (n t)").bitcast(F32)
+            nc.scalar.copy(out=dst.rearrange("p (n u) -> p n u", u=2), in_=bank.rearrange("p u n -> p n u"))
 
         weighted = {}
         g_rows = {}
@@ -262,8 +264,11 @@ def tile_attend_gnce_w_kernel(tc, xT, wT, y, wt, xm, offs, out):
         def on_x_last(name, shape, dtype, u):
             return reuse.tile(shape, dtype, name=name, tag=f"x_last{u}", align_bytes=ALIGN, offset=u * 2 * HALF * 4)
 
-        def gradient(c, tag=None):
-            g_rows[c] = new_tile(f"g_rows{c}", [P, PACK, HALF], BF16, tag)
+        def on_y_last(name, shape, dtype, shift):
+            return reuse.tile(shape, dtype, name=name, align_bytes=ALIGN, offset=Y_LAST + shift)
+
+        def gradient(c, rows):
+            g_rows[c] = rows
             for t in range(PACK):
                 nc.vector.scalar_tensor_tensor(
                     out=g_rows[c][:, t, :],
@@ -275,16 +280,17 @@ def tile_attend_gnce_w_kernel(tc, xT, wT, y, wt, xm, offs, out):
                 )
 
         def lay_g(engine, c, cols):
-            if (c, LOW) not in g_laid:
-                g_laid[c, LOW] = new_tile(f"g_laid{c}0", [P, HALF, PACK], BF16, "g_turned11" if c else None)
             side_by_side(engine, g_laid[c, LOW][:, cols, :], g_rows[c][:, :, cols])
 
         g_codes, g_scales = {}, {}
 
-        def quantise_g(c, h, scales, tag=None):
-            g_codes[c, h] = new_tile(f"g_codes{c}{h}", [P, HALF], U32, tag)
+        def quantise_g(c, h, scales, parts=1):
+            g_codes[c, h] = new_tile(f"g_codes{c}{h}", [P, HALF], U32)
             g_scales[c, h] = scales
-            quantise(g_codes[c, h][:], scales, g_laid[c, h][:].rearrange("p n t -> p (n t)"), E5M2)
+            for i in range(parts):
+                cols = slice(i * HALF // parts, (i + 1) * HALF // parts)
+                laid = g_laid[c, h][:, cols, :].rearrange("p n t -> p (n t)")
+                quantise(g_codes[c, h][:, cols], scales[:, cols], laid, E5M2)
 
         m_bf, m_codes, m_scales, acc, dense = {}, {}, {}, {}, {}
 
@@ -328,53 +334,59 @@ def tile_attend_gnce_w_kernel(tc, xT, wT, y, wt, xm, offs, out):
             scores(1, PACK - 1, 4 + h, (h,))
         for u in range(2):
             weigh(0, u, on_x_last(f"weighted0{u}", [P, 2, HALF], F32, u))
-        gradient(0)
+        gradient(0, new_tile("g_rows0", [P, PACK, HALF], BF16))
         weigh(1, 0, on_x_last("weighted10", [P, 2, HALF], F32, 0))
         for s in range(2):
             turn(0, s, "y", range(PACK))
             turn(0, s, "s", range(PACK))
-        gradient_turned(0, 0)
-        weigh(1, 1, new_tile("weighted11", [P, 2, HALF], F32, "y01"))
+        words = [P, 2 * P, 2]
+        gradient_turned(0, 0, new_tile("g_turned00", words, BF16))
+        weigh(1, 1, reuse.tile([P, 2, HALF], F32, name="weighted11", tag="y_high0", align_bytes=ALIGN, offset=Y_HIGH))
+        gradient_turned(0, 1, new_tile("g_turned01", words, BF16))
+        g_laid[0, LOW] = new_tile("g_laid00", [P, HALF, PACK], BF16)
         lay_g(nc.scalar, 0, slice(0, HALF))
+        g_laid.update({(c, HIGH): new_tile(f"g_laid{c}1", [P, HALF, PACK], BF16) for c in range(CHUNKS)})
         turn(1, 0, "y", range(PACK))
+        turn_back(0, 0, 2)
         turn(1, 0, "s", range(PACK))
         turn(1, 1, "y", range(1))
         turn(1, 1, "s", range(PACK))
         turn(1, 1, "y", range(1, PACK))
-        gradient_turned(0, 1, "y_block0")
-        for s in range(2):
-            gradient_turned(1, s)
-        first_m = new_tile("m_bf0", [P, CHUNKS, P, PACK], BF16)
-        for c in range(CHUNKS):
-            lay_m(nc.scalar, 0, c, first_m[:, c])
-        turn_back(0, 2, (1, 0))
-        turn_back(1, 3, (0, 1))
-        gradient(1, "y_block1")
+        gradient(1, new_tile("g_rows1", [P, PACK, HALF], BF16, "sig0"))
+        gradient_turned(1, 0, on_x_last("g_turned10", words, BF16, 0))
+        gradient_turned(1, 1, reuse.tile(words, BF16, name="g_turned11", tag="y_high0", align_bytes=ALIGN, offset=Y_HIGH))
+        lay_m(nc.scalar, 0, 0, new_tile("m_bf00", [P, P, PACK], BF16)[:])
+        g_laid[1, LOW] = new_tile("g_laid10", [P, HALF, PACK], BF16)
+        lay_m(nc.vector, 0, 1, on_y_last("m_bf01", [P, P, PACK], BF16, 2048)[:])
         lay_g(nc.scalar, 1, slice(0, G_SPLIT))
-        quantise_m(0, range(CHUNKS), on_x_last("m_codes0", [P, CHUNKS * P], U32, 0)[:], first_m[:].rearrange("p c n t -> p (c n t)"))
-        scales = new_tile("g_scales", [P, 2, CHUNKS, HALF], U8, "y01")
+        turn_back(0, 1, 3)
+        for s in range(2):
+            turn_back(1, s, 6 + s)
+        scales = on_y_last("g_scales", [P, 2, CHUNKS, HALF], U8, 0)
+        quantise_g(0, LOW, scales[:, LOW, 0])
+        m_first = on_y_last("m_codes0", [P, CHUNKS * P], U32, 1024)
+        for c in range(CHUNKS):
+            quantise_m(0, range(c, c + 1), m_first[:, c * P : (c + 1) * P], m_bf[0, c].rearrange("p n t -> p (n t)"))
         acc.update({(0, HIGH): new_bank(4)[:, 0:HALF], (0, LOW): new_bank(5)[:, 0:HALF]})
-        for c in range(CHUNKS):
-            quantise_g(c, HIGH, scales[:, HIGH, c])
-            product(0, c, HIGH, c == 0)
-        lay_g(nc.vector, 1, slice(G_SPLIT, HALF))
-        for c in range(CHUNKS):
-            quantise_g(c, LOW, scales[:, LOW, c], None if c else "g_laid11")
-            product(0, c, LOW, c == 0)
-        lay_m(nc.scalar, 1, 1, new_tile("m_bf11", [P, P, PACK], BF16, "y10")[:])
-        copy_out("dense01", acc[0, HIGH])
+        for h in (LOW, HIGH):
+            for c in range(CHUNKS):
+                if c + h:
+                    quantise_g(c, h, scales[:, h, c], 1 + c * h)
+                product(0, c, h, c == 0)
+        copy_out("dense00", acc[0, LOW])
+        lay_m(nc.scalar, 1, 1, reuse.tile([P, P, PACK], BF16, name="m_bf11", tag="y_high0", align_bytes=ALIGN, offset=Y_HIGH)[:])
 
         def quantise_piece(b, c, tag=None):
             codes = new_tile(f"m_codes{b}{c}", [P, P], U32, tag)
             quantise_m(b, range(c, c + 1), codes[:], m_bf[b, c].rearrange("p n t -> p (n t)"))
 
-        acc.update({(1, HIGH): new_bank(6)[:, 0:HALF], (1, LOW): new_bank(7)[:, 0:HALF]})
-        lay_m(nc.vector, 1, 0, new_tile("m_bf10", [P, P, PACK], BF16, "g_laid00")[:])
-        quantise_piece(1, 1, "g_turned11")
-        scatter(0, "dense01", listed(HIGH))
-        copy_out("dense00", acc[0, LOW])
-        quantise_piece(1, 0)
+        acc.update({(1, HIGH): new_bank(2)[:, 0:HALF], (1, LOW): new_bank(3)[:, 0:HALF]})
+        lay_m(nc.vector, 1, 0, new_tile("m_bf10", [P, P, PACK], BF16, "g_laid01")[:])
+        quantise_piece(1, 1, "g_laid10")
         scatter(0, "dense00", listed(LOW))
+        copy_out("dense01", acc[0, HIGH])
+        quantise_piece(1, 0)
+        scatter(0, "dense01", listed(HIGH))
         store(0)
         for c in (1, 0):
             for h in (HIGH, LOW):
@@ -393,8 +405,8 @@ def tile_attend_gnce_w_kernel(tc, xT, wT, y, wt, xm, offs, out):
             scatter(b, f"dense{b}", offsets[:])
             store(b)
 
-        lay_m(nc.scalar, 2, 0, on_x_last("m_bf20", [P, P, PACK], BF16, 0)[:])
-        lay_m(nc.vector, 2, 1, new_tile("m_bf21", [P, P, PACK], BF16, "dense00")[:])
+        lay_m(nc.scalar, 2, 0, on_y_last("m_bf20", [P, P, PACK], BF16, 1024)[:])
+        lay_m(nc.vector, 2, 1, new_tile("m_bf21", [P, P, PACK], BF16, "dense01")[:])
         for h in (HIGH, LOW):
             copy_out(f"dense1{h}", acc[1, h])
             scatter(1, f"dense1{h}", listed(h))

@@ -24,7 +24,7 @@ HALF = N // 2
 LOW, HIGH = 0, 1
 ALIGN = 256
 X_SHARES = (80, 64)
-EARLY = 80
+EARLY = 64
 Y_LAST = 4096
 Y_HIGH = 8192
 G_SPLIT = 256

@@ -27,7 +27,7 @@ X_SHARES = (80, 64)
 EARLY = 64
 Y_LAST = 4096
 Y_HIGH = 8192
-G_SPLIT = 256
+G_SPLIT = 224
 
 
 def tile_attend_gnce_w_kernel(tc, xT, wT, y, wt, xm, offs, out):
@@ -180,30 +180,32 @@ def tile_attend_gnce_w_kernel(tc, xT, wT, y, wt, xm, offs, out):
                 stop=True,
             )
 
-        sig = [new_tile(f"sig{c}", [P, PACK, N], F32) for c in range(CHUNKS)]
+        sig = [new_tile(f"sig{c}", [P, 2, PACK, HALF], F32) for c in range(CHUNKS)]
 
-        def scores(c, t, k, halves):
-            bank = new_bank(k)
+        def scores(c, k, places, halves):
+            bank = new_bank(k)[:, 0 : len(places) * len(halves) * HALF]
+            parts = bank.rearrange("p (h t n) -> p h t n", h=len(halves), t=len(places))
             for h in halves:
-                score_pass(bank[:, half(h)], c, t, h)
-            cols = slice(min(halves) * HALF, (max(halves) + 1) * HALF)
-            nc.scalar.activation(out=sig[c][:, t, cols], in_=bank[:, cols], func=ACT.Sigmoid, scale=-1.0)
+                for t in places:
+                    score_pass(parts[:, h - halves.start, t - places.start, :], c, t, h)
+            dst = sig[c][:, halves.start : halves.stop, places.start : places.stop, :]
+            nc.scalar.activation(out=dst, in_=parts, func=ACT.Sigmoid, scale=-1.0)
 
+        low, high, both = range(LOW, LOW + 1), range(HIGH, HIGH + 1), range(2)
         pairs = (slice(0, 2), slice(2, PACK))
         for places, share in zip(pairs, X_SHARES):
             lay_x(nc.vector, 0, x_first, 0, 0, share, places)
             lay_x(nc.scalar, 0, x_first, 0, share, P, places)
         quantise_x(0)
-        for t in range(PACK):
-            for i, h in enumerate((LOW, HIGH)):
-                scores(0, t, 2 * t + i, (h,))
+        for k, (places, halves) in enumerate([(range(t, t + 1), h) for t in range(2) for h in (low, high)] + [(range(2, 3), low), (range(3, PACK), low), (range(2, PACK), high)]):
+            scores(0, k, places, halves)
         lay_x(nc.vector, 1, x_early, 0, 0, EARLY, slice(0, PACK))
         for places in pairs:
             lay_x(nc.vector, 1, x_last, EARLY, EARLY, P, places)
         quantise_x(1)
 
         sums, turned, g_turned = {}, {}, {}
-        sum_bank = {(0, 0): 6, (0, 1): 7, (1, 0): 0, (1, 1): 1}
+        sum_bank = {(0, 0): 3, (0, 1): 4, (1, 0): 5, (1, 1): 6}
 
         def turn(c, s, what, places):
             if (c, s) not in sums:
@@ -212,7 +214,7 @@ def tile_attend_gnce_w_kernel(tc, xT, wT, y, wt, xm, offs, out):
             for t in places:
                 cols = slice(s * P, (s + 1) * P)
                 if what == "s":
-                    src = sig[c][:, t, half(HIGH)][:, cols]
+                    src = sig[c][:, HIGH, t, cols]
                 else:
                     src = y_raw[c, HIGH][:, t, cols]
                 turned[c, s] = turned[c, s] + 1
@@ -238,13 +240,14 @@ def tile_attend_gnce_w_kernel(tc, xT, wT, y, wt, xm, offs, out):
 
         g_laid = {}
 
-        def turn_back(c, s, k):
-            bank = new_bank(k)[:, 0 : 2 * P].rearrange("p (u n) -> p u n", u=2)
-            words = g_turned[c, s][:].rearrange("p w e -> p (w e)").bitcast(F32)
-            for u in range(2):
-                nc.tensor.transpose(bank[:, u, :], words[:, u * P : (u + 1) * P], identity[:])
-            dst = g_laid[c, HIGH][:, s * P : (s + 1) * P, :].rearrange("p n t -> p (n t)").bitcast(F32)
-            nc.scalar.copy(out=dst.rearrange("p (n u) -> p n u", u=2), in_=bank.rearrange("p u n -> p n u"))
+        def turn_back(c, blocks, k):
+            bank = new_bank(k)[:, 0 : len(blocks) * 2 * P].rearrange("p (s u n) -> p s u n", u=2, n=P)
+            for s in blocks:
+                words = g_turned[c, s][:].rearrange("p w e -> p (w e)").bitcast(F32)
+                for u in range(2):
+                    nc.tensor.transpose(bank[:, s - blocks.start, u, :], words[:, u * P : (u + 1) * P], identity[:])
+            dst = g_laid[c, HIGH][:, blocks.start * P : blocks.stop * P, :].rearrange("p n t -> p (n t)").bitcast(F32)
+            nc.scalar.copy(out=dst.rearrange("p (s n u) -> p s n u", u=2, n=P), in_=bank.rearrange("p s u n -> p s n u"))
 
         weighted = {}
         g_rows = {}
@@ -254,7 +257,7 @@ def tile_attend_gnce_w_kernel(tc, xT, wT, y, wt, xm, offs, out):
                 weighted[c, t] = part[:, t % 2, :]
                 nc.vector.tensor_scalar(
                     out=weighted[c, t],
-                    in0=sig[c][:, t, half(LOW)],
+                    in0=sig[c][:, LOW, t, :],
                     scalar1=1.0,
                     scalar2=minus[:, c, t : t + 1],
                     op0=ALU.subtract,
@@ -326,12 +329,8 @@ def tile_attend_gnce_w_kernel(tc, xT, wT, y, wt, xm, offs, out):
         def store(b):
             nc.sync.dma_start(out=out[b * P : (b + 1) * P, :], in_=window[b][:])
 
-        for h in (LOW, HIGH):
-            scores(1, 0, h, (h,))
-        for t in range(1, PACK - 1):
-            scores(1, t, 1 + t, (HIGH, LOW))
-        for h in (LOW, HIGH):
-            scores(1, PACK - 1, 4 + h, (h,))
+        for k, (places, halves) in zip((7, 0, 1, 2), ((range(0, 2), low), (range(2, PACK), low), (range(0, 2), high), (range(2, PACK), high))):
+            scores(1, k, places, halves)
         for u in range(2):
             weigh(0, u, on_x_last(f"weighted0{u}", [P, 2, HALF], F32, u))
         gradient(0, new_tile("g_rows0", [P, PACK, HALF], BF16))
@@ -347,7 +346,6 @@ def tile_attend_gnce_w_kernel(tc, xT, wT, y, wt, xm, offs, out):
         lay_g(nc.scalar, 0, slice(0, HALF))
         g_laid.update({(c, HIGH): new_tile(f"g_laid{c}1", [P, HALF, PACK], BF16) for c in range(CHUNKS)})
         turn(1, 0, "y", range(PACK))
-        turn_back(0, 0, 2)
         turn(1, 0, "s", range(PACK))
         turn(1, 1, "y", range(1))
         turn(1, 1, "s", range(PACK))
@@ -359,15 +357,16 @@ def tile_attend_gnce_w_kernel(tc, xT, wT, y, wt, xm, offs, out):
         g_laid[1, LOW] = new_tile("g_laid10", [P, HALF, PACK], BF16)
         lay_m(nc.vector, 0, 1, on_y_last("m_bf01", [P, P, PACK], BF16, 2048)[:])
         lay_g(nc.scalar, 1, slice(0, G_SPLIT))
-        turn_back(0, 1, 3)
+        lay_g(nc.vector, 1, slice(G_SPLIT, HALF))
+        turn_back(0, range(2), 7)
         for s in range(2):
-            turn_back(1, s, 6 + s)
+            turn_back(1, range(s, s + 1), s)
         scales = on_y_last("g_scales", [P, 2, CHUNKS, HALF], U8, 0)
         quantise_g(0, LOW, scales[:, LOW, 0])
         m_first = on_y_last("m_codes0", [P, CHUNKS * P], U32, 1024)
         for c in range(CHUNKS):
             quantise_m(0, range(c, c + 1), m_first[:, c * P : (c + 1) * P], m_bf[0, c].rearrange("p n t -> p (n t)"))
-        acc.update({(0, HIGH): new_bank(4)[:, 0:HALF], (0, LOW): new_bank(5)[:, 0:HALF]})
+        acc.update({(0, HIGH): new_bank(2)[:, 0:HALF], (0, LOW): new_bank(3)[:, 0:HALF]})
         for h in (LOW, HIGH):
             for c in range(CHUNKS):
                 if c + h:
@@ -380,7 +379,7 @@ def tile_attend_gnce_w_kernel(tc, xT, wT, y, wt, xm, offs, out):
             codes = new_tile(f"m_codes{b}{c}", [P, P], U32, tag)
             quantise_m(b, range(c, c + 1), codes[:], m_bf[b, c].rearrange("p n t -> p (n t)"))
 
-        acc.update({(1, HIGH): new_bank(2)[:, 0:HALF], (1, LOW): new_bank(3)[:, 0:HALF]})
+        acc.update({(1, HIGH): new_bank(4)[:, 0:HALF], (1, LOW): new_bank(5)[:, 0:HALF]})
         lay_m(nc.vector, 1, 0, new_tile("m_bf10", [P, P, PACK], BF16, "g_laid01")[:])
         quantise_piece(1, 1, "g_laid10")
         scatter(0, "dense00", listed(LOW))
@@ -412,10 +411,10 @@ def tile_attend_gnce_w_kernel(tc, xT, wT, y, wt, xm, offs, out):
             scatter(1, f"dense1{h}", listed(h))
             quantise_piece(2, h)
         store(1)
-        bank = products(2, 0)
+        bank = products(2, 6)
         lay_m(nc.scalar, 3, 0, new_tile("m_bf30", [P, P, PACK], BF16, "m_codes10")[:])
         lay_m(nc.vector, 3, 1, new_tile("m_bf31", [P, P, PACK], BF16, "dense11")[:])
         for c in range(CHUNKS):
             quantise_piece(3, c)
         output(2, bank)
-        output(3, products(3, 1))
+        output(3, products(3, 7))

@@ -25,9 +25,10 @@ LOW, HIGH = 0, 1
 ALIGN = 256
 X_SHARES = (80, 64)
 EARLY = 64
+M_SPLIT = 96
 Y_LAST = 4096
-Y_HIGH = 8192
-G_SPLIT = 224
+POOL_COLS = 112
+G_SPLIT = 144
 
 
 def tile_attend_gnce_w_kernel(tc, xT, wT, y, wt, xm, offs, out):
@@ -47,6 +48,8 @@ def tile_attend_gnce_w_kernel(tc, xT, wT, y, wt, xm, offs, out):
         def copy_on(engine, dst, src):
             if engine is nc.vector:
                 nc.vector.tensor_copy(out=dst, in_=src)
+            elif engine is nc.gpsimd:
+                nc.gpsimd.tensor_scalar(out=dst, in0=src, scalar1=1.0, scalar2=0.0, op0=ALU.mult, op1=ALU.add)
             else:
                 nc.scalar.copy(out=dst, in_=src)
 
@@ -128,8 +131,7 @@ def tile_attend_gnce_w_kernel(tc, xT, wT, y, wt, xm, offs, out):
                 m_raw[b, c] = part[:, :, (b - blocks.start) * P : (b - blocks.start + 1) * P]
 
         load_y(0, LOW)
-        y_high = reuse.tile([P, PACK, HALF], F32, name="y_high", align_bytes=ALIGN, offset=Y_HIGH)
-        y_raw[0, HIGH] = load(y_high, y_rows[0, :, :, half(HIGH)])
+        load_y(0, HIGH)
         y_last = reuse.tile([P, PACK, HALF], F32, name="y_last", align_bytes=ALIGN, offset=Y_LAST)
         y_raw[1, HIGH] = load(y_last, y_rows[1, :, :, half(HIGH)])
         load_y(1, LOW)
@@ -180,7 +182,7 @@ def tile_attend_gnce_w_kernel(tc, xT, wT, y, wt, xm, offs, out):
                 stop=True,
             )
 
-        sig = [new_tile(f"sig{c}", [P, 2, PACK, HALF], F32) for c in range(CHUNKS)]
+        sig = {(c, h): new_tile(f"sig{c}{h}", [P, 1, PACK, HALF], F32) for c in range(CHUNKS) for h in range(2)}
 
         def scores(c, k, places, halves):
             bank = new_bank(k)[:, 0 : len(places) * len(halves) * HALF]
@@ -188,7 +190,7 @@ def tile_attend_gnce_w_kernel(tc, xT, wT, y, wt, xm, offs, out):
             for h in halves:
                 for t in places:
                     score_pass(parts[:, h - halves.start, t - places.start, :], c, t, h)
-            dst = sig[c][:, halves.start : halves.stop, places.start : places.stop, :]
+            dst = sig[c, halves.start][:, :, places.start : places.stop, :]
             nc.scalar.activation(out=dst, in_=parts, func=ACT.Sigmoid, scale=-1.0)
 
         low, high, both = range(LOW, LOW + 1), range(HIGH, HIGH + 1), range(2)
@@ -214,7 +216,7 @@ def tile_attend_gnce_w_kernel(tc, xT, wT, y, wt, xm, offs, out):
             for t in places:
                 cols = slice(s * P, (s + 1) * P)
                 if what == "s":
-                    src = sig[c][:, HIGH, t, cols]
+                    src = sig[c, HIGH][:, 0, t, cols]
                 else:
                     src = y_raw[c, HIGH][:, t, cols]
                 turned[c, s] = turned[c, s] + 1
@@ -257,7 +259,7 @@ def tile_attend_gnce_w_kernel(tc, xT, wT, y, wt, xm, offs, out):
                 weighted[c, t] = part[:, t % 2, :]
                 nc.vector.tensor_scalar(
                     out=weighted[c, t],
-                    in0=sig[c][:, LOW, t, :],
+                    in0=sig[c, LOW][:, 0, t, :],
                     scalar1=1.0,
                     scalar2=minus[:, c, t : t + 1],
                     op0=ALU.subtract,
@@ -334,30 +336,31 @@ def tile_attend_gnce_w_kernel(tc, xT, wT, y, wt, xm, offs, out):
         for u in range(2):
             weigh(0, u, on_x_last(f"weighted0{u}", [P, 2, HALF], F32, u))
         gradient(0, new_tile("g_rows0", [P, PACK, HALF], BF16))
-        weigh(1, 0, on_x_last("weighted10", [P, 2, HALF], F32, 0))
+        for u in range(2):
+            weigh(1, u, on_x_last(f"weighted1{u}", [P, 2, HALF], F32, u))
         for s in range(2):
             turn(0, s, "y", range(PACK))
             turn(0, s, "s", range(PACK))
         words = [P, 2 * P, 2]
         gradient_turned(0, 0, new_tile("g_turned00", words, BF16))
-        weigh(1, 1, reuse.tile([P, 2, HALF], F32, name="weighted11", tag="y_high0", align_bytes=ALIGN, offset=Y_HIGH))
         gradient_turned(0, 1, new_tile("g_turned01", words, BF16))
-        g_laid[0, LOW] = new_tile("g_laid00", [P, HALF, PACK], BF16)
-        lay_g(nc.scalar, 0, slice(0, HALF))
+        g_laid[0, LOW] = new_tile("g_laid00", [P, HALF, PACK], BF16, "sig10")
+        lay_g(nc.gpsimd, 0, slice(0, POOL_COLS))
+        lay_g(nc.scalar, 0, slice(POOL_COLS, HALF))
         g_laid.update({(c, HIGH): new_tile(f"g_laid{c}1", [P, HALF, PACK], BF16) for c in range(CHUNKS)})
         turn(1, 0, "y", range(PACK))
         turn(1, 0, "s", range(PACK))
         turn(1, 1, "y", range(1))
         turn(1, 1, "s", range(PACK))
         turn(1, 1, "y", range(1, PACK))
-        gradient(1, new_tile("g_rows1", [P, PACK, HALF], BF16, "sig0"))
+        gradient(1, new_tile("g_rows1", [P, PACK, HALF], BF16, "sig01"))
         gradient_turned(1, 0, on_x_last("g_turned10", words, BF16, 0))
-        gradient_turned(1, 1, reuse.tile(words, BF16, name="g_turned11", tag="y_high0", align_bytes=ALIGN, offset=Y_HIGH))
+        gradient_turned(1, 1, on_x_last("g_turned11", words, BF16, 1))
         lay_m(nc.scalar, 0, 0, new_tile("m_bf00", [P, P, PACK], BF16)[:])
         g_laid[1, LOW] = new_tile("g_laid10", [P, HALF, PACK], BF16)
-        lay_m(nc.vector, 0, 1, on_y_last("m_bf01", [P, P, PACK], BF16, 2048)[:])
+        lay_m(nc.scalar, 0, 1, new_tile("m_bf01", [P, P, PACK], BF16)[:])
+        lay_g(nc.gpsimd, 1, slice(G_SPLIT, HALF))
         lay_g(nc.scalar, 1, slice(0, G_SPLIT))
-        lay_g(nc.vector, 1, slice(G_SPLIT, HALF))
         turn_back(0, range(2), 7)
         for s in range(2):
             turn_back(1, range(s, s + 1), s)
@@ -373,14 +376,16 @@ def tile_attend_gnce_w_kernel(tc, xT, wT, y, wt, xm, offs, out):
                     quantise_g(c, h, scales[:, h, c], 1 + c * h)
                 product(0, c, h, c == 0)
         copy_out("dense00", acc[0, LOW])
-        lay_m(nc.scalar, 1, 1, reuse.tile([P, P, PACK], BF16, name="m_bf11", tag="y_high0", align_bytes=ALIGN, offset=Y_HIGH)[:])
+        m_bf[1, 1] = on_x_last("m_bf11", [P, P, PACK], BF16, 1)[:]
+        for engine, cols in ((nc.scalar, slice(0, M_SPLIT)), (nc.vector, slice(M_SPLIT, P))):
+            side_by_side(engine, m_bf[1, 1][:, cols, :], m_raw[1, 1][:, :, cols])
 
         def quantise_piece(b, c, tag=None):
             codes = new_tile(f"m_codes{b}{c}", [P, P], U32, tag)
             quantise_m(b, range(c, c + 1), codes[:], m_bf[b, c].rearrange("p n t -> p (n t)"))
 
         acc.update({(1, HIGH): new_bank(4)[:, 0:HALF], (1, LOW): new_bank(5)[:, 0:HALF]})
-        lay_m(nc.vector, 1, 0, new_tile("m_bf10", [P, P, PACK], BF16, "g_laid01")[:])
+        lay_m(nc.vector, 1, 0, new_tile("m_bf10", [P, P, PACK], BF16, "g_laid11")[:])
         quantise_piece(1, 1, "g_laid10")
         scatter(0, "dense00", listed(LOW))
         copy_out("dense01", acc[0, HIGH])

@@ -28,7 +28,7 @@ EARLY = 64
 M_SPLIT = 96
 Y_LAST = 4096
 POOL_COLS = 112
-G_SPLIT = 144
+G_SPLIT = 128
 
 
 def tile_attend_gnce_w_kernel(tc, xT, wT, y, wt, xm, offs, out):
@@ -242,13 +242,13 @@ def tile_attend_gnce_w_kernel(tc, xT, wT, y, wt, xm, offs, out):
 
         g_laid = {}
 
-        def turn_back(c, blocks, k):
+        def turn_back(c, blocks, k, laid):
             bank = new_bank(k)[:, 0 : len(blocks) * 2 * P].rearrange("p (s u n) -> p s u n", u=2, n=P)
             for s in blocks:
                 words = g_turned[c, s][:].rearrange("p w e -> p (w e)").bitcast(F32)
                 for u in range(2):
                     nc.tensor.transpose(bank[:, s - blocks.start, u, :], words[:, u * P : (u + 1) * P], identity[:])
-            dst = g_laid[c, HIGH][:, blocks.start * P : blocks.stop * P, :].rearrange("p n t -> p (n t)").bitcast(F32)
+            dst = laid[:].rearrange("p n t -> p (n t)").bitcast(F32)
             nc.scalar.copy(out=dst.rearrange("p (s n u) -> p s n u", u=2, n=P), in_=bank.rearrange("p s u n -> p s n u"))
 
         weighted = {}
@@ -289,13 +289,12 @@ def tile_attend_gnce_w_kernel(tc, xT, wT, y, wt, xm, offs, out):
 
         g_codes, g_scales = {}, {}
 
-        def quantise_g(c, h, scales, parts=1):
+        def quantise_g(c, h, scales, parts):
             g_codes[c, h] = new_tile(f"g_codes{c}{h}", [P, HALF], U32)
             g_scales[c, h] = scales
-            for i in range(parts):
-                cols = slice(i * HALF // parts, (i + 1) * HALF // parts)
-                laid = g_laid[c, h][:, cols, :].rearrange("p n t -> p (n t)")
-                quantise(g_codes[c, h][:, cols], scales[:, cols], laid, E5M2)
+            for i, laid in enumerate(parts):
+                cols = slice(i * HALF // len(parts), (i + 1) * HALF // len(parts))
+                quantise(g_codes[c, h][:, cols], scales[:, cols], laid[:].rearrange("p n t -> p (n t)"), E5M2)
 
         m_bf, m_codes, m_scales, acc, dense = {}, {}, {}, {}, {}
 
@@ -347,7 +346,6 @@ def tile_attend_gnce_w_kernel(tc, xT, wT, y, wt, xm, offs, out):
         g_laid[0, LOW] = new_tile("g_laid00", [P, HALF, PACK], BF16, "sig10")
         lay_g(nc.gpsimd, 0, slice(0, POOL_COLS))
         lay_g(nc.scalar, 0, slice(POOL_COLS, HALF))
-        g_laid.update({(c, HIGH): new_tile(f"g_laid{c}1", [P, HALF, PACK], BF16) for c in range(CHUNKS)})
         turn(1, 0, "y", range(PACK))
         turn(1, 0, "s", range(PACK))
         turn(1, 1, "y", range(1))
@@ -356,24 +354,26 @@ def tile_attend_gnce_w_kernel(tc, xT, wT, y, wt, xm, offs, out):
         gradient(1, new_tile("g_rows1", [P, PACK, HALF], BF16, "sig01"))
         gradient_turned(1, 0, on_x_last("g_turned10", words, BF16, 0))
         gradient_turned(1, 1, on_x_last("g_turned11", words, BF16, 1))
-        lay_m(nc.scalar, 0, 0, new_tile("m_bf00", [P, P, PACK], BF16)[:])
+        first_m = new_tile("m_bf0", [P, CHUNKS, P, PACK], BF16)
+        lay_m(nc.scalar, 0, 0, first_m[:, 0])
         g_laid[1, LOW] = new_tile("g_laid10", [P, HALF, PACK], BF16)
-        lay_m(nc.scalar, 0, 1, new_tile("m_bf01", [P, P, PACK], BF16)[:])
+        lay_m(nc.scalar, 0, 1, first_m[:, 1])
         lay_g(nc.gpsimd, 1, slice(G_SPLIT, HALF))
         lay_g(nc.scalar, 1, slice(0, G_SPLIT))
-        turn_back(0, range(2), 7)
+        g_laid[0, HIGH] = new_tile("g_laid01", [P, HALF, PACK], BF16)
+        turn_back(0, range(2), 7, g_laid[0, HIGH])
+        last_words = [new_tile(f"last_words{s}", [P, P, PACK], BF16) for s in range(2)]
         for s in range(2):
-            turn_back(1, range(s, s + 1), s)
+            turn_back(1, range(s, s + 1), s, last_words[s])
         scales = on_y_last("g_scales", [P, 2, CHUNKS, HALF], U8, 0)
-        quantise_g(0, LOW, scales[:, LOW, 0])
+        quantise_g(0, LOW, scales[:, LOW, 0], [g_laid[0, LOW]])
         m_first = on_y_last("m_codes0", [P, CHUNKS * P], U32, 1024)
-        for c in range(CHUNKS):
-            quantise_m(0, range(c, c + 1), m_first[:, c * P : (c + 1) * P], m_bf[0, c].rearrange("p n t -> p (n t)"))
+        quantise_m(0, range(CHUNKS), m_first[:], first_m[:].rearrange("p c n t -> p (c n t)"))
         acc.update({(0, HIGH): new_bank(2)[:, 0:HALF], (0, LOW): new_bank(3)[:, 0:HALF]})
         for h in (LOW, HIGH):
             for c in range(CHUNKS):
                 if c + h:
-                    quantise_g(c, h, scales[:, h, c], 1 + c * h)
+                    quantise_g(c, h, scales[:, h, c], last_words if c * h else [g_laid[c, h]])
                 product(0, c, h, c == 0)
         copy_out("dense00", acc[0, LOW])
         m_bf[1, 1] = on_x_last("m_bf11", [P, P, PACK], BF16, 1)[:]
@@ -385,7 +385,7 @@ def tile_attend_gnce_w_kernel(tc, xT, wT, y, wt, xm, offs, out):
             quantise_m(b, range(c, c + 1), codes[:], m_bf[b, c].rearrange("p n t -> p (n t)"))
 
         acc.update({(1, HIGH): new_bank(4)[:, 0:HALF], (1, LOW): new_bank(5)[:, 0:HALF]})
-        lay_m(nc.vector, 1, 0, new_tile("m_bf10", [P, P, PACK], BF16, "g_laid11")[:])
+        lay_m(nc.vector, 1, 0, new_tile("m_bf10", [P, P, PACK], BF16, "last_words0")[:])
         quantise_piece(1, 1, "g_laid10")
         scatter(0, "dense00", listed(LOW))
         copy_out("dense01", acc[0, HIGH])

@@ -25,10 +25,10 @@ LOW, HIGH = 0, 1
 ALIGN = 256
 X_SHARES = (80, 64)
 EARLY = 64
-M_SPLIT = 96
+M_SPLIT = 80
 Y_LAST = 4096
 POOL_COLS = 112
-G_SPLIT = 128
+G_SPLIT = 112
 
 
 def tile_attend_gnce_w_kernel(tc, xT, wT, y, wt, xm, offs, out):
@@ -309,15 +309,15 @@ def tile_attend_gnce_w_kernel(tc, xT, wT, y, wt, xm, offs, out):
                 m_scales[b, c] = scales[:, i * P : (i + 1) * P]
             quantise(codes, scales[:], laid, E4M3)
 
-        def product(b, c, h, opens):
+        def product(b, c, h, opens, closes=None, cols=slice(0, HALF)):
             nc.tensor.matmul_mx(
-                out=acc[b, h],
+                out=acc[b, h][:, cols],
                 lhsT=m_codes[b, c].bitcast(E4M3),
                 lhsT_scale=m_scales[b, c],
-                rhs=g_codes[c, h][:].bitcast(E5M2),
-                rhs_scale=g_scales[c, h],
+                rhs=g_codes[c, h][:, cols].bitcast(E5M2),
+                rhs_scale=g_scales[c, h][:, cols],
                 start=opens,
-                stop=not opens,
+                stop=not opens if closes is None else closes,
             )
 
         def copy_out(name, src):
@@ -372,9 +372,14 @@ def tile_attend_gnce_w_kernel(tc, xT, wT, y, wt, xm, offs, out):
         acc.update({(0, HIGH): new_bank(2)[:, 0:HALF], (0, LOW): new_bank(3)[:, 0:HALF]})
         for h in (LOW, HIGH):
             for c in range(CHUNKS):
-                if c + h:
-                    quantise_g(c, h, scales[:, h, c], last_words if c * h else [g_laid[c, h]])
-                product(0, c, h, c == 0)
+                if c == 0:
+                    if h:
+                        quantise_g(c, h, scales[:, h, c], [g_laid[c, h]])
+                    product(0, c, h, True)
+                else:
+                    quantise_g(c, h, scales[:, h, c], last_words if h else [g_laid[c, h][:, 0:P, :], g_laid[c, h][:, P:HALF, :]])
+                    for i in range(2):
+                        product(0, c, h, False, i == 1, slice(i * P, (i + 1) * P))
         copy_out("dense00", acc[0, LOW])
         m_bf[1, 1] = on_x_last("m_bf11", [P, P, PACK], BF16, 1)[:]
         for engine, cols in ((nc.scalar, slice(0, M_SPLIT)), (nc.vector, slice(M_SPLIT, P))):

from contextlib import ExitStack

import concourse.mybir as mybir
from concourse.masks import make_identity

D, R, T, N = 512, 1024, 2048, 512
FLOPS = 2 * 2 * D * R * N

F32 = mybir.dt.float32
BF16 = mybir.dt.bfloat16
U32 = mybir.dt.uint32
U16 = mybir.dt.uint16
U8 = mybir.dt.uint8
E4M3 = mybir.dt.float8_e4m3fn_x4
E5M2 = mybir.dt.float8_e5m2_x4
ACT = mybir.ActivationFunctionType
ALU = mybir.AluOpType

P = 128
PACK = 4
K_PASS = P * PACK
CHUNKS = R // K_PASS
HALF = N // 2
LOW, HIGH = 0, 1
ALIGN = 256
X_SHARES = (80, 64)
EARLY = 64
M_SPLIT = 80
Y_LAST = 4096
POOL_COLS = 112
G_SPLIT = 112


def tile_attend_gnce_w_kernel(tc, xT, wT, y, wt, xm, offs, out):
    nc = tc.nc
    with ExitStack() as ctx:
        lists = ctx.enter_context(tc.tile_pool(name="lists", bufs=1))
        keep = ctx.enter_context(tc.tile_pool(name="keep", bufs=1))
        reuse = ctx.enter_context(tc.tile_pool(name="reuse", bufs=1))
        banks = ctx.enter_context(tc.psum_pool(name="banks", bufs=1))

        def new_bank(k):
            return banks.tile([P, N], F32, name=f"bank{k}", tag=f"bank{k}")

        def new_tile(name, shape, dtype, tag=None):
            return keep.tile(shape, dtype, name=name, tag=tag or name, align_bytes=ALIGN)

        def copy_on(engine, dst, src):
            if engine is nc.vector:
                nc.vector.tensor_copy(out=dst, in_=src)
            elif engine is nc.gpsimd:
                nc.gpsimd.tensor_scalar(out=dst, in0=src, scalar1=1.0, scalar2=0.0, op0=ALU.mult, op1=ALU.add)
            else:
                nc.scalar.copy(out=dst, in_=src)

        def side_by_side(engine, dst, src):
            copy_on(engine, dst.rearrange("p (n i) t -> p n t i", i=4), src.rearrange("p t (n i) -> p n t i", i=4))

        def quantise(codes, scales, laid, fmt):
            nc.vector.quantize_mx(out=codes.bitcast(fmt), scales=scales, in_=laid)

        def half(h):
            return slice(h * HALF, (h + 1) * HALF)

        apart = P // CHUNKS
        wt_rows = new_tile("wt_rows", [P, K_PASS], F32)
        nc.scalar.dma_start(out=wt_rows[0:P:apart, :], in_=wt[0].rearrange("(c k) o -> c (k o)", c=CHUNKS))
        warm_in = keep.tile([P, 1], F32, name="warm_in")
        warm_out = keep.tile([P, 1], F32, name="warm_out")
        nc.gpsimd.memset(warm_in[:], 0.0)
        nc.scalar.activation(out=warm_out[:], in_=warm_in[:], func=ACT.Sigmoid)
        identity = keep.tile([P, P], F32, name="identity")
        make_identity(nc, identity[:])
        wt_dealt = keep.tile([P, PACK, P], F32, name="wt_dealt")
        nc.gpsimd.memset(wt_dealt[:], 0.0)
        for c in range(CHUNKS):
            row = slice(c * apart, c * apart + 1)
            nc.scalar.activation(
                out=wt_dealt[row, :, :],
                in_=wt_rows[row, :].rearrange("c (p t) -> c t p", t=PACK),
                func=ACT.Copy,
                scale=-1.0,
            )
        wt_bank = new_bank(7)[:].rearrange("p (t k) -> p t k", t=PACK)
        for t in range(PACK):
            nc.tensor.transpose(wt_bank[:, t, :], wt_dealt[:, t, :], identity[:])
        minus = keep.tile([P, CHUNKS, PACK], F32, name="minus")
        nc.scalar.copy(out=minus[:], in_=wt_bank.rearrange("p t (c k) -> p c t k", c=CHUNKS)[:, :, :, 0])

        def place_of(bank, t):
            return bank[:].rearrange("p (e u m) -> p e u m", e=2, u=2)[:, t % 2, t // 2, :]

        def by_words(bank):
            return bank[:].rearrange("p (e w) -> p w e", e=2)

        minus_row = [new_tile(f"minus_row{c}", [P, 2 * P, 2], F32) for c in range(CHUNKS)]
        for c in range(CHUNKS):
            bank = new_bank(5 + c)
            for t in range(PACK):
                nc.tensor.transpose(place_of(bank, t), minus[:, c, t : t + 1].to_broadcast([P, P]), identity[:])
            nc.vector.tensor_copy(out=minus_row[c][:], in_=by_words(bank))

        def load(tile, src):
            nc.sync.dma_start(out=tile[:], in_=src)
            return tile

        def load_new(name, src):
            return load(new_tile(name, list(src.shape), F32), src)

        offsets = lists.tile([P, N // 16], U16, name="offsets")
        w_rows = wT.rearrange("(p t) c -> p t c", t=PACK)
        x_rows = xT[0].rearrange("(p j) r -> p j r", j=PACK)
        y_rows = y[0].rearrange("(c p t) i -> c p t i", c=CHUNKS, t=PACK)
        m_rows = xm[0].rearrange("(c p t) d -> c p t d", c=CHUNKS, t=PACK)

        table = [load_new("table0", w_rows[:, 0, :])]
        nc.sync.dma_start(offsets[:], offs)
        table.extend(load_new(f"table{t}", w_rows[:, t, :]) for t in range(1, PACK))
        x_first = load_new("x_first", x_rows[:, :, 0:K_PASS])
        x_early = load_new("x_early", x_rows[:, :, K_PASS : K_PASS + PACK * EARLY])
        x_last = reuse.tile([P, PACK, PACK * (P - EARLY)], F32, name="x_last", align_bytes=ALIGN, offset=0)
        load(x_last, x_rows[:, :, K_PASS + PACK * EARLY : R])
        y_raw, m_raw = {}, {}

        def load_y(c, h):
            y_raw[c, h] = load_new(f"y{c}{h}", y_rows[c, :, :, half(h)])

        def load_m(c, blocks):
            part = load_new(f"m_part{c}{blocks.start}", m_rows[c, :, :, blocks.start * P : blocks.stop * P])
            for b in blocks:
                m_raw[b, c] = part[:, :, (b - blocks.start) * P : (b - blocks.start + 1) * P]

        load_y(0, LOW)
        load_y(0, HIGH)
        y_last = reuse.tile([P, PACK, HALF], F32, name="y_last", align_bytes=ALIGN, offset=Y_LAST)
        y_raw[1, HIGH] = load(y_last, y_rows[1, :, :, half(HIGH)])
        load_y(1, LOW)
        for c in range(CHUNKS):
            load_m(c, range(1))
        for blocks in (range(1, 2), range(2, D // P)):
            for c in range(CHUNKS):
                load_m(c, blocks)

        window = [new_tile(f"window{b}", [P, T], F32) for b in range(D // P)]
        for b in range(D // P):
            (nc.vector if b < 2 else nc.gpsimd).memset(window[b][:], 0.0)

        def listed(h):
            return offsets[:, h * HALF // 16 : (h + 1) * HALF // 16]

        w_bf = [new_tile(f"w_bf{h}", [P, HALF, PACK], BF16) for h in range(2)]
        for t in range(PACK):
            nc.scalar.activation(out=w_bf[HIGH][:, :, t], in_=table[t][:].indirect(listed(HIGH)), func=ACT.Copy)
            nc.vector.tensor_copy(out=w_bf[LOW][:, :, t], in_=table[t][:].indirect(listed(LOW)))
        w_codes = [new_tile(f"w_codes{h}", [P, HALF], U32) for h in range(2)]
        w_scales = {HIGH: new_tile("w_scales1", [P, HALF], U8), LOW: new_tile("w_scales0", [P, HALF], U8, "table3")}
        for h in (HIGH, LOW):
            quantise(w_codes[h][:], w_scales[h][:], w_bf[h][:].rearrange("p n t -> p (n t)"), E4M3)

        x_bf = [new_tile(f"x_bf{c}", [P, PACK, P, PACK], BF16) for c in range(CHUNKS)]
        x_codes = [new_tile(f"x_codes{c}", [P, K_PASS], U32) for c in range(CHUNKS)]
        x_scales = [new_tile(f"x_scales{c}", [P, K_PASS], U8) for c in range(CHUNKS)]

        def lay_x(engine, c, raw, first, lo, hi, places):
            src = raw[:].rearrange("p j (m t) -> p m j t", t=PACK)[:, lo - first : hi - first, :, places]
            copy_on(engine, x_bf[c][:, places, lo:hi, :].rearrange("p t m j -> p m j t"), src)

        def quantise_x(c):
            for lo, hi in ((0, 1), (1, 2), (2, PACK)):
                cols = slice(lo * P, hi * P)
                laid = x_bf[c][:, lo:hi, :, :].rearrange("p t m j -> p (t m j)")
                quantise(x_codes[c][:, cols], x_scales[c][:, cols], laid, E4M3)

        def score_pass(dst, c, t, h):
            nc.tensor.matmul_mx(
                out=dst,
                lhsT=x_codes[c][:, t * P : (t + 1) * P].bitcast(E4M3),
                lhsT_scale=x_scales[c][:, t * P : (t + 1) * P],
                rhs=w_codes[h][:].bitcast(E4M3),
                rhs_scale=w_scales[h][:],
                start=True,
                stop=True,
            )

        sig = {(c, h): new_tile(f"sig{c}{h}", [P, 1, PACK, HALF], F32) for c in range(CHUNKS) for h in range(2)}

        def scores(c, k, places, halves):
            bank = new_bank(k)[:, 0 : len(places) * len(halves) * HALF]
            parts = bank.rearrange("p (h t n) -> p h t n", h=len(halves), t=len(places))
            for h in halves:
                for t in places:
                    score_pass(parts[:, h - halves.start, t - places.start, :], c, t, h)
            dst = sig[c, halves.start][:, :, places.start : places.stop, :]
            nc.scalar.activation(out=dst, in_=parts, func=ACT.Sigmoid, scale=-1.0)

        low, high, both = range(LOW, LOW + 1), range(HIGH, HIGH + 1), range(2)
        pairs = (slice(0, 2), slice(2, PACK))
        for places, share in zip(pairs, X_SHARES):
            lay_x(nc.vector, 0, x_first, 0, 0, share, places)
            lay_x(nc.scalar, 0, x_first, 0, share, P, places)
        quantise_x(0)
        for k, (places, halves) in enumerate([(range(t, t + 1), h) for t in range(2) for h in (low, high)] + [(range(2, 3), low), (range(3, PACK), low), (range(2, PACK), high)]):
            scores(0, k, places, halves)
        lay_x(nc.vector, 1, x_early, 0, 0, EARLY, slice(0, PACK))
        for places in pairs:
            lay_x(nc.vector, 1, x_last, EARLY, EARLY, P, places)
        quantise_x(1)

        sums, turned, g_turned = {}, {}, {}
        sum_bank = {(0, 0): 3, (0, 1): 4, (1, 0): 5, (1, 1): 6}

        def turn(c, s, what, places):
            if (c, s) not in sums:
                sums[c, s] = new_bank(sum_bank[c, s])
                turned[c, s] = 0
            for t in places:
                cols = slice(s * P, (s + 1) * P)
                if what == "s":
                    src = sig[c, HIGH][:, 0, t, cols]
                else:
                    src = y_raw[c, HIGH][:, t, cols]
                turned[c, s] = turned[c, s] + 1
                nc.tensor.matmul(
                    place_of(sums[c, s], t),
                    lhsT=src,
                    rhs=identity[:],
                    start=turned[c, s] == 1,
                    stop=turned[c, s] == 2 * PACK,
                    is_transpose=True,
                )

        def gradient_turned(c, s, dst):
            g_turned[c, s] = dst
            nc.vector.scalar_tensor_tensor(
                out=g_turned[c, s][:],
                in0=by_words(sums[c, s]),
                scalar=1.0,
                in1=minus_row[c][:],
                op0=ALU.subtract,
                op1=ALU.mult,
            )

        g_laid = {}

        def turn_back(c, blocks, k, laid):
            bank = new_bank(k)[:, 0 : len(blocks) * 2 * P].rearrange("p (s u n) -> p s u n", u=2, n=P)
            for s in blocks:
                words = g_turned[c, s][:].rearrange("p w e -> p (w e)").bitcast(F32)
                for u in range(2):
                    nc.tensor.transpose(bank[:, s - blocks.start, u, :], words[:, u * P : (u + 1) * P], identity[:])
            dst = laid[:].rearrange("p n t -> p (n t)").bitcast(F32)
            nc.scalar.copy(out=dst.rearrange("p (s n u) -> p s n u", u=2, n=P), in_=bank.rearrange("p s u n -> p s n u"))

        weighted = {}
        g_rows = {}

        def weigh(c, u, part):
            for t in (2 * u, 2 * u + 1):
                weighted[c, t] = part[:, t % 2, :]
                nc.vector.tensor_scalar(
                    out=weighted[c, t],
                    in0=sig[c, LOW][:, 0, t, :],
                    scalar1=1.0,
                    scalar2=minus[:, c, t : t + 1],
                    op0=ALU.subtract,
                    op1=ALU.mult,
                )

        def on_x_last(name, shape, dtype, u):
            return reuse.tile(shape, dtype, name=name, tag=f"x_last{u}", align_bytes=ALIGN, offset=u * 2 * HALF * 4)

        def on_y_last(name, shape, dtype, shift):
            return reuse.tile(shape, dtype, name=name, align_bytes=ALIGN, offset=Y_LAST + shift)

        def gradient(c, rows):
            g_rows[c] = rows
            for t in range(PACK):
                nc.vector.scalar_tensor_tensor(
                    out=g_rows[c][:, t, :],
                    in0=y_raw[c, LOW][:, t, :],
                    scalar=minus[:, c, t : t + 1],
                    in1=weighted[c, t],
                    op0=ALU.mult,
                    op1=ALU.add,
                )

        def lay_g(engine, c, cols):
            side_by_side(engine, g_laid[c, LOW][:, cols, :], g_rows[c][:, :, cols])

        g_codes, g_scales = {}, {}

        def quantise_g(c, h, scales, parts):
            g_codes[c, h] = new_tile(f"g_codes{c}{h}", [P, HALF], U32)
            g_scales[c, h] = scales
            for i, laid in enumerate(parts):
                cols = slice(i * HALF // len(parts), (i + 1) * HALF // len(parts))
                quantise(g_codes[c, h][:, cols], scales[:, cols], laid[:].rearrange("p n t -> p (n t)"), E5M2)

        m_bf, m_codes, m_scales, acc, dense = {}, {}, {}, {}, {}

        def lay_m(engine, b, c, dst):
            m_bf[b, c] = dst
            side_by_side(engine, dst, m_raw[b, c])

        def quantise_m(b, chunks, codes, laid):
            scales = new_tile(f"m_scales{b}{chunks.start}", [P, len(chunks) * P], U8)
            for i, c in enumerate(chunks):
                m_codes[b, c] = codes[:, i * P : (i + 1) * P]
                m_scales[b, c] = scales[:, i * P : (i + 1) * P]
            quantise(codes, scales[:], laid, E4M3)

        def product(b, c, h, opens, closes=None, cols=slice(0, HALF)):
            nc.tensor.matmul_mx(
                out=acc[b, h][:, cols],
                lhsT=m_codes[b, c].bitcast(E4M3),
                lhsT_scale=m_scales[b, c],
                rhs=g_codes[c, h][:, cols].bitcast(E5M2),
                rhs_scale=g_scales[c, h][:, cols],
                start=opens,
                stop=not opens if closes is None else closes,
            )

        def copy_out(name, src):
            dense[name] = new_tile(name, list(src.shape), F32)
            nc.scalar.copy(out=dense[name][:], in_=src)

        def scatter(b, name, where):
            nc.vector.tensor_copy(out=window[b][:].indirect(where), in_=dense[name][:])

        def store(b):
            nc.sync.dma_start(out=out[b * P : (b + 1) * P, :], in_=window[b][:])

        for k, (places, halves) in zip((7, 0, 1, 2), ((range(0, 2), low), (range(2, PACK), low), (range(0, 2), high), (range(2, PACK), high))):
            scores(1, k, places, halves)
        for u in range(2):
            weigh(0, u, on_x_last(f"weighted0{u}", [P, 2, HALF], F32, u))
        gradient(0, new_tile("g_rows0", [P, PACK, HALF], BF16))
        for u in range(2):
            weigh(1, u, on_x_last(f"weighted1{u}", [P, 2, HALF], F32, u))
        for s in range(2):
            turn(0, s, "y", range(PACK))
            turn(0, s, "s", range(PACK))
        words = [P, 2 * P, 2]
        gradient_turned(0, 0, new_tile("g_turned00", words, BF16))
        gradient_turned(0, 1, new_tile("g_turned01", words, BF16))
        g_laid[0, LOW] = new_tile("g_laid00", [P, HALF, PACK], BF16, "sig10")
        lay_g(nc.gpsimd, 0, slice(0, POOL_COLS))
        lay_g(nc.scalar, 0, slice(POOL_COLS, HALF))
        turn(1, 0, "y", range(PACK))
        turn(1, 0, "s", range(PACK))
        turn(1, 1, "y", range(1))
        turn(1, 1, "s", range(PACK))
        turn(1, 1, "y", range(1, PACK))
        gradient(1, new_tile("g_rows1", [P, PACK, HALF], BF16, "sig01"))
        gradient_turned(1, 0, on_x_last("g_turned10", words, BF16, 0))
        gradient_turned(1, 1, on_x_last("g_turned11", words, BF16, 1))
        first_m = new_tile("m_bf0", [P, CHUNKS, P, PACK], BF16)
        lay_m(nc.scalar, 0, 0, first_m[:, 0])
        g_laid[1, LOW] = new_tile("g_laid10", [P, HALF, PACK], BF16)
        lay_m(nc.scalar, 0, 1, first_m[:, 1])
        lay_g(nc.gpsimd, 1, slice(G_SPLIT, HALF))
        lay_g(nc.scalar, 1, slice(0, G_SPLIT))
        g_laid[0, HIGH] = new_tile("g_laid01", [P, HALF, PACK], BF16)
        turn_back(0, range(2), 7, g_laid[0, HIGH])
        last_words = [new_tile(f"last_words{s}", [P, P, PACK], BF16) for s in range(2)]
        for s in range(2):
            turn_back(1, range(s, s + 1), s, last_words[s])
        scales = on_y_last("g_scales", [P, 2, CHUNKS, HALF], U8, 0)
        quantise_g(0, LOW, scales[:, LOW, 0], [g_laid[0, LOW]])
        m_first = on_y_last("m_codes0", [P, CHUNKS * P], U32, 1024)
        quantise_m(0, range(CHUNKS), m_first[:], first_m[:].rearrange("p c n t -> p (c n t)"))
        acc.update({(0, HIGH): new_bank(2)[:, 0:HALF], (0, LOW): new_bank(3)[:, 0:HALF]})
        for h in (LOW, HIGH):
            for c in range(CHUNKS):
                if c == 0:
                    if h:
                        quantise_g(c, h, scales[:, h, c], [g_laid[c, h]])
                    product(0, c, h, True)
                else:
                    quantise_g(c, h, scales[:, h, c], last_words if h else [g_laid[c, h][:, 0:P, :], g_laid[c, h][:, P:HALF, :]])
                    for i in range(2):
                        product(0, c, h, False, i == 1, slice(i * P, (i + 1) * P))
        copy_out("dense00", acc[0, LOW])
        m_bf[1, 1] = on_x_last("m_bf11", [P, P, PACK], BF16, 1)[:]
        for engine, cols in ((nc.scalar, slice(0, M_SPLIT)), (nc.vector, slice(M_SPLIT, P))):
            side_by_side(engine, m_bf[1, 1][:, cols, :], m_raw[1, 1][:, :, cols])

        def quantise_piece(b, c, tag=None):
            codes = new_tile(f"m_codes{b}{c}", [P, P], U32, tag)
            quantise_m(b, range(c, c + 1), codes[:], m_bf[b, c].rearrange("p n t -> p (n t)"))

        acc.update({(1, HIGH): new_bank(4)[:, 0:HALF], (1, LOW): new_bank(5)[:, 0:HALF]})
        lay_m(nc.vector, 1, 0, new_tile("m_bf10", [P, P, PACK], BF16, "last_words0")[:])
        quantise_piece(1, 1, "g_laid10")
        scatter(0, "dense00", listed(LOW))
        copy_out("dense01", acc[0, HIGH])
        quantise_piece(1, 0)
        scatter(0, "dense01", listed(HIGH))
        store(0)
        for c in (1, 0):
            for h in (HIGH, LOW):
                product(1, c, h, c == 1)

        def products(b, k):
            bank = new_bank(k)
            for h in (HIGH, LOW):
                acc[b, h] = bank[:, half(h)]
                for c in range(CHUNKS):
                    product(b, c, h, c == 0)
            return bank

        def output(b, bank):
            copy_out(f"dense{b}", bank[:])
            scatter(b, f"dense{b}", offsets[:])
            store(b)

        lay_m(nc.scalar, 2, 0, on_y_last("m_bf20", [P, P, PACK], BF16, 1024)[:])
        lay_m(nc.vector, 2, 1, new_tile("m_bf21", [P, P, PACK], BF16, "dense01")[:])
        for h in (HIGH, LOW):
            copy_out(f"dense1{h}", acc[1, h])
            scatter(1, f"dense1{h}", listed(h))
            quantise_piece(2, h)
        store(1)
        bank = products(2, 6)
        lay_m(nc.scalar, 3, 0, new_tile("m_bf30", [P, P, PACK], BF16, "m_codes10")[:])
        lay_m(nc.vector, 3, 1, new_tile("m_bf31", [P, P, PACK], BF16, "dense11")[:])
        for c in range(CHUNKS):
            quantise_piece(3, c)
        output(2, bank)
        output(3, products(3, 7))
